import numpy as np
import ml_dtypes


def mxq(x, axis, fmt="e4m3"):
    dtype, down = {"e4m3": (ml_dtypes.float8_e4m3fn, 7), "e5m2": (ml_dtypes.float8_e5m2, 14)}[fmt]
    v = np.moveaxis(np.asarray(x, np.float32).astype(ml_dtypes.bfloat16).astype(np.float64), axis, -1)
    blocks = v.reshape(v.shape[:-1] + (-1, 32))
    amax = np.abs(blocks).max(-1, keepdims=True)
    byte = np.maximum(np.where(amax > 0, np.frexp(amax)[1] - 1 + 127, 0) - down, 1)
    scale = np.exp2(byte - 127.0)
    codes = (blocks / scale).astype(np.float32).astype(dtype).astype(np.float64)
    return np.moveaxis((codes * scale).reshape(v.shape), -1, axis)


WIDE = False


def mx_kscale(k):
    if not WIDE:
        return np.ones(k)
    levels = np.array([18, -18])
    if k % 512:
        return np.exp2(np.random.permutation(np.resize(levels, k // 32))).repeat(32)
    a = np.empty((k // 512, 16))
    for p in range(k // 512):
        a[p, :8] = np.random.permutation(np.resize(levels, 8))
        for g in range(8):
            far = levels[np.abs(levels - a[p, g]) >= 10]
            a[p, g + 8] = far[np.random.randint(len(far))]
    return np.exp2(a.ravel()).repeat(32)


def f64(x):
    return np.asarray(x).astype(np.float64)


def striped(idx):
    return np.tile(np.asarray(idx).reshape(-1, 16).T, (8, 1)).astype(np.uint16)


def unstriped(offs):
    return offs[:16].T.reshape(-1).astype(np.int64)


B, N, T, D, DV, R = 2, 512, 2048, 512, 512, 512


def setup_inputs():
    n = np.random.standard_normal
    idx = np.random.permutation(T)[:B * N]
    s = mx_kscale(D)[:, None]
    z = mx_kscale(R)[:, None]
    v = mx_kscale(DV)[:, None]
    q = n((B, D, R))
    do = n((B, DV, R))
    return {
        "qT": (q * s).astype(np.float32),
        "kT": (n((D, T)) * (0.50 / np.sqrt(D)) / s).astype(np.float32),
        "vT": (n((DV, T)) / np.sqrt(DV) / v).astype(np.float32),
        "doT": (do * v).astype(np.float32),
        "lse": (np.log(N) + 0.12 + 0.1 * n((B, R, 1))).astype(np.float32),
        "delta": (0.3 * n((B, R, 1))).astype(np.float32),
        "rw": (np.random.uniform(0.5, 1.5, (B, R, 1)) * N / np.sqrt(R) * z).astype(np.float32),
        "qm": (q.transpose(0, 2, 1) / z).astype(np.float32),
        "dom": (do.transpose(0, 2, 1) / z).astype(np.float32),
        "offs": striped(idx),
    }


def reference(qT, kT, vT, doT, lse, delta, rw, qm, dom, offs):
    idx = unstriped(offs)
    pick = lambda x: x[:, idx].reshape(x.shape[0], B, N).transpose(1, 0, 2)
    a = mxq(f64(qT), 1, "e4m3").transpose(0, 2, 1) @ mxq(pick(f64(kT)), 1, "e4m3")
    p = np.exp(a - f64(lse))
    dp = mxq(f64(doT), 1, "e5m2").transpose(0, 2, 1) @ mxq(pick(f64(vT)), 1, "e4m3")
    ds = f64(rw) * p * (dp - f64(delta))
    dk = mxq(f64(qm), 1, "e4m3").transpose(0, 2, 1) @ mxq(ds, 1, "e5m2")
    dv = mxq(f64(dom), 1, "e5m2").transpose(0, 2, 1) @ mxq(f64(rw) * p, 1, "e4m3")
    gk = np.zeros((D, T))
    gk[:, idx] = dk.transpose(1, 0, 2).reshape(D, B * N)
    gv = np.zeros((DV, T))
    gv[:, idx] = dv.transpose(1, 0, 2).reshape(DV, B * N)
    return gk, gv

@@ -1,0 +1,267 @@
+from contextlib import ExitStack
+
+import concourse.mybir as mybir
+
+B, N, T, D, R = 2, 512, 2048, 512, 512
+FLOPS = 4 * 2 * B * N * D * R
+
+F32 = mybir.dt.float32
+BF16 = mybir.dt.bfloat16
+U32 = mybir.dt.uint32
+U16 = mybir.dt.uint16
+U8 = mybir.dt.uint8
+E4 = mybir.dt.float8_e4m3fn_x4
+E5 = mybir.dt.float8_e5m2_x4
+ACT = mybir.ActivationFunctionType
+ALU = mybir.AluOpType
+
+P = 128
+PACK = 4
+W = 512
+LIST_COLS = N // 16
+
+
+def tile_attend_gat_lse_kv_kernel(tc, qT, kT, vT, doT, lse, delta, rw, qm, dom, offs, out_0, out_1):
+    nc = tc.nc
+    with ExitStack() as ctx:
+        keep = ctx.enter_context(tc.tile_pool(name="keep", bufs=1))
+        work = ctx.enter_context(tc.tile_pool(name="work", bufs=1))
+        psum = ctx.enter_context(tc.psum_pool(name="psum", bufs=4))
+
+        offsets = keep.tile([P, B * LIST_COLS], U16, name="offsets")
+        nc.sync.dma_start(offsets[:], offs)
+        lists = [offsets[:, b * LIST_COLS : (b + 1) * LIST_COLS] for b in range(B)]
+
+        def load_plane(pool_t, j, slot):
+            plane = work.tile([P, T], F32, name="plane", tag="slot%d" % slot, align_bytes=64)
+            nc.sync.dma_start(plane[:], pool_t.rearrange("(p j) t -> p j t", j=PACK)[:, j, :])
+            return plane
+
+        def load_rows(x, slot):
+            rows = work.tile([P, PACK, W], F32, name="rows", tag="slot%d" % slot, align_bytes=64)
+            nc.sync.dma_start(rows[:], x.rearrange("(p j) w -> p j w", j=PACK))
+            return rows
+
+        def load_pair_half(u, h, slot):
+            half = work.tile([P, 2, T // 2], F32, name="half", tag="slot%d" % slot, align_bytes=64)
+            src = vT.rearrange("(p j) t -> p j t", j=PACK)[:, 2 * u : 2 * u + 2, h * (T // 2) : (h + 1) * (T // 2)]
+            nc.sync.dma_start(half[:], src)
+            return half
+
+        def load_per_row(x, name):
+            col = keep.tile([P, B, PACK], F32, name=name)
+            nc.scalar.dma_start(col[:], x.rearrange("b (p t) o -> p b (t o)", t=PACK))
+            return col
+
+        def new_grouped():
+            return work.tile([P, W * PACK], BF16, name="grouped", tag="grouped", bufs=6, align_bytes=64)
+
+        def new_moving():
+            return work.tile([P, W * PACK], BF16, name="moving", tag="moving", bufs=4, align_bytes=64)
+
+        def new_operand(fmt):
+            codes = work.tile([P, W], U32, name="codes", tag="codes", bufs=11, align_bytes=64)
+            scales = work.tile([P, W], U8, name="scales", tag="scales", bufs=11, align_bytes=64)
+            return codes, scales, fmt
+
+        def quantise(operand, grouped, c0=0, c1=W):
+            codes, scales, fmt = operand
+            nc.vector.quantize_mx(out=codes[:, c0:c1].bitcast(fmt), scales=scales[:, c0:c1], in_=grouped[:, PACK * c0 : PACK * c1])
+
+        def quantised(grouped, fmt):
+            operand = new_operand(fmt)
+            quantise(operand, grouped)
+            return operand
+
+        def cast_dealt(grouped, rows, s0=0, s1=P):
+            nc.scalar.copy(
+                out=grouped.rearrange("p (t s j) -> p s j t", t=PACK, j=PACK)[:, s0:s1, :, :],
+                in_=rows[:].rearrange("p j (s t) -> p s j t", t=PACK)[:, s0:s1, :, :],
+            )
+
+        def woven(grouped):
+            return grouped.rearrange("p (c i j) -> p c j i", i=4, j=PACK)
+
+        def planes_woven(planes):
+            return planes.rearrange("p j (c i) -> p c j i", i=4)
+
+        def cast_plain(grouped, rows, c0=0, c1=W):
+            nc.scalar.copy(out=woven(grouped)[:, c0 // 4 : c1 // 4, :, :], in_=planes_woven(rows[:])[:, c0 // 4 : c1 // 4, :, :])
+
+        def product(tag, stationary, j, moving):
+            bank = psum.tile([P, W], F32, name="bank", tag=tag)
+            cols = slice(j * P, (j + 1) * P)
+            nc.tensor.matmul_mx(
+                out=bank[:],
+                lhsT=stationary[0][:, cols].bitcast(stationary[2]),
+                lhsT_scale=stationary[1][:, cols],
+                rhs=moving[0][:].bitcast(moving[2]),
+                rhs_scale=moving[1][:],
+                start=True,
+                stop=True,
+            )
+            return bank
+
+        def put(bank, j, b, staged=None, out=None):
+            if staged is None:
+                staged = work.tile([P, W], F32, name="staged", tag="staged", bufs=4)[:]
+            nc.scalar.copy(out=staged, in_=bank[:])
+            nc.vector.tensor_copy(windows[j][:].indirect(lists[b]), staged)
+            if out is not None:
+                nc.sync.dma_start(out[j * P : (j + 1) * P, :], windows[j][:])
+
+        def weights(b, q_op, k_op):
+            p = keep.tile([P, PACK, W], F32, name="p%d" % b)
+            for t in range(PACK):
+                bank = product("score", q_op, t, k_op)
+                nc.scalar.activation(out=p[:, t, :], in_=bank[:], func=ACT.Exp, bias=neg_lse[:, b, t : t + 1])
+            return p
+
+        def gate_weights(pw, p, gates):
+            spread = gates.rearrange("p (c j i) -> p c j i", c=1, i=1).broadcast_to([P, W // 4, PACK, 4])
+            nc.vector.tensor_tensor(woven(pw), planes_woven(p[:]), spread, ALU.mult)
+
+        def centred(b, do_op, v_op):
+            g = work.tile([P, PACK, W], F32, name="centred")
+            for t in range(PACK):
+                bank = product("score", do_op, t, v_op)
+                nc.scalar.activation(
+                    out=g[:, t, :], in_=bank[:], func=ACT.Identity, bias=neg_rw_delta[:, b, t : t + 1], scale=rw_sb[:, b, t : t + 1]
+                )
+            return g
+
+        def cast_pairs(pairs, half, h):
+            dst = pairs[:, h * (T // 2) : (h + 1) * (T // 2)].bitcast(BF16).rearrange("p (c i j) -> p c j i", i=4, j=2)
+            nc.scalar.activation(out=dst, in_=half[:].rearrange("p j (c i) -> p c j i", i=4), func=ACT.Copy)
+
+        def weave_pairs(gathered):
+            vq = new_moving()
+            nc.scalar.copy(
+                out=vq[:].bitcast(U32).rearrange("p (c i u) -> p c u i", i=4, u=2),
+                in_=gathered[:].rearrange("p u (c i) -> p c u i", i=4),
+            )
+            return vq
+
+        k_planes = [load_plane(kT, 0, 0), load_plane(kT, 1, 1)]
+        q0_raw = load_rows(qT[0], 2)
+        k_planes.append(load_plane(kT, 2, 3))
+        k_planes.append(load_plane(kT, 3, 4))
+        dom0_raw = load_rows(dom[0], 5)
+        q1_raw = load_rows(qT[1], 6)
+        dom1_raw = load_rows(dom[1], 7)
+        lse_sb = load_per_row(lse, "lse_sb")
+        delta_sb = load_per_row(delta, "delta_sb")
+        rw_sb = load_per_row(rw, "rw_sb")
+
+        windows = [keep.tile([P, T], F32, name="window%d" % j) for j in range(PACK)]
+        for window in windows:
+            nc.vector.memset(window[:], 0.0)
+
+        neg_lse = keep.tile([P, B, PACK], F32, name="neg_lse")
+        neg_rw_delta = keep.tile([P, B, PACK], F32, name="neg_rw_delta")
+        staged_3 = keep.tile([P, W], F32, name="staged_3")
+        nc.vector.tensor_scalar(neg_lse[:], lse_sb[:], -1.0, None, ALU.mult)
+        nc.vector.scalar_tensor_tensor(neg_rw_delta[:], rw_sb[:], -1.0, delta_sb[:], ALU.mult, ALU.mult)
+        nc.vector.tensor_copy(staged_3[:, 0:PACK], rw_sb[:, 1, :])
+
+        keys = keep.tile([P, 6 * W], BF16, name="keys", align_bytes=64)
+        k0_grouped = keys[:, 2 * W : 6 * W]
+        for j in range(PACK):
+            nc.vector.tensor_copy(k0_grouped.rearrange("p (n j) -> p n j", j=PACK)[:, :, j], k_planes[j][:].indirect(lists[0]))
+            if j < 2:
+                nc.vector.tensor_copy(keys[:, j * W : (j + 1) * W], k_planes[j][:].indirect(lists[1]))
+            if j == 1:
+                q0_grouped = new_grouped()
+                cast_dealt(q0_grouped[:], q0_raw)
+                q0 = quantised(q0_grouped, E4)
+        k0 = quantised(k0_grouped, E4)
+        p0 = weights(0, q0, k0)
+
+        for j in range(2, PACK):
+            nc.vector.tensor_copy(keys[:, j * W : (j + 1) * W], k_planes[j][:].indirect(lists[1]))
+        k1_grouped = new_moving()
+        nc.vector.tensor_copy(woven(k1_grouped[:]), planes_woven(keys[:, 0 : PACK * W].rearrange("p (j n) -> p j n", j=PACK)))
+
+        v_halves = [load_pair_half(n // 2, n % 2, n) for n in range(4)]
+
+        pw0_grouped = new_moving()
+        gate_weights(pw0_grouped[:], p0, rw_sb[:, 0, :])
+        dom0_grouped = new_grouped()
+        dom0 = new_operand(E5)
+        cast_plain(dom0_grouped[:], dom0_raw, 0, W // 2)
+        quantise(dom0, dom0_grouped, 0, W // 2)
+        pw0 = quantised(pw0_grouped, E4)
+        q1_grouped = new_grouped()
+        cast_dealt(q1_grouped[:], q1_raw, 0, P // 2)
+        cast_dealt(q1_grouped[:], q1_raw, P // 2, P)
+        k1 = quantised(k1_grouped, E4)
+        q1 = quantised(q1_grouped, E4)
+
+        put(product("grad", dom0, 0, pw0), 0, 0)
+        cast_plain(dom0_grouped[:], dom0_raw, W // 2, W)
+        quantise(dom0, dom0_grouped, W // 2, W)
+        put(product("grad", dom0, 1, pw0), 1, 0)
+        p1 = weights(1, q1, k1)
+        put(product("grad", dom0, 2, pw0), 2, 0)
+        dv0_last = product("grad", dom0, 3, pw0)
+
+        do0_raw = load_rows(doT[0], 4)
+        qm0_raw = load_rows(qm[0], 6)
+        do1_raw = load_rows(doT[1], 5)
+
+        dom1_grouped = new_grouped()
+        cast_plain(dom1_grouped[:], dom1_raw)
+        dom1 = quantised(dom1_grouped, E5)
+        qm1_raw = load_rows(qm[1], 7)
+
+        v_pairs = [keep.tile([P, T], U32, name="v_pairs%d" % u) for u in range(2)]
+        cast_pairs(v_pairs[0], v_halves[0], 0)
+        cast_pairs(v_pairs[0], v_halves[1], 1)
+        pw1_grouped = work.tile([P, W * PACK], BF16, name="pw1_grouped", tag="slot1", align_bytes=64)
+        gate_weights(pw1_grouped[:], p1, staged_3[:, 0:PACK])
+        pw1 = quantised(pw1_grouped, E4)
+        put(dv0_last, 3, 0, staged=staged_3[:])
+
+        v_gathered = [keep.tile([P, 2, W], U32, name="v_gathered%d" % b) for b in range(B)]
+        for b in range(B):
+            nc.vector.tensor_copy(v_gathered[b][:, 0, :], v_pairs[0][:].indirect(lists[b]))
+        dv1 = [product("grad", dom1, j, pw1) for j in range(PACK)]
+        cast_pairs(v_pairs[1], v_halves[2], 0)
+        put(dv1[0], 0, 1, out=out_1)
+        do0_grouped = new_grouped()
+        cast_dealt(do0_grouped[:], do0_raw)
+        do0 = quantised(do0_grouped, E5)
+        cast_pairs(v_pairs[1], v_halves[3], 1)
+        nc.vector.tensor_copy(v_gathered[0][:, 1, :], v_pairs[1][:].indirect(lists[0]))
+        staged_5 = work.tile([P, W], F32, name="staged_5", tag="slot3", align_bytes=64)
+        put(dv1[1], 1, 1, staged=staged_5[:], out=out_1)
+        v0 = quantised(weave_pairs(v_gathered[0]), E4)
+        put(dv1[2], 2, 1, out=out_1)
+        nc.vector.tensor_copy(v_gathered[1][:, 1, :], v_pairs[1][:].indirect(lists[1]))
+        g0 = centred(0, do0, v0)
+        qm0_grouped = new_grouped()
+        cast_plain(qm0_grouped[:], qm0_raw)
+        qm0 = quantised(qm0_grouped, E4)
+        ds0_grouped = new_moving()
+        nc.vector.tensor_tensor(woven(ds0_grouped[:]), planes_woven(g0[:]), planes_woven(p0[:]), ALU.mult)
+        ds0 = quantised(ds0_grouped, E5)
+        put(dv1[3], 3, 1, staged=p0[:, 0, :], out=out_1)
+
+        dk0 = [product("grad", qm0, j, ds0) for j in range(PACK)]
+        put(dk0[0], 0, 0)
+        v1 = quantised(weave_pairs(v_gathered[1]), E4)
+        do1_grouped = new_grouped()
+        cast_dealt(do1_grouped[:], do1_raw)
+        do1 = quantised(do1_grouped, E5)
+        put(dk0[1], 1, 0)
+        put(dk0[2], 2, 0)
+        g1 = centred(1, do1, v1)
+        qm1_grouped = new_grouped()
+        cast_plain(qm1_grouped[:], qm1_raw)
+        qm1 = quantised(qm1_grouped, E4)
+        ds1_grouped = new_moving()
+        nc.vector.tensor_tensor(woven(ds1_grouped[:]), planes_woven(g1[:]), planes_woven(p1[:]), ALU.mult)
+        ds1 = quantised(ds1_grouped, E5)
+        put(dk0[3], 3, 0, staged=p1[:, 0, :])
+        for j in range(PACK):
+            put(product("grad", qm1, j, ds1), j, 1, out=out_0)

@@ -79,14 +79,14 @@ def tile_attend_gat_lse_kv_kernel(tc, qT, kT, vT, doT, lse, delta, rw, qm, dom, 
                 in_=rows[:].rearrange("p j (s t) -> p s j t", t=PACK)[:, s0:s1, :, :],
             )
 
-        def woven(grouped):
-            return grouped.rearrange("p (c i j) -> p c j i", i=4, j=PACK)
+        def woven(grouped, run=2):
+            return grouped.rearrange("p (c i j) -> p c j i", i=run, j=PACK)
 
-        def planes_woven(planes):
-            return planes.rearrange("p j (c i) -> p c j i", i=4)
+        def planes_woven(planes, run=2):
+            return planes.rearrange("p j (c i) -> p c j i", i=run)
 
         def cast_plain(grouped, rows, c0=0, c1=W):
-            nc.scalar.copy(out=woven(grouped)[:, c0 // 4 : c1 // 4, :, :], in_=planes_woven(rows[:])[:, c0 // 4 : c1 // 4, :, :])
+            nc.scalar.copy(out=woven(grouped)[:, c0 // 2 : c1 // 2, :, :], in_=planes_woven(rows[:])[:, c0 // 2 : c1 // 2, :, :])
 
         def product(tag, stationary, j, moving):
             bank = psum.tile([P, W], F32, name="bank", tag=tag)
@@ -117,9 +117,14 @@ def tile_attend_gat_lse_kv_kernel(tc, qT, kT, vT, doT, lse, delta, rw, qm, dom, 
                 nc.scalar.activation(out=p[:, t, :], in_=bank[:], func=ACT.Exp, bias=neg_lse[:, b, t : t + 1])
             return p
 
-        def gate_weights(pw, p, gates):
-            spread = gates.rearrange("p (c j i) -> p c j i", c=1, i=1).broadcast_to([P, W // 4, PACK, 4])
-            nc.vector.tensor_tensor(woven(pw), planes_woven(p[:]), spread, ALU.mult)
+        def multiply(engine, pieces, out, in0, in1):
+            step = W // 2 // pieces
+            for c in range(0, W // 2, step):
+                engine.tensor_tensor(out[:, c : c + step, :, :], in0[:, c : c + step, :, :], in1[:, c : c + step, :, :], ALU.mult)
+
+        def gate_weights(engine, pieces, pw, p, gates):
+            spread = gates.rearrange("p (c j i) -> p c j i", c=1, i=1).broadcast_to([P, W // 2, PACK, 2])
+            multiply(engine, pieces, woven(pw), planes_woven(p[:]), spread)
 
         def centred(b, do_op, v_op):
             g = work.tile([P, PACK, W], F32, name="centred")
@@ -180,24 +185,24 @@ def tile_attend_gat_lse_kv_kernel(tc, qT, kT, vT, doT, lse, delta, rw, qm, dom, 
         for j in range(2, PACK):
             nc.vector.tensor_copy(keys[:, j * W : (j + 1) * W], k_planes[j][:].indirect(lists[1]))
         k1_grouped = new_moving()
-        nc.vector.tensor_copy(woven(k1_grouped[:]), planes_woven(keys[:, 0 : PACK * W].rearrange("p (j n) -> p j n", j=PACK)))
+        nc.vector.tensor_copy(woven(k1_grouped[:], 4), planes_woven(keys[:, 0 : PACK * W].rearrange("p (j n) -> p j n", j=PACK), 4))
 
         v_halves = [load_pair_half(n // 2, n % 2, n) for n in range(4)]
 
         pw0_grouped = new_moving()
-        gate_weights(pw0_grouped[:], p0, rw_sb[:, 0, :])
+        gate_weights(nc.vector, 1, pw0_grouped[:], p0, rw_sb[:, 0, :])
         dom0_grouped = new_grouped()
         dom0 = new_operand(E5)
         cast_plain(dom0_grouped[:], dom0_raw, 0, W // 2)
         quantise(dom0, dom0_grouped, 0, W // 2)
         pw0 = quantised(pw0_grouped, E4)
         q1_grouped = new_grouped()
-        cast_dealt(q1_grouped[:], q1_raw, 0, P // 2)
-        cast_dealt(q1_grouped[:], q1_raw, P // 2, P)
+        cast_dealt(q1_grouped[:], q1_raw)
         k1 = quantised(k1_grouped, E4)
         q1 = quantised(q1_grouped, E4)
 
-        put(product("grad", dom0, 0, pw0), 0, 0)
+        staged_0 = work.tile([P, W], F32, name="staged_0", tag="slot6", align_bytes=64)
+        put(product("grad", dom0, 0, pw0), 0, 0, staged=staged_0[:])
         cast_plain(dom0_grouped[:], dom0_raw, W // 2, W)
         quantise(dom0, dom0_grouped, W // 2, W)
         put(product("grad", dom0, 1, pw0), 1, 0)
@@ -217,8 +222,8 @@ def tile_attend_gat_lse_kv_kernel(tc, qT, kT, vT, doT, lse, delta, rw, qm, dom, 
         v_pairs = [keep.tile([P, T], U32, name="v_pairs%d" % u) for u in range(2)]
         cast_pairs(v_pairs[0], v_halves[0], 0)
         cast_pairs(v_pairs[0], v_halves[1], 1)
-        pw1_grouped = work.tile([P, W * PACK], BF16, name="pw1_grouped", tag="slot1", align_bytes=64)
-        gate_weights(pw1_grouped[:], p1, staged_3[:, 0:PACK])
+        pw1_grouped = new_moving()
+        gate_weights(nc.gpsimd, 4, pw1_grouped[:], p1, staged_3[:, 0:PACK])
         pw1 = quantised(pw1_grouped, E4)
         put(dv0_last, 3, 0, staged=staged_3[:])
 
@@ -245,14 +250,14 @@ def tile_attend_gat_lse_kv_kernel(tc, qT, kT, vT, doT, lse, delta, rw, qm, dom, 
         ds0_grouped = new_moving()
         nc.vector.tensor_tensor(woven(ds0_grouped[:]), planes_woven(g0[:]), planes_woven(p0[:]), ALU.mult)
         ds0 = quantised(ds0_grouped, E5)
-        put(dv1[3], 3, 1, staged=p0[:, 0, :], out=out_1)
-
-        dk0 = [product("grad", qm0, j, ds0) for j in range(PACK)]
-        put(dk0[0], 0, 0)
         v1 = quantised(weave_pairs(v_gathered[1]), E4)
         do1_grouped = new_grouped()
         cast_dealt(do1_grouped[:], do1_raw)
         do1 = quantised(do1_grouped, E5)
+        put(dv1[3], 3, 1, staged=p0[:, 0, :], out=out_1)
+
+        dk0 = [product("grad", qm0, j, ds0) for j in range(PACK)]
+        put(dk0[0], 0, 0)
         put(dk0[1], 1, 0)
         put(dk0[2], 2, 0)
         g1 = centred(1, do1, v1)
@@ -260,7 +265,7 @@ def tile_attend_gat_lse_kv_kernel(tc, qT, kT, vT, doT, lse, delta, rw, qm, dom, 
         cast_plain(qm1_grouped[:], qm1_raw)
         qm1 = quantised(qm1_grouped, E4)
         ds1_grouped = new_moving()
-        nc.vector.tensor_tensor(woven(ds1_grouped[:]), planes_woven(g1[:]), planes_woven(p1[:]), ALU.mult)
+        multiply(nc.gpsimd, 4, woven(ds1_grouped[:]), planes_woven(g1[:]), planes_woven(p1[:]))
         ds1 = quantised(ds1_grouped, E5)
         put(dk0[3], 3, 0, staged=p1[:, 0, :])
         for j in range(PACK):

@@ -9,6 +9,7 @@ F32 = mybir.dt.float32
 BF16 = mybir.dt.bfloat16
 U32 = mybir.dt.uint32
 U16 = mybir.dt.uint16
+I32 = mybir.dt.int32
 U8 = mybir.dt.uint8
 E4 = mybir.dt.float8_e4m3fn_x4
 E5 = mybir.dt.float8_e5m2_x4
@@ -19,6 +20,7 @@ P = 128
 PACK = 4
 W = 512
 LIST_COLS = N // 16
+VECTOR_SHARE = 640
 
 
 def tile_attend_gat_lse_kv_kernel(tc, qT, kT, vT, doT, lse, delta, rw, qm, dom, offs, out_0, out_1):
@@ -29,78 +31,81 @@ def tile_attend_gat_lse_kv_kernel(tc, qT, kT, vT, doT, lse, delta, rw, qm, dom, 
         psum = ctx.enter_context(tc.psum_pool(name="psum", bufs=4))
 
         offsets = keep.tile([P, B * LIST_COLS], U16, name="offsets")
-        nc.sync.dma_start(offsets[:], offs)
         lists = [offsets[:, b * LIST_COLS : (b + 1) * LIST_COLS] for b in range(B)]
-
-        def load_plane(pool_t, j, slot):
-            plane = work.tile([P, T], F32, name="plane", tag="slot%d" % slot, align_bytes=64)
-            nc.sync.dma_start(plane[:], pool_t.rearrange("(p j) t -> p j t", j=PACK)[:, j, :])
-            return plane
 
         def load_rows(x, slot):
             rows = work.tile([P, PACK, W], F32, name="rows", tag="slot%d" % slot, align_bytes=64)
             nc.sync.dma_start(rows[:], x.rearrange("(p j) w -> p j w", j=PACK))
             return rows
 
-        def load_pair_half(u, h, slot):
-            half = work.tile([P, 2, T // 2], F32, name="half", tag="slot%d" % slot, align_bytes=64)
-            src = vT.rearrange("(p j) t -> p j t", j=PACK)[:, 2 * u : 2 * u + 2, h * (T // 2) : (h + 1) * (T // 2)]
-            nc.sync.dma_start(half[:], src)
-            return half
+        def load_rows_half(x, h, tag):
+            rows = work.tile([P, PACK, W // 2], F32, name="rows_half", tag=tag, align_bytes=64)
+            nc.sync.dma_start(rows[:], x.rearrange("(p j) w -> p j w", j=PACK)[:, :, h * (W // 2) : (h + 1) * (W // 2)])
+            return rows
+
+        def load_pair_part(pool_t, u, t0, t1, slot):
+            part = work.tile([P, 2, t1 - t0], F32, name="part", tag="slot%d" % slot, align_bytes=64)
+            nc.sync.dma_start(part[:], pool_t.rearrange("(p j) t -> p j t", j=PACK)[:, 2 * u : 2 * u + 2, t0:t1])
+            return part
 
         def load_per_row(x, name):
             col = keep.tile([P, B, PACK], F32, name=name)
-            nc.scalar.dma_start(col[:], x.rearrange("b (p t) o -> p b (t o)", t=PACK))
+            nc.sync.dma_start(col[:], x.rearrange("b (p t) o -> p b (t o)", t=PACK))
             return col
 
         def new_grouped():
-            return work.tile([P, W * PACK], BF16, name="grouped", tag="grouped", bufs=6, align_bytes=64)
+            return work.tile([P, W * PACK], BF16, name="grouped", tag="grouped", bufs=4, align_bytes=64)
 
         def new_moving():
             return work.tile([P, W * PACK], BF16, name="moving", tag="moving", bufs=4, align_bytes=64)
 
-        def new_operand(fmt):
-            codes = work.tile([P, W], U32, name="codes", tag="codes", bufs=11, align_bytes=64)
+        def new_operand(fmt, tag="codes", bufs=10):
+            codes = work.tile([P, W], U32, name="codes", tag=tag, bufs=bufs, align_bytes=64)
             scales = work.tile([P, W], U8, name="scales", tag="scales", bufs=11, align_bytes=64)
             return codes, scales, fmt
 
-        def quantise(operand, grouped, c0=0, c1=W):
+        def quantise(operand, grouped, c0=0):
             codes, scales, fmt = operand
-            nc.vector.quantize_mx(out=codes[:, c0:c1].bitcast(fmt), scales=scales[:, c0:c1], in_=grouped[:, PACK * c0 : PACK * c1])
+            c1 = c0 + grouped.shape[1] // PACK
+            nc.vector.quantize_mx(out=codes[:, c0:c1].bitcast(fmt), scales=scales[:, c0:c1], in_=grouped)
 
         def quantised(grouped, fmt):
             operand = new_operand(fmt)
-            quantise(operand, grouped)
+            quantise(operand, grouped[:])
             return operand
 
-        def cast_dealt(grouped, rows, s0=0, s1=P):
+        def cast_dealt(grouped, rows, s0=0):
+            s1 = s0 + rows.shape[2] // PACK
             nc.scalar.copy(
                 out=grouped.rearrange("p (t s j) -> p s j t", t=PACK, j=PACK)[:, s0:s1, :, :],
-                in_=rows[:].rearrange("p j (s t) -> p s j t", t=PACK)[:, s0:s1, :, :],
+                in_=rows[:].rearrange("p j (s t) -> p s j t", t=PACK),
             )
 
-        def woven(grouped, run=2):
+        def woven(grouped, run):
             return grouped.rearrange("p (c i j) -> p c j i", i=run, j=PACK)
 
-        def planes_woven(planes, run=2):
+        def planes_woven(planes, run):
             return planes.rearrange("p j (c i) -> p c j i", i=run)
 
-        def cast_plain(grouped, rows, c0=0, c1=W):
-            nc.scalar.copy(out=woven(grouped)[:, c0 // 2 : c1 // 2, :, :], in_=planes_woven(rows[:])[:, c0 // 2 : c1 // 2, :, :])
+        def cast_plain(grouped, rows):
+            nc.scalar.copy(out=woven(grouped, 4), in_=planes_woven(rows[:], 4))
 
         def product(tag, stationary, j, moving):
             bank = psum.tile([P, W], F32, name="bank", tag=tag)
+            product_into(bank[:], stationary, j, moving, slice(0, W))
+            return bank
+
+        def product_into(out, stationary, j, moving, slots):
             cols = slice(j * P, (j + 1) * P)
             nc.tensor.matmul_mx(
-                out=bank[:],
+                out=out,
                 lhsT=stationary[0][:, cols].bitcast(stationary[2]),
                 lhsT_scale=stationary[1][:, cols],
-                rhs=moving[0][:].bitcast(moving[2]),
-                rhs_scale=moving[1][:],
+                rhs=moving[0][:, slots].bitcast(moving[2]),
+                rhs_scale=moving[1][:, slots],
                 start=True,
                 stop=True,
             )
-            return bank
 
         def put(bank, j, b, staged=None, out=None):
             if staged is None:
@@ -117,17 +122,22 @@ def tile_attend_gat_lse_kv_kernel(tc, qT, kT, vT, doT, lse, delta, rw, qm, dom, 
                 nc.scalar.activation(out=p[:, t, :], in_=bank[:], func=ACT.Exp, bias=neg_lse[:, b, t : t + 1])
             return p
 
-        def multiply(engine, pieces, out, in0, in1):
-            step = W // 2 // pieces
-            for c in range(0, W // 2, step):
-                engine.tensor_tensor(out[:, c : c + step, :, :], in0[:, c : c + step, :, :], in1[:, c : c + step, :, :], ALU.mult)
+        def weights_in_halves(b, p, q_op, k_op):
+            for h in range(2):
+                slots = slice(h * (W // 2), (h + 1) * (W // 2))
+                for t0 in range(0, PACK, 2):
+                    bank = psum.tile([P, 2, W // 2], F32, name="bank_pair", tag="score")
+                    for e in range(2):
+                        product_into(bank[:, e, :], q_op, t0 + e, k_op, slots)
+                    for e in range(2):
+                        nc.scalar.activation(out=p[h][:, t0 + e, :], in_=bank[:, e, :], func=ACT.Exp, bias=neg_lse[:, b, t0 + e : t0 + e + 1])
 
-        def gate_weights(engine, pieces, pw, p, gates):
-            spread = gates.rearrange("p (c j i) -> p c j i", c=1, i=1).broadcast_to([P, W // 2, PACK, 2])
-            multiply(engine, pieces, woven(pw), planes_woven(p[:]), spread)
+        def gate_weights(pw, p, gates):
+            spread = gates.rearrange("p (c j i) -> p c j i", c=1, i=1).broadcast_to([P, p.shape[2] // 2, PACK, 2])
+            nc.vector.tensor_tensor(woven(pw, 2), planes_woven(p, 2), spread, ALU.mult)
 
         def centred(b, do_op, v_op):
-            g = work.tile([P, PACK, W], F32, name="centred")
+            g = work.tile([P, PACK, W], F32, name="centred", align_bytes=64)
             for t in range(PACK):
                 bank = product("score", do_op, t, v_op)
                 nc.scalar.activation(
@@ -135,137 +145,175 @@ def tile_attend_gat_lse_kv_kernel(tc, qT, kT, vT, doT, lse, delta, rw, qm, dom, 
                 )
             return g
 
-        def cast_pairs(pairs, half, h):
-            dst = pairs[:, h * (T // 2) : (h + 1) * (T // 2)].bitcast(BF16).rearrange("p (c i j) -> p c j i", i=4, j=2)
-            nc.scalar.activation(out=dst, in_=half[:].rearrange("p j (c i) -> p c j i", i=4), func=ACT.Copy)
+        def cast_pairs(pairs, part, t0, on_vector=False):
+            dst = pairs[:, t0 : t0 + part.shape[2]].bitcast(BF16).rearrange("p (c i j) -> p c j i", i=4, j=2)
+            src = part.rearrange("p j (c i) -> p c j i", i=4)
+            if on_vector:
+                nc.vector.tensor_copy(dst, src)
+            else:
+                nc.scalar.activation(out=dst, in_=src, func=ACT.Copy)
+
+        def new_pairs(u):
+            return work.tile([P, T], U32, name="pairs", tag="pairs%d" % u)
 
         def weave_pairs(gathered):
             vq = new_moving()
             nc.scalar.copy(
                 out=vq[:].bitcast(U32).rearrange("p (c i u) -> p c u i", i=4, u=2),
-                in_=gathered[:].rearrange("p u (c i) -> p c u i", i=4),
+                in_=gathered.rearrange("p u (c i) -> p c u i", i=4),
             )
             return vq
 
-        k_planes = [load_plane(kT, 0, 0), load_plane(kT, 1, 1)]
-        q0_raw = load_rows(qT[0], 2)
-        k_planes.append(load_plane(kT, 2, 3))
-        k_planes.append(load_plane(kT, 3, 4))
-        dom0_raw = load_rows(dom[0], 5)
-        q1_raw = load_rows(qT[1], 6)
-        dom1_raw = load_rows(dom[1], 7)
+        k_parts = [load_pair_part(kT, 0, 0, T // 2, 0)]
+        nc.sync.dma_start(offsets[:], offs)
+        k_parts.append(load_pair_part(kT, 0, T // 2, T, 1))
+        k_parts.append(load_pair_part(kT, 1, 0, T // 2, 2))
+        k_parts.append(load_pair_part(kT, 1, T // 2, 3 * T // 4, 3))
+        k_parts.append(load_pair_part(kT, 1, 3 * T // 4, T, 4))
+        q0_raw = [load_rows_half(qT[0], h, "q0_raw%d" % h) for h in range(2)]
         lse_sb = load_per_row(lse, "lse_sb")
-        delta_sb = load_per_row(delta, "delta_sb")
+        dom0_raw = [load_rows_half(dom[0], h, "dom0_raw%d" % h) for h in range(2)]
         rw_sb = load_per_row(rw, "rw_sb")
+        q1_raw = load_rows(qT[1], 5)
+        delta_sb = load_per_row(delta, "delta_sb")
+        dom1_raw = load_rows(dom[1], 6)
 
         windows = [keep.tile([P, T], F32, name="window%d" % j) for j in range(PACK)]
         for window in windows:
             nc.vector.memset(window[:], 0.0)
 
-        neg_lse = keep.tile([P, B, PACK], F32, name="neg_lse")
-        neg_rw_delta = keep.tile([P, B, PACK], F32, name="neg_rw_delta")
-        staged_3 = keep.tile([P, W], F32, name="staged_3")
-        nc.vector.tensor_scalar(neg_lse[:], lse_sb[:], -1.0, None, ALU.mult)
-        nc.vector.scalar_tensor_tensor(neg_rw_delta[:], rw_sb[:], -1.0, delta_sb[:], ALU.mult, ALU.mult)
-        nc.vector.tensor_copy(staged_3[:, 0:PACK], rw_sb[:, 1, :])
-
-        keys = keep.tile([P, 6 * W], BF16, name="keys", align_bytes=64)
-        k0_grouped = keys[:, 2 * W : 6 * W]
-        for j in range(PACK):
-            nc.vector.tensor_copy(k0_grouped.rearrange("p (n j) -> p n j", j=PACK)[:, :, j], k_planes[j][:].indirect(lists[0]))
-            if j < 2:
-                nc.vector.tensor_copy(keys[:, j * W : (j + 1) * W], k_planes[j][:].indirect(lists[1]))
-            if j == 1:
-                q0_grouped = new_grouped()
-                cast_dealt(q0_grouped[:], q0_raw)
-                q0 = quantised(q0_grouped, E4)
+        k_pairs = [new_pairs(0), new_pairs(1)]
+        for h in range(2):
+            cast_pairs(k_pairs[0], k_parts[h][:, :, 0:VECTOR_SHARE], h * (T // 2), on_vector=True)
+            cast_pairs(k_pairs[0], k_parts[h][:, :, VECTOR_SHARE:], h * (T // 2) + VECTOR_SHARE)
+        k0_grouped = new_moving()
+        k0_words = k0_grouped[:].bitcast(U32).rearrange("p (n u) -> p n u", u=2)
+        shared = keep.tile([P, 3 * W], U32, name="shared", align_bytes=64)
+        q0_grouped = shared[:, W : 3 * W].bitcast(BF16)
+        nc.vector.tensor_copy(k0_words[:, :, 0], k_pairs[0][:].indirect(lists[0]))
+        nc.vector.tensor_copy(shared[:, 0:W], k_pairs[0][:].indirect(lists[1]))
+        cast_pairs(k_pairs[1], k_parts[2][:], 0)
+        cast_pairs(k_pairs[1], k_parts[3][:], T // 2, on_vector=True)
+        cast_pairs(k_pairs[1], k_parts[4][:], 3 * T // 4, on_vector=True)
+        nc.vector.tensor_copy(k0_words[:, :, 1], k_pairs[1][:].indirect(lists[0]))
         k0 = quantised(k0_grouped, E4)
-        p0 = weights(0, q0, k0)
-
-        for j in range(2, PACK):
-            nc.vector.tensor_copy(keys[:, j * W : (j + 1) * W], k_planes[j][:].indirect(lists[1]))
-        k1_grouped = new_moving()
-        nc.vector.tensor_copy(woven(k1_grouped[:], 4), planes_woven(keys[:, 0 : PACK * W].rearrange("p (j n) -> p j n", j=PACK), 4))
-
-        v_halves = [load_pair_half(n // 2, n % 2, n) for n in range(4)]
-
-        pw0_grouped = new_moving()
-        gate_weights(nc.vector, 1, pw0_grouped[:], p0, rw_sb[:, 0, :])
+        for h in range(2):
+            cast_dealt(q0_grouped, q0_raw[h], h * (P // 2))
+        q0 = quantised(q0_grouped, E4)
         dom0_grouped = new_grouped()
-        dom0 = new_operand(E5)
-        cast_plain(dom0_grouped[:], dom0_raw, 0, W // 2)
-        quantise(dom0, dom0_grouped, 0, W // 2)
-        pw0 = quantised(pw0_grouped, E4)
+        for h in range(2):
+            cast_plain(dom0_grouped[:, 2 * W * h : 2 * W * (h + 1)], dom0_raw[h])
+        neg_lse = work.tile([P, B, PACK], F32, name="neg_lse", tag="dom0_raw1", align_bytes=64)
+        nc.scalar.mul(neg_lse[:], lse_sb[:], -1.0)
+        p0 = [work.tile([P, PACK, W // 2], F32, name="p0_%d" % h, align_bytes=64) for h in range(2)]
+        weights_in_halves(0, p0, q0, k0)
+
+        nc.vector.tensor_copy(shared[:, W : 2 * W], k_pairs[1][:].indirect(lists[1]))
+        k1_grouped = new_moving()
+        nc.vector.tensor_copy(
+            k1_grouped[:].bitcast(I32).rearrange("p (c i u) -> p c u i", i=4, u=2),
+            shared[:, 0 : 2 * W].bitcast(I32).rearrange("p (u c i) -> p c u i", i=4, u=2),
+        )
+        v_halves = [load_pair_part(vT, n // 2, (n % 2) * (T // 2), (n % 2 + 1) * (T // 2), n) for n in range(4)]
+
+        pw0_grouped = [work.tile([P, 2 * W], BF16, name="pw0_grouped%d" % h, align_bytes=64) for h in range(2)]
+        pw0 = new_operand(E4, "pw0_codes", 1)
+        for h in range(2):
+            gate_weights(pw0_grouped[h][:], p0[h][:], rw_sb[:, 0, :])
+        dom0 = quantised(dom0_grouped, E5)
+        for h in range(2):
+            quantise(pw0, pw0_grouped[h][:], h * (W // 2))
         q1_grouped = new_grouped()
         cast_dealt(q1_grouped[:], q1_raw)
-        k1 = quantised(k1_grouped, E4)
+        k1 = new_operand(E4, "pw0_grouped0", 1)
+        quantise(k1, k1_grouped[:])
         q1 = quantised(q1_grouped, E4)
+        neg_rw_delta = keep.tile([P, B, PACK], F32, name="neg_rw_delta")
+        nc.vector.scalar_tensor_tensor(neg_rw_delta[:], rw_sb[:], -1.0, delta_sb[:], ALU.mult, ALU.mult)
 
-        staged_0 = work.tile([P, W], F32, name="staged_0", tag="slot6", align_bytes=64)
-        put(product("grad", dom0, 0, pw0), 0, 0, staged=staged_0[:])
-        cast_plain(dom0_grouped[:], dom0_raw, W // 2, W)
-        quantise(dom0, dom0_grouped, W // 2, W)
-        put(product("grad", dom0, 1, pw0), 1, 0)
+        for j in range(2):
+            put(product("grad", dom0, j, pw0), j, 0)
         p1 = weights(1, q1, k1)
         put(product("grad", dom0, 2, pw0), 2, 0)
         dv0_last = product("grad", dom0, 3, pw0)
 
         do0_raw = load_rows(doT[0], 4)
-        qm0_raw = load_rows(qm[0], 6)
-        do1_raw = load_rows(doT[1], 5)
+        qm0_raw = load_rows(qm[0], 5)
 
-        dom1_grouped = new_grouped()
-        cast_plain(dom1_grouped[:], dom1_raw)
-        dom1 = quantised(dom1_grouped, E5)
-        qm1_raw = load_rows(qm[1], 7)
+        dom1_grouped = work.tile([P, W * PACK], BF16, name="dom1_grouped", tag="pw0_codes", bufs=1, align_bytes=64)
+        dom1 = new_operand(E5)
+        cast_plain(dom1_grouped[:, 0 : 2 * W], dom1_raw[:, :, 0 : W // 2])
+        quantise(dom1, dom1_grouped[:, 0 : 2 * W])
 
-        v_pairs = [keep.tile([P, T], U32, name="v_pairs%d" % u) for u in range(2)]
-        cast_pairs(v_pairs[0], v_halves[0], 0)
-        cast_pairs(v_pairs[0], v_halves[1], 1)
+        pw1_planes = [work.tile([P, PACK, W // 2], F32, name="pw1_planes", tag="q0_raw%d" % h, align_bytes=64) for h in range(2)]
+        for h in range(2):
+            for t in range(PACK):
+                nc.scalar.activation(
+                    out=pw1_planes[h][:, t, :], in_=p1[:, t, h * (W // 2) : (h + 1) * (W // 2)], func=ACT.Copy, scale=rw_sb[:, 1, t : t + 1]
+                )
         pw1_grouped = new_moving()
-        gate_weights(nc.gpsimd, 4, pw1_grouped[:], p1, staged_3[:, 0:PACK])
+        for h in range(2):
+            cast_plain(pw1_grouped[:, 2 * W * h : 2 * W * (h + 1)], pw1_planes[h])
         pw1 = quantised(pw1_grouped, E4)
+        staged_3 = work.tile([P, W], F32, name="staged_3", tag="q0_raw0", align_bytes=64)
         put(dv0_last, 3, 0, staged=staged_3[:])
+        cast_plain(dom1_grouped[:, 2 * W : 4 * W], dom1_raw[:, :, W // 2 : W])
+        quantise(dom1, dom1_grouped[:, 2 * W : 4 * W], W // 2)
+        do1_raw = load_rows(doT[1], 6)
 
-        v_gathered = [keep.tile([P, 2, W], U32, name="v_gathered%d" % b) for b in range(B)]
+        dv1 = [product("grad", dom1, j, pw1) for j in range(PACK)]
+        v_pairs = [new_pairs(0), new_pairs(1)]
+        v_gathered = [work.tile([P, 2, W], U32, name="v_gathered%d" % b) for b in range(B)]
+        put(dv1[0], 0, 1, out=out_1)
+        for h in range(2):
+            cast_pairs(v_pairs[0], v_halves[0][:, :, h * (T // 4) : (h + 1) * (T // 4)], h * (T // 4))
+        qm1_raw = load_rows(qm[1], 0)
+        cast_pairs(v_pairs[0], v_halves[1][:], T // 2)
         for b in range(B):
             nc.vector.tensor_copy(v_gathered[b][:, 0, :], v_pairs[0][:].indirect(lists[b]))
-        dv1 = [product("grad", dom1, j, pw1) for j in range(PACK)]
-        cast_pairs(v_pairs[1], v_halves[2], 0)
-        put(dv1[0], 0, 1, out=out_1)
+        put(dv1[1], 1, 1, out=out_1)
+        cast_pairs(v_pairs[1], v_halves[2][:], 0)
+        cast_pairs(v_pairs[1], v_halves[3][:], T // 2)
+        for b in range(B):
+            nc.vector.tensor_copy(v_gathered[b][:, 1, :], v_pairs[1][:].indirect(lists[b]))
         do0_grouped = new_grouped()
         cast_dealt(do0_grouped[:], do0_raw)
         do0 = quantised(do0_grouped, E5)
-        cast_pairs(v_pairs[1], v_halves[3], 1)
-        nc.vector.tensor_copy(v_gathered[0][:, 1, :], v_pairs[1][:].indirect(lists[0]))
-        staged_5 = work.tile([P, W], F32, name="staged_5", tag="slot3", align_bytes=64)
-        put(dv1[1], 1, 1, staged=staged_5[:], out=out_1)
-        v0 = quantised(weave_pairs(v_gathered[0]), E4)
-        put(dv1[2], 2, 1, out=out_1)
-        nc.vector.tensor_copy(v_gathered[1][:, 1, :], v_pairs[1][:].indirect(lists[1]))
-        g0 = centred(0, do0, v0)
+        v0 = quantised(weave_pairs(v_gathered[0][:]), E4)
+        staged_6 = work.tile([P, W], F32, name="staged_6", tag="slot4", align_bytes=64)
+        put(dv1[2], 2, 1, staged=staged_6[:], out=out_1)
         qm0_grouped = new_grouped()
-        cast_plain(qm0_grouped[:], qm0_raw)
-        qm0 = quantised(qm0_grouped, E4)
+        qm0 = new_operand(E4)
+        cast_plain(qm0_grouped[:, 0 : 2 * W], qm0_raw[:, :, 0 : W // 2])
+        g0 = centred(0, do0, v0)
+        cast_plain(qm0_grouped[:, 2 * W : 4 * W], qm0_raw[:, :, W // 2 : W])
         ds0_grouped = new_moving()
-        nc.vector.tensor_tensor(woven(ds0_grouped[:]), planes_woven(g0[:]), planes_woven(p0[:]), ALU.mult)
-        ds0 = quantised(ds0_grouped, E5)
-        v1 = quantised(weave_pairs(v_gathered[1]), E4)
-        do1_grouped = new_grouped()
+        ds0 = new_operand(E5, "pw0_codes", 1)
+        for h in range(2):
+            nc.vector.tensor_tensor(
+                woven(ds0_grouped[:, 2 * W * h : 2 * W * (h + 1)], 2),
+                planes_woven(g0[:, :, h * (W // 2) : (h + 1) * (W // 2)], 2),
+                planes_woven(p0[h][:], 2),
+                ALU.mult,
+            )
+        quantise(qm0, qm0_grouped[:])
+        quantise(ds0, ds0_grouped[:])
+        v1 = quantised(weave_pairs(v_gathered[1][:]), E4)
+        staged_7 = work.tile([P, W], F32, name="staged_7", tag="p0_1", align_bytes=64)
+        put(dv1[3], 3, 1, staged=staged_7[:], out=out_1)
+        do1_grouped = work.tile([P, W * PACK], BF16, name="do1_grouped", tag="centred", align_bytes=64)
         cast_dealt(do1_grouped[:], do1_raw)
         do1 = quantised(do1_grouped, E5)
-        put(dv1[3], 3, 1, staged=p0[:, 0, :], out=out_1)
 
         dk0 = [product("grad", qm0, j, ds0) for j in range(PACK)]
-        put(dk0[0], 0, 0)
-        put(dk0[1], 1, 0)
-        put(dk0[2], 2, 0)
+        for j in range(PACK - 1):
+            put(dk0[j], j, 0)
         g1 = centred(1, do1, v1)
-        qm1_grouped = new_grouped()
+        qm1_grouped = work.tile([P, W * PACK], BF16, name="qm1_grouped", tag="pw0_codes", bufs=1, align_bytes=64)
         cast_plain(qm1_grouped[:], qm1_raw)
         qm1 = quantised(qm1_grouped, E4)
         ds1_grouped = new_moving()
-        multiply(nc.gpsimd, 4, woven(ds1_grouped[:]), planes_woven(g1[:]), planes_woven(p1[:]))
+        nc.vector.tensor_tensor(woven(ds1_grouped[:], 2), planes_woven(g1[:], 2), planes_woven(p1[:], 2), ALU.mult)
         ds1 = quantised(ds1_grouped, E5)
         put(dk0[3], 3, 0, staged=p1[:, 0, :])
         for j in range(PACK):

@@ -136,13 +136,19 @@ def tile_attend_gat_lse_kv_kernel(tc, qT, kT, vT, doT, lse, delta, rw, qm, dom, 
             spread = gates.rearrange("p (c j i) -> p c j i", c=1, i=1).broadcast_to([P, p.shape[2] // 2, PACK, 2])
             nc.vector.tensor_tensor(woven(pw, 2), planes_woven(p, 2), spread, ALU.mult)
 
-        def centred(b, do_op, v_op):
+        def centred(b, do_op, v_op, pieces):
             g = work.tile([P, PACK, W], F32, name="centred", align_bytes=64)
-            for t in range(PACK):
-                bank = product("score", do_op, t, v_op)
-                nc.scalar.activation(
-                    out=g[:, t, :], in_=bank[:], func=ACT.Identity, bias=neg_rw_delta[:, b, t : t + 1], scale=rw_sb[:, b, t : t + 1]
-                )
+            banks = [product("score", do_op, t, v_op) for t in range(PACK)]
+            for h in range(pieces):
+                slots = slice(h * (W // pieces), (h + 1) * (W // pieces))
+                for t in range(PACK):
+                    nc.scalar.activation(
+                        out=g[:, t, slots],
+                        in_=banks[t][:, slots],
+                        func=ACT.Identity,
+                        bias=neg_rw_delta[:, b, t : t + 1],
+                        scale=rw_sb[:, b, t : t + 1],
+                    )
             return g
 
         def cast_pairs(pairs, part, t0, on_vector=False):
@@ -201,9 +207,9 @@ def tile_attend_gat_lse_kv_kernel(tc, qT, kT, vT, doT, lse, delta, rw, qm, dom, 
             cast_dealt(q0_grouped, q0_raw[h], h * (P // 2))
         q0 = quantised(q0_grouped, E4)
         dom0_grouped = new_grouped()
-        for h in range(2):
-            cast_plain(dom0_grouped[:, 2 * W * h : 2 * W * (h + 1)], dom0_raw[h])
-        neg_lse = work.tile([P, B, PACK], F32, name="neg_lse", tag="dom0_raw1", align_bytes=64)
+        cast_plain(dom0_grouped[:, 0 : 2 * W], dom0_raw[0])
+        cast_plain(dom0_grouped[:, 2 * W : 3 * W], dom0_raw[1][:, :, 0:P])
+        neg_lse = work.tile([P, B, PACK], F32, name="neg_lse", tag="dom0_raw0", align_bytes=64)
         nc.scalar.mul(neg_lse[:], lse_sb[:], -1.0)
         p0 = [work.tile([P, PACK, W // 2], F32, name="p0_%d" % h, align_bytes=64) for h in range(2)]
         weights_in_halves(0, p0, q0, k0)
@@ -220,7 +226,9 @@ def tile_attend_gat_lse_kv_kernel(tc, qT, kT, vT, doT, lse, delta, rw, qm, dom, 
         pw0 = new_operand(E4, "pw0_codes", 1)
         for h in range(2):
             gate_weights(pw0_grouped[h][:], p0[h][:], rw_sb[:, 0, :])
-        dom0 = quantised(dom0_grouped, E5)
+        dom0 = new_operand(E5)
+        quantise(dom0, dom0_grouped[:, 0 : 2 * W])
+        quantise(dom0, dom0_grouped[:, 2 * W : 3 * W], 2 * P)
         for h in range(2):
             quantise(pw0, pw0_grouped[h][:], h * (W // 2))
         q1_grouped = new_grouped()
@@ -231,6 +239,9 @@ def tile_attend_gat_lse_kv_kernel(tc, qT, kT, vT, doT, lse, delta, rw, qm, dom, 
         neg_rw_delta = keep.tile([P, B, PACK], F32, name="neg_rw_delta")
         nc.vector.scalar_tensor_tensor(neg_rw_delta[:], rw_sb[:], -1.0, delta_sb[:], ALU.mult, ALU.mult)
 
+        dom0_tail = work.tile([P, W], BF16, name="dom0_tail", tag="pw0_grouped1", align_bytes=64)
+        cast_plain(dom0_tail[:], dom0_raw[1][:, :, P : 2 * P])
+        quantise(dom0, dom0_tail[:], 3 * P)
         for j in range(2):
             put(product("grad", dom0, j, pw0), j, 0)
         p1 = weights(1, q1, k1)
@@ -285,7 +296,7 @@ def tile_attend_gat_lse_kv_kernel(tc, qT, kT, vT, doT, lse, delta, rw, qm, dom, 
         qm0_grouped = new_grouped()
         qm0 = new_operand(E4)
         cast_plain(qm0_grouped[:, 0 : 2 * W], qm0_raw[:, :, 0 : W // 2])
-        g0 = centred(0, do0, v0)
+        g0 = centred(0, do0, v0, 2)
         cast_plain(qm0_grouped[:, 2 * W : 4 * W], qm0_raw[:, :, W // 2 : W])
         ds0_grouped = new_moving()
         ds0 = new_operand(E5, "pw0_codes", 1)
@@ -308,7 +319,7 @@ def tile_attend_gat_lse_kv_kernel(tc, qT, kT, vT, doT, lse, delta, rw, qm, dom, 
         dk0 = [product("grad", qm0, j, ds0) for j in range(PACK)]
         for j in range(PACK - 1):
             put(dk0[j], j, 0)
-        g1 = centred(1, do1, v1)
+        g1 = centred(1, do1, v1, 1)
         qm1_grouped = work.tile([P, W * PACK], BF16, name="qm1_grouped", tag="pw0_codes", bufs=1, align_bytes=64)
         cast_plain(qm1_grouped[:], qm1_raw)
         qm1 = quantised(qm1_grouped, E4)

@@ -324,7 +324,7 @@ def tile_attend_gat_lse_kv_kernel(tc, qT, kT, vT, doT, lse, delta, rw, qm, dom, 
         cast_plain(qm1_grouped[:], qm1_raw)
         qm1 = quantised(qm1_grouped, E4)
         ds1_grouped = new_moving()
-        nc.vector.tensor_tensor(woven(ds1_grouped[:], 2), planes_woven(g1[:], 2), planes_woven(p1[:], 2), ALU.mult)
+        nc.gpsimd.tensor_tensor(ds1_grouped[:].rearrange("p (c j) -> p c j", j=PACK), g1[:].rearrange("p j c -> p c j"), p1[:].rearrange("p j c -> p c j"), ALU.mult)
         ds1 = quantised(ds1_grouped, E5)
         put(dk0[3], 3, 0, staged=p1[:, 0, :])
         for j in range(PACK):

@@ -9,7 +9,6 @@ F32 = mybir.dt.float32
 BF16 = mybir.dt.bfloat16
 U32 = mybir.dt.uint32
 U16 = mybir.dt.uint16
-I32 = mybir.dt.int32
 U8 = mybir.dt.uint8
 E4 = mybir.dt.float8_e4m3fn_x4
 E5 = mybir.dt.float8_e5m2_x4
@@ -19,8 +18,8 @@ ALU = mybir.AluOpType
 P = 128
 PACK = 4
 W = 512
+HALF = W // 2
 LIST_COLS = N // 16
-VECTOR_SHARE = 640
 
 
 def tile_attend_gat_lse_kv_kernel(tc, qT, kT, vT, doT, lse, delta, rw, qm, dom, offs, out_0, out_1):
@@ -28,23 +27,18 @@ def tile_attend_gat_lse_kv_kernel(tc, qT, kT, vT, doT, lse, delta, rw, qm, dom, 
     with ExitStack() as ctx:
         keep = ctx.enter_context(tc.tile_pool(name="keep", bufs=1))
         work = ctx.enter_context(tc.tile_pool(name="work", bufs=1))
-        psum = ctx.enter_context(tc.psum_pool(name="psum", bufs=4))
+        psum = ctx.enter_context(tc.psum_pool(name="psum", bufs=1))
 
         offsets = keep.tile([P, B * LIST_COLS], U16, name="offsets")
         lists = [offsets[:, b * LIST_COLS : (b + 1) * LIST_COLS] for b in range(B)]
 
-        def load_rows(x, slot):
-            rows = work.tile([P, PACK, W], F32, name="rows", tag="slot%d" % slot, align_bytes=64)
-            nc.sync.dma_start(rows[:], x.rearrange("(p j) w -> p j w", j=PACK))
+        def load_rows(x, tag, c0=0, c1=W):
+            rows = work.tile([P, PACK, c1 - c0], F32, name="rows", tag=tag, align_bytes=64)
+            nc.sync.dma_start(rows[:], x.rearrange("(p j) w -> p j w", j=PACK)[:, :, c0:c1])
             return rows
 
-        def load_rows_half(x, h, tag):
-            rows = work.tile([P, PACK, W // 2], F32, name="rows_half", tag=tag, align_bytes=64)
-            nc.sync.dma_start(rows[:], x.rearrange("(p j) w -> p j w", j=PACK)[:, :, h * (W // 2) : (h + 1) * (W // 2)])
-            return rows
-
-        def load_pair_part(pool_t, u, t0, t1, slot):
-            part = work.tile([P, 2, t1 - t0], F32, name="part", tag="slot%d" % slot, align_bytes=64)
+        def load_pair_part(pool_t, u, t0, t1, tag):
+            part = work.tile([P, 2, t1 - t0], F32, name="part", tag=tag, align_bytes=64)
             nc.sync.dma_start(part[:], pool_t.rearrange("(p j) t -> p j t", j=PACK)[:, 2 * u : 2 * u + 2, t0:t1])
             return part
 
@@ -53,15 +47,15 @@ def tile_attend_gat_lse_kv_kernel(tc, qT, kT, vT, doT, lse, delta, rw, qm, dom, 
             nc.sync.dma_start(col[:], x.rearrange("b (p t) o -> p b (t o)", t=PACK))
             return col
 
-        def new_grouped():
-            return work.tile([P, W * PACK], BF16, name="grouped", tag="grouped", bufs=4, align_bytes=64)
+        def new_grouped(tag, columns=W):
+            return work.tile([P, columns * PACK], BF16, name="grouped", tag=tag, align_bytes=64)
 
-        def new_moving():
-            return work.tile([P, W * PACK], BF16, name="moving", tag="moving", bufs=4, align_bytes=64)
+        def new_planes(tag, columns=W):
+            return work.tile([P, PACK, columns], F32, name="planes", tag=tag, align_bytes=64)
 
-        def new_operand(fmt, tag="codes", bufs=10):
-            codes = work.tile([P, W], U32, name="codes", tag=tag, bufs=bufs, align_bytes=64)
-            scales = work.tile([P, W], U8, name="scales", tag="scales", bufs=11, align_bytes=64)
+        def new_operand(fmt, tag):
+            codes = work.tile([P, W], U32, name="codes", tag="codes_" + tag, align_bytes=64)
+            scales = work.tile([P, W], U8, name="scales", tag="scales_" + tag, align_bytes=64)
             return codes, scales, fmt
 
         def quantise(operand, grouped, c0=0):
@@ -69,8 +63,8 @@ def tile_attend_gat_lse_kv_kernel(tc, qT, kT, vT, doT, lse, delta, rw, qm, dom, 
             c1 = c0 + grouped.shape[1] // PACK
             nc.vector.quantize_mx(out=codes[:, c0:c1].bitcast(fmt), scales=scales[:, c0:c1], in_=grouped)
 
-        def quantised(grouped, fmt):
-            operand = new_operand(fmt)
+        def quantised(grouped, fmt, tag):
+            operand = new_operand(fmt, tag)
             quantise(operand, grouped[:])
             return operand
 
@@ -78,7 +72,7 @@ def tile_attend_gat_lse_kv_kernel(tc, qT, kT, vT, doT, lse, delta, rw, qm, dom, 
             s1 = s0 + rows.shape[2] // PACK
             nc.scalar.copy(
                 out=grouped.rearrange("p (t s j) -> p s j t", t=PACK, j=PACK)[:, s0:s1, :, :],
-                in_=rows[:].rearrange("p j (s t) -> p s j t", t=PACK),
+                in_=rows.rearrange("p j (s t) -> p s j t", t=PACK),
             )
 
         def woven(grouped, run):
@@ -88,12 +82,15 @@ def tile_attend_gat_lse_kv_kernel(tc, qT, kT, vT, doT, lse, delta, rw, qm, dom, 
             return planes.rearrange("p j (c i) -> p c j i", i=run)
 
         def cast_plain(grouped, rows):
-            nc.scalar.copy(out=woven(grouped, 4), in_=planes_woven(rows[:], 4))
+            nc.scalar.copy(out=woven(grouped, 4), in_=planes_woven(rows, 4))
 
-        def product(tag, stationary, j, moving):
-            bank = psum.tile([P, W], F32, name="bank", tag=tag)
-            product_into(bank[:], stationary, j, moving, slice(0, W))
-            return bank
+        def cast_plain_gpsimd(grouped, rows):
+            nc.gpsimd.tensor_scalar(
+                grouped.rearrange("p (c j) -> p c j", j=PACK), rows.rearrange("p j c -> p c j"), 1.0, 0.0, ALU.mult, ALU.add
+            )
+
+        def new_bank(tag):
+            return psum.tile([P, W], F32, name="bank", tag=tag)
 
         def product_into(out, stationary, j, moving, slots):
             cols = slice(j * P, (j + 1) * P)
@@ -107,49 +104,19 @@ def tile_attend_gat_lse_kv_kernel(tc, qT, kT, vT, doT, lse, delta, rw, qm, dom, 
                 stop=True,
             )
 
-        def put(bank, j, b, staged=None, out=None):
+        def products(kind, stationary, moving):
+            banks = [new_bank("%s%d" % (kind, j)) for j in range(PACK)]
+            for j in range(PACK):
+                product_into(banks[j][:], stationary, j, moving, slice(0, W))
+            return banks
+
+        def put(bank, j, b, tag=None, out=None, staged=None):
             if staged is None:
-                staged = work.tile([P, W], F32, name="staged", tag="staged", bufs=4)[:]
-            nc.scalar.copy(out=staged, in_=bank[:])
-            nc.vector.tensor_copy(windows[j][:].indirect(lists[b]), staged)
+                staged = work.tile([P, W], F32, name="staged", tag=tag or "staged%d" % j, align_bytes=64)
+            nc.scalar.copy(out=staged[:], in_=bank[:])
+            nc.vector.tensor_copy(windows[j][:].indirect(lists[b]), staged[:])
             if out is not None:
                 nc.sync.dma_start(out[j * P : (j + 1) * P, :], windows[j][:])
-
-        def weights(b, q_op, k_op):
-            p = keep.tile([P, PACK, W], F32, name="p%d" % b)
-            for t in range(PACK):
-                bank = product("score", q_op, t, k_op)
-                nc.scalar.activation(out=p[:, t, :], in_=bank[:], func=ACT.Exp, bias=neg_lse[:, b, t : t + 1])
-            return p
-
-        def weights_in_halves(b, p, q_op, k_op):
-            for h in range(2):
-                slots = slice(h * (W // 2), (h + 1) * (W // 2))
-                for t0 in range(0, PACK, 2):
-                    bank = psum.tile([P, 2, W // 2], F32, name="bank_pair", tag="score")
-                    for e in range(2):
-                        product_into(bank[:, e, :], q_op, t0 + e, k_op, slots)
-                    for e in range(2):
-                        nc.scalar.activation(out=p[h][:, t0 + e, :], in_=bank[:, e, :], func=ACT.Exp, bias=neg_lse[:, b, t0 + e : t0 + e + 1])
-
-        def gate_weights(pw, p, gates):
-            spread = gates.rearrange("p (c j i) -> p c j i", c=1, i=1).broadcast_to([P, p.shape[2] // 2, PACK, 2])
-            nc.vector.tensor_tensor(woven(pw, 2), planes_woven(p, 2), spread, ALU.mult)
-
-        def centred(b, do_op, v_op, pieces):
-            g = work.tile([P, PACK, W], F32, name="centred", align_bytes=64)
-            banks = [product("score", do_op, t, v_op) for t in range(PACK)]
-            for h in range(pieces):
-                slots = slice(h * (W // pieces), (h + 1) * (W // pieces))
-                for t in range(PACK):
-                    nc.scalar.activation(
-                        out=g[:, t, slots],
-                        in_=banks[t][:, slots],
-                        func=ACT.Identity,
-                        bias=neg_rw_delta[:, b, t : t + 1],
-                        scale=rw_sb[:, b, t : t + 1],
-                    )
-            return g
 
         def cast_pairs(pairs, part, t0, on_vector=False):
             dst = pairs[:, t0 : t0 + part.shape[2]].bitcast(BF16).rearrange("p (c i j) -> p c j i", i=4, j=2)
@@ -159,30 +126,41 @@ def tile_attend_gat_lse_kv_kernel(tc, qT, kT, vT, doT, lse, delta, rw, qm, dom, 
             else:
                 nc.scalar.activation(out=dst, in_=src, func=ACT.Copy)
 
+        def cast_pairs_shared(pairs, part, t0, on_vector):
+            cast_pairs(pairs, part[:, :, 0:on_vector], t0, on_vector=True)
+            cast_pairs(pairs, part[:, :, on_vector:], t0 + on_vector)
+
         def new_pairs(u):
             return work.tile([P, T], U32, name="pairs", tag="pairs%d" % u)
 
-        def weave_pairs(gathered):
-            vq = new_moving()
+        def pair_words(grouped, u):
+            return grouped.bitcast(U32).rearrange("p (n u) -> p n u", u=2)[:, :, u]
+
+        def weave_pairs(grouped, gathered):
             nc.scalar.copy(
-                out=vq[:].bitcast(U32).rearrange("p (c i u) -> p c u i", i=4, u=2),
+                out=grouped.bitcast(U32).rearrange("p (c i u) -> p c u i", i=4, u=2),
                 in_=gathered.rearrange("p u (c i) -> p c u i", i=4),
             )
-            return vq
 
-        k_parts = [load_pair_part(kT, 0, 0, T // 2, 0)]
+        def centred(g, banks, h, bias, scale):
+            for t in range(PACK):
+                nc.scalar.activation(
+                    out=g[:, t, :], in_=banks[t][:, h * HALF : (h + 1) * HALF], func=ACT.Identity, bias=bias[:, t : t + 1], scale=scale[:, t : t + 1]
+                )
+
+        k_parts = [load_pair_part(kT, 0, 0, T // 2, "part0")]
         nc.sync.dma_start(offsets[:], offs)
-        k_parts.append(load_pair_part(kT, 0, T // 2, T, 1))
-        k_parts.append(load_pair_part(kT, 1, 0, T // 2, 2))
-        k_parts.append(load_pair_part(kT, 1, T // 2, 3 * T // 4, 3))
-        k_parts.append(load_pair_part(kT, 1, 3 * T // 4, T, 4))
-        q0_raw = [load_rows_half(qT[0], h, "q0_raw%d" % h) for h in range(2)]
+        k_parts.append(load_pair_part(kT, 0, T // 2, T, "part1"))
+        q0_raw = load_rows(qT[0], "raw0")
+        k_parts.append(load_pair_part(kT, 1, 0, T // 2, "part2"))
         lse_sb = load_per_row(lse, "lse_sb")
-        dom0_raw = [load_rows_half(dom[0], h, "dom0_raw%d" % h) for h in range(2)]
+        k_parts.append(load_pair_part(kT, 1, T // 2, 3 * T // 4, "part3"))
+        k_parts.append(load_pair_part(kT, 1, 3 * T // 4, T, "part4"))
+        dom0_raw = [load_rows(dom[0], ("raw4", "raw5")[h], h * HALF, (h + 1) * HALF) for h in range(2)]
         rw_sb = load_per_row(rw, "rw_sb")
-        q1_raw = load_rows(qT[1], 5)
+        q1_raw = load_rows(qT[1], "raw1")
         delta_sb = load_per_row(delta, "delta_sb")
-        dom1_raw = load_rows(dom[1], 6)
+        dom1_raw = load_rows(dom[1], "raw2")
 
         windows = [keep.tile([P, T], F32, name="window%d" % j) for j in range(PACK)]
         for window in windows:
@@ -190,142 +168,141 @@ def tile_attend_gat_lse_kv_kernel(tc, qT, kT, vT, doT, lse, delta, rw, qm, dom, 
 
         k_pairs = [new_pairs(0), new_pairs(1)]
         for h in range(2):
-            cast_pairs(k_pairs[0], k_parts[h][:, :, 0:VECTOR_SHARE], h * (T // 2), on_vector=True)
-            cast_pairs(k_pairs[0], k_parts[h][:, :, VECTOR_SHARE:], h * (T // 2) + VECTOR_SHARE)
-        k0_grouped = new_moving()
-        k0_words = k0_grouped[:].bitcast(U32).rearrange("p (n u) -> p n u", u=2)
-        shared = keep.tile([P, 3 * W], U32, name="shared", align_bytes=64)
-        q0_grouped = shared[:, W : 3 * W].bitcast(BF16)
-        nc.vector.tensor_copy(k0_words[:, :, 0], k_pairs[0][:].indirect(lists[0]))
-        nc.vector.tensor_copy(shared[:, 0:W], k_pairs[0][:].indirect(lists[1]))
-        cast_pairs(k_pairs[1], k_parts[2][:], 0)
+            cast_pairs_shared(k_pairs[0], k_parts[h], h * (T // 2), 672)
+        k0_grouped = [new_grouped("k0_%d" % h, HALF) for h in range(2)]
+        k1_grouped = new_grouped("g1")
+        half_lists = [offsets[:, h * (LIST_COLS // 2) : (h + 1) * (LIST_COLS // 2)] for h in range(2)]
+        for h in range(2):
+            nc.vector.tensor_copy(pair_words(k0_grouped[h][:], 0), k_pairs[0][:].indirect(half_lists[h]))
+        nc.vector.tensor_copy(pair_words(k1_grouped[:], 0), k_pairs[0][:].indirect(lists[1]))
+        q0_grouped = new_grouped("g0")
+        cast_dealt(q0_grouped[:], q0_raw[:])
+        q0 = quantised(q0_grouped, E4, "a")
+        cast_pairs_shared(k_pairs[1], k_parts[2], 0, 256)
         cast_pairs(k_pairs[1], k_parts[3][:], T // 2, on_vector=True)
-        cast_pairs(k_pairs[1], k_parts[4][:], 3 * T // 4, on_vector=True)
-        nc.vector.tensor_copy(k0_words[:, :, 1], k_pairs[1][:].indirect(lists[0]))
-        k0 = quantised(k0_grouped, E4)
+        cast_pairs_shared(k_pairs[1], k_parts[4], 3 * T // 4, 352)
+        neg_lse1 = work.tile([P, PACK], F32, name="neg_lse1", tag="after_exp1", align_bytes=64)
+        nc.scalar.mul(neg_lse1[:], lse_sb[:, 1, :], -1.0)
+        dom0_grouped = new_grouped("g2")
         for h in range(2):
-            cast_dealt(q0_grouped, q0_raw[h], h * (P // 2))
-        q0 = quantised(q0_grouped, E4)
-        dom0_grouped = new_grouped()
-        cast_plain(dom0_grouped[:, 0 : 2 * W], dom0_raw[0])
-        cast_plain(dom0_grouped[:, 2 * W : 3 * W], dom0_raw[1][:, :, 0:P])
-        neg_lse = work.tile([P, B, PACK], F32, name="neg_lse", tag="dom0_raw0", align_bytes=64)
-        nc.scalar.mul(neg_lse[:], lse_sb[:], -1.0)
-        p0 = [work.tile([P, PACK, W // 2], F32, name="p0_%d" % h, align_bytes=64) for h in range(2)]
-        weights_in_halves(0, p0, q0, k0)
-
-        nc.vector.tensor_copy(shared[:, W : 2 * W], k_pairs[1][:].indirect(lists[1]))
-        k1_grouped = new_moving()
-        nc.vector.tensor_copy(
-            k1_grouped[:].bitcast(I32).rearrange("p (c i u) -> p c u i", i=4, u=2),
-            shared[:, 0 : 2 * W].bitcast(I32).rearrange("p (u c i) -> p c u i", i=4, u=2),
-        )
-        v_halves = [load_pair_part(vT, n // 2, (n % 2) * (T // 2), (n % 2 + 1) * (T // 2), n) for n in range(4)]
-
-        pw0_grouped = [work.tile([P, 2 * W], BF16, name="pw0_grouped%d" % h, align_bytes=64) for h in range(2)]
-        pw0 = new_operand(E4, "pw0_codes", 1)
+            cast_plain(dom0_grouped[:, h * 2 * W : (h + 1) * 2 * W], dom0_raw[h][:])
+        neg_lse0 = work.tile([P, PACK], F32, name="neg_lse0", tag="raw5", align_bytes=64)
+        nc.scalar.mul(neg_lse0[:], lse_sb[:, 0, :], -1.0)
+        k0 = new_operand(E4, "b")
+        p0 = [new_planes("p0_%d" % h, HALF) for h in range(2)]
         for h in range(2):
-            gate_weights(pw0_grouped[h][:], p0[h][:], rw_sb[:, 0, :])
-        dom0 = new_operand(E5)
-        quantise(dom0, dom0_grouped[:, 0 : 2 * W])
-        quantise(dom0, dom0_grouped[:, 2 * W : 3 * W], 2 * P)
+            nc.vector.tensor_copy(pair_words(k0_grouped[h][:], 1), k_pairs[1][:].indirect(half_lists[h]))
+            quantise(k0, k0_grouped[h][:], h * HALF)
+            for t0 in range(0, PACK, 2):
+                bank = psum.tile([P, 2, HALF], F32, name="bank_pair", tag="score%d" % (2 * h + t0 // 2))
+                for e in range(2):
+                    product_into(bank[:, e, :], q0, t0 + e, k0, slice(h * HALF, (h + 1) * HALF))
+                for e in range(2):
+                    nc.scalar.activation(out=p0[h][:, t0 + e, :], in_=bank[:, e, :], func=ACT.Exp, bias=neg_lse0[:, t0 + e : t0 + e + 1])
+        v_rows = [load_pair_part(vT, u, 0, T, "part%d" % (2 * u)) for u in range(2)]
+        qm0_raw = load_rows(qm[0], "raw0")
+        do0_raw = load_rows(doT[0], "part1")
+
+        dom0 = quantised(dom0_grouped, E5, "c")
+        pw0 = new_operand(E4, "d")
+        pw0_grouped = [new_grouped("k0_%d" % h, HALF) for h in range(2)]
+        gates0 = rw_sb[:, 0, :].rearrange("p (c j i) -> p c j i", c=1, i=1).broadcast_to([P, HALF // 2, PACK, 2])
         for h in range(2):
-            quantise(pw0, pw0_grouped[h][:], h * (W // 2))
-        q1_grouped = new_grouped()
-        cast_dealt(q1_grouped[:], q1_raw)
-        k1 = new_operand(E4, "pw0_grouped0", 1)
-        quantise(k1, k1_grouped[:])
-        q1 = quantised(q1_grouped, E4)
-        neg_rw_delta = keep.tile([P, B, PACK], F32, name="neg_rw_delta")
-        nc.vector.scalar_tensor_tensor(neg_rw_delta[:], rw_sb[:], -1.0, delta_sb[:], ALU.mult, ALU.mult)
-
-        dom0_tail = work.tile([P, W], BF16, name="dom0_tail", tag="pw0_grouped1", align_bytes=64)
-        cast_plain(dom0_tail[:], dom0_raw[1][:, :, P : 2 * P])
-        quantise(dom0, dom0_tail[:], 3 * P)
-        for j in range(2):
-            put(product("grad", dom0, j, pw0), j, 0)
-        p1 = weights(1, q1, k1)
-        put(product("grad", dom0, 2, pw0), 2, 0)
-        dv0_last = product("grad", dom0, 3, pw0)
-
-        do0_raw = load_rows(doT[0], 4)
-        qm0_raw = load_rows(qm[0], 5)
-
-        dom1_grouped = work.tile([P, W * PACK], BF16, name="dom1_grouped", tag="pw0_codes", bufs=1, align_bytes=64)
-        dom1 = new_operand(E5)
-        cast_plain(dom1_grouped[:, 0 : 2 * W], dom1_raw[:, :, 0 : W // 2])
-        quantise(dom1, dom1_grouped[:, 0 : 2 * W])
-
-        pw1_planes = [work.tile([P, PACK, W // 2], F32, name="pw1_planes", tag="q0_raw%d" % h, align_bytes=64) for h in range(2)]
+            nc.vector.tensor_tensor(woven(pw0_grouped[h][:], 2), planes_woven(p0[h][:], 2), gates0, ALU.mult)
         for h in range(2):
-            for t in range(PACK):
-                nc.scalar.activation(
-                    out=pw1_planes[h][:, t, :], in_=p1[:, t, h * (W // 2) : (h + 1) * (W // 2)], func=ACT.Copy, scale=rw_sb[:, 1, t : t + 1]
-                )
-        pw1_grouped = new_moving()
-        for h in range(2):
-            cast_plain(pw1_grouped[:, 2 * W * h : 2 * W * (h + 1)], pw1_planes[h])
-        pw1 = quantised(pw1_grouped, E4)
-        staged_3 = work.tile([P, W], F32, name="staged_3", tag="q0_raw0", align_bytes=64)
-        put(dv0_last, 3, 0, staged=staged_3[:])
-        cast_plain(dom1_grouped[:, 2 * W : 4 * W], dom1_raw[:, :, W // 2 : W])
-        quantise(dom1, dom1_grouped[:, 2 * W : 4 * W], W // 2)
-        do1_raw = load_rows(doT[1], 6)
+            quantise(pw0, pw0_grouped[h][:], h * HALF)
+        dv0 = products("grad", dom0, pw0)
 
-        dv1 = [product("grad", dom1, j, pw1) for j in range(PACK)]
-        v_pairs = [new_pairs(0), new_pairs(1)]
-        v_gathered = [work.tile([P, 2, W], U32, name="v_gathered%d" % b) for b in range(B)]
-        put(dv1[0], 0, 1, out=out_1)
-        for h in range(2):
-            cast_pairs(v_pairs[0], v_halves[0][:, :, h * (T // 4) : (h + 1) * (T // 4)], h * (T // 4))
-        qm1_raw = load_rows(qm[1], 0)
-        cast_pairs(v_pairs[0], v_halves[1][:], T // 2)
+        q1_grouped = new_grouped("raw5")
+        cast_dealt(q1_grouped[:], q1_raw[:])
+        do1_raw = load_rows(doT[1], "raw1")
+        nc.vector.tensor_copy(pair_words(k1_grouped[:], 1), k_pairs[1][:].indirect(lists[1]))
+        k1 = quantised(k1_grouped, E4, "e")
+        q1 = quantised(q1_grouped, E4, "f")
+        neg_rw_delta = [work.tile([P, PACK], F32, name="neg_rw_delta", tag="after_centred%d" % b, align_bytes=64) for b in range(B)]
         for b in range(B):
-            nc.vector.tensor_copy(v_gathered[b][:, 0, :], v_pairs[0][:].indirect(lists[b]))
-        put(dv1[1], 1, 1, out=out_1)
-        cast_pairs(v_pairs[1], v_halves[2][:], 0)
-        cast_pairs(v_pairs[1], v_halves[3][:], T // 2)
-        for b in range(B):
-            nc.vector.tensor_copy(v_gathered[b][:, 1, :], v_pairs[1][:].indirect(lists[b]))
-        do0_grouped = new_grouped()
-        cast_dealt(do0_grouped[:], do0_raw)
-        do0 = quantised(do0_grouped, E5)
-        v0 = quantised(weave_pairs(v_gathered[0][:]), E4)
-        staged_6 = work.tile([P, W], F32, name="staged_6", tag="slot4", align_bytes=64)
-        put(dv1[2], 2, 1, staged=staged_6[:], out=out_1)
-        qm0_grouped = new_grouped()
-        qm0 = new_operand(E4)
-        cast_plain(qm0_grouped[:, 0 : 2 * W], qm0_raw[:, :, 0 : W // 2])
-        g0 = centred(0, do0, v0, 2)
-        cast_plain(qm0_grouped[:, 2 * W : 4 * W], qm0_raw[:, :, W // 2 : W])
-        ds0_grouped = new_moving()
-        ds0 = new_operand(E5, "pw0_codes", 1)
-        for h in range(2):
-            nc.vector.tensor_tensor(
-                woven(ds0_grouped[:, 2 * W * h : 2 * W * (h + 1)], 2),
-                planes_woven(g0[:, :, h * (W // 2) : (h + 1) * (W // 2)], 2),
-                planes_woven(p0[h][:], 2),
-                ALU.mult,
-            )
-        quantise(qm0, qm0_grouped[:])
-        quantise(ds0, ds0_grouped[:])
-        v1 = quantised(weave_pairs(v_gathered[1][:]), E4)
-        staged_7 = work.tile([P, W], F32, name="staged_7", tag="p0_1", align_bytes=64)
-        put(dv1[3], 3, 1, staged=staged_7[:], out=out_1)
-        do1_grouped = work.tile([P, W * PACK], BF16, name="do1_grouped", tag="centred", align_bytes=64)
-        cast_dealt(do1_grouped[:], do1_raw)
-        do1 = quantised(do1_grouped, E5)
+            nc.vector.scalar_tensor_tensor(neg_rw_delta[b][:], rw_sb[:, b, :], -1.0, delta_sb[:, b, :], ALU.mult, ALU.mult)
+        dom1_grouped = new_grouped("raw5")
+        cast_plain_gpsimd(dom1_grouped[:], dom1_raw[:])
 
-        dk0 = [product("grad", qm0, j, ds0) for j in range(PACK)]
-        for j in range(PACK - 1):
-            put(dk0[j], j, 0)
-        g1 = centred(1, do1, v1, 1)
-        qm1_grouped = work.tile([P, W * PACK], BF16, name="qm1_grouped", tag="pw0_codes", bufs=1, align_bytes=64)
-        cast_plain(qm1_grouped[:], qm1_raw)
-        qm1 = quantised(qm1_grouped, E4)
-        ds1_grouped = new_moving()
-        nc.gpsimd.tensor_tensor(ds1_grouped[:].rearrange("p (c j) -> p c j", j=PACK), g1[:].rearrange("p j c -> p c j"), p1[:].rearrange("p j c -> p c j"), ALU.mult)
-        ds1 = quantised(ds1_grouped, E5)
-        put(dk0[3], 3, 0, staged=p1[:, 0, :])
+        put(dv0[0], 0, 0)
+        put(dv0[1], 1, 0)
+        scores1 = products("score", q1, k1)
+        p1 = new_planes("p1")
+        pw1_planes = new_planes("raw2")
+        for t in range(PACK):
+            nc.scalar.activation(out=p1[:, t, :], in_=scores1[t][:], func=ACT.Exp, bias=neg_lse1[:, t : t + 1])
+            nc.gpsimd.tensor_scalar(pw1_planes[:, t, :], p1[:, t, :], rw_sb[:, 1, t : t + 1], 0.0, ALU.mult, ALU.add)
+        put(dv0[2], 2, 0)
+        put(dv0[3], 3, 0, tag="codes_dom1")
+        pw1_grouped = new_grouped("g1")
+        cast_plain_gpsimd(pw1_grouped[:], pw1_planes[:])
+        qm0_grouped = new_grouped("raw2")
+        cast_plain_gpsimd(qm0_grouped[:], qm0_raw[:])
+        v_pairs = [work.tile([P, T], U32, name="pairs", tag="after_exp1", align_bytes=64), new_pairs(1)]
+        for n in range(4):
+            cast_pairs(v_pairs[n // 2], v_rows[n // 2][:, :, (n % 2) * (T // 2) : (n % 2 + 1) * (T // 2)], (n % 2) * (T // 2))
+        qm1_raw = load_rows(qm[1], "part0")
+        pw1 = quantised(pw1_grouped, E4, "a")
+        dom1 = quantised(dom1_grouped, E5, "dom1")
+        dv1 = products("grad", dom1, pw1)
+
+        v0_gathered = work.tile([P, 2, W], U32, name="v0_gathered", tag="gathered", align_bytes=64)
+        for u in range(2):
+            nc.vector.tensor_copy(v0_gathered[:, u, :], v_pairs[u][:].indirect(lists[0]))
+        qm0 = quantised(qm0_grouped, E4, "c")
+        after_v_casts = new_grouped("part2", W + HALF)
+        put(dv1[0], 0, 1, out=out_1, staged=after_v_casts[:, PACK * W :].bitcast(F32))
+        do0_grouped = after_v_casts[:, 0 : PACK * W]
+        cast_dealt(do0_grouped, do0_raw[:])
+        v0_grouped = new_grouped("part1")
+        weave_pairs(v0_grouped[:], v0_gathered[:])
+        do0 = quantised(do0_grouped, E5, "e")
+        v0 = quantised(v0_grouped, E4, "f")
+        v1_gathered = work.tile([P, 2, W], U32, name="v1_gathered", tag="gathered", align_bytes=64)
+        for u in range(2):
+            nc.vector.tensor_copy(v1_gathered[:, u, :], v_pairs[u][:].indirect(lists[1]))
+        put(dv1[1], 1, 1, tag="part1", out=out_1)
+        dp0 = products("score", do0, v0)
+        g0 = [new_planes("g0_%d" % h, HALF) for h in range(2)]
+        ds0_planes = [new_planes("ds0_%d" % h, HALF) for h in range(2)]
+        for h in range(2):
+            centred(g0[h], dp0, h, neg_rw_delta[0], rw_sb[:, 0, :])
+            nc.gpsimd.tensor_tensor(ds0_planes[h][:], g0[h][:], p0[h][:], ALU.mult)
+        dp1_inputs = new_grouped("after_centred0", 2 * W + HALF)
+        put(dv1[2], 2, 1, out=out_1, staged=dp1_inputs[:, 2 * PACK * W :].bitcast(F32))
+        ds0_grouped = new_grouped("g0")
+        for h in range(2):
+            cast_plain(ds0_grouped[:, h * 2 * W : (h + 1) * 2 * W], ds0_planes[h][:])
+        v1_grouped = dp1_inputs[:, 0 : PACK * W]
+        do1_grouped = dp1_inputs[:, PACK * W : 2 * PACK * W]
+        weave_pairs(v1_grouped, v1_gathered[:])
+        for h in range(2):
+            cast_dealt(do1_grouped, do1_raw[:, :, h * HALF : (h + 1) * HALF], h * (P // 2))
+        ds0 = quantised(ds0_grouped, E5, "d")
+        do1 = quantised(do1_grouped, E5, "e")
+        v1 = quantised(v1_grouped, E4, "f")
+        put(dv1[3], 3, 1, tag="ds0_1", out=out_1)
+        dk0 = products("grad", qm0, ds0)
+
+        put(dk0[0], 0, 0)
+        dp1 = products("score", do1, v1)
+        g1 = [new_planes("g0_%d" % h, HALF) for h in range(2)]
+        ds1_planes = [new_planes("p0_%d" % h, HALF) for h in range(2)]
+        for h in range(2):
+            centred(g1[h], dp1, h, neg_rw_delta[1], rw_sb[:, 1, :])
+            nc.gpsimd.tensor_tensor(ds1_planes[h][:], g1[h][:], p1[:, :, h * HALF : (h + 1) * HALF], ALU.mult)
+        put(dk0[1], 1, 0)
+        put(dk0[2], 2, 0)
+        ds1_grouped = new_grouped("g0")
+        for h in range(2):
+            cast_plain(ds1_grouped[:, h * 2 * W : (h + 1) * 2 * W], ds1_planes[h][:])
+        qm1_grouped = new_grouped("after_centred1")
+        for h in range(2):
+            cast_plain(qm1_grouped[:, h * 2 * W : (h + 1) * 2 * W], qm1_raw[:, :, h * HALF : (h + 1) * HALF])
+        qm1 = quantised(qm1_grouped, E4, "a")
+        ds1 = quantised(ds1_grouped, E5, "b")
+        put(dk0[3], 3, 0, tag="p0_1")
+        dk1 = products("grad", qm1, ds1)
         for j in range(PACK):
-            put(product("grad", qm1, j, ds1), j, 1, out=out_0)
+            put(dk1[j], j, 1, out=out_0)

@@ -53,8 +53,8 @@ def tile_attend_gat_lse_kv_kernel(tc, qT, kT, vT, doT, lse, delta, rw, qm, dom, 
         def new_planes(tag, columns=W):
             return work.tile([P, PACK, columns], F32, name="planes", tag=tag, align_bytes=64)
 
-        def new_operand(fmt, tag):
-            codes = work.tile([P, W], U32, name="codes", tag="codes_" + tag, align_bytes=64)
+        def new_operand(fmt, tag, codes_tag=None):
+            codes = work.tile([P, W], U32, name="codes", tag=codes_tag or "codes_" + tag, align_bytes=64)
             scales = work.tile([P, W], U8, name="scales", tag="scales_" + tag, align_bytes=64)
             return codes, scales, fmt
 
@@ -153,13 +153,14 @@ def tile_attend_gat_lse_kv_kernel(tc, qT, kT, vT, doT, lse, delta, rw, qm, dom, 
         k_parts.append(load_pair_part(kT, 0, T // 2, T, "part1"))
         q0_raw = load_rows(qT[0], "raw0")
         k_parts.append(load_pair_part(kT, 1, 0, T // 2, "part2"))
-        lse_sb = load_per_row(lse, "lse_sb")
         k_parts.append(load_pair_part(kT, 1, T // 2, 3 * T // 4, "part3"))
         k_parts.append(load_pair_part(kT, 1, 3 * T // 4, T, "part4"))
-        dom0_raw = [load_rows(dom[0], ("raw4", "raw5")[h], h * HALF, (h + 1) * HALF) for h in range(2)]
+        lse_sb = load_per_row(lse, "lse_sb")
+        dom0_raw = [load_rows(dom[0], "raw4", 0, HALF), load_rows(dom[0], "raw5", HALF, HALF + P)]
         rw_sb = load_per_row(rw, "rw_sb")
-        q1_raw = load_rows(qT[1], "raw1")
         delta_sb = load_per_row(delta, "delta_sb")
+        q1_raw = load_rows(qT[1], "raw1")
+        dom0_raw.append(load_rows(dom[0], "dom0_tail_raw", HALF + P, W))
         dom1_raw = load_rows(dom[1], "raw2")
 
         windows = [keep.tile([P, T], F32, name="window%d" % j) for j in range(PACK)]
@@ -183,9 +184,9 @@ def tile_attend_gat_lse_kv_kernel(tc, qT, kT, vT, doT, lse, delta, rw, qm, dom, 
         cast_pairs_shared(k_pairs[1], k_parts[4], 3 * T // 4, 352)
         neg_lse1 = work.tile([P, PACK], F32, name="neg_lse1", tag="after_exp1", align_bytes=64)
         nc.scalar.mul(neg_lse1[:], lse_sb[:, 1, :], -1.0)
-        dom0_grouped = new_grouped("g2")
-        for h in range(2):
-            cast_plain(dom0_grouped[:, h * 2 * W : (h + 1) * 2 * W], dom0_raw[h][:])
+        dom0_grouped = [new_grouped("g2", HALF), new_grouped("g3", HALF)]
+        cast_plain(dom0_grouped[0][:], dom0_raw[0][:])
+        cast_plain(dom0_grouped[1][:, 0:W], dom0_raw[1][:])
         neg_lse0 = work.tile([P, PACK], F32, name="neg_lse0", tag="raw5", align_bytes=64)
         nc.scalar.mul(neg_lse0[:], lse_sb[:, 0, :], -1.0)
         k0 = new_operand(E4, "b")
@@ -193,17 +194,15 @@ def tile_attend_gat_lse_kv_kernel(tc, qT, kT, vT, doT, lse, delta, rw, qm, dom, 
         for h in range(2):
             nc.vector.tensor_copy(pair_words(k0_grouped[h][:], 1), k_pairs[1][:].indirect(half_lists[h]))
             quantise(k0, k0_grouped[h][:], h * HALF)
-            for t0 in range(0, PACK, 2):
-                bank = psum.tile([P, 2, HALF], F32, name="bank_pair", tag="score%d" % (2 * h + t0 // 2))
-                for e in range(2):
-                    product_into(bank[:, e, :], q0, t0 + e, k0, slice(h * HALF, (h + 1) * HALF))
-                for e in range(2):
-                    nc.scalar.activation(out=p0[h][:, t0 + e, :], in_=bank[:, e, :], func=ACT.Exp, bias=neg_lse0[:, t0 + e : t0 + e + 1])
+            for t in range(PACK):
+                bank = psum.tile([P, HALF], F32, name="half_bank", tag="%s%d" % (("score", "grad")[h], t))
+                product_into(bank[:], q0, t, k0, slice(h * HALF, (h + 1) * HALF))
+                nc.scalar.activation(out=p0[h][:, t, :], in_=bank[:], func=ACT.Exp, bias=neg_lse0[:, t : t + 1])
         v_rows = [load_pair_part(vT, u, 0, T, "part%d" % (2 * u)) for u in range(2)]
-        qm0_raw = load_rows(qm[0], "raw0")
         do0_raw = load_rows(doT[0], "part1")
 
-        dom0 = quantised(dom0_grouped, E5, "c")
+        dom0 = [new_operand(E5, "c")]
+        quantise(dom0[0], dom0_grouped[0][:])
         pw0 = new_operand(E4, "d")
         pw0_grouped = [new_grouped("k0_%d" % h, HALF) for h in range(2)]
         gates0 = rw_sb[:, 0, :].rearrange("p (c j i) -> p c j i", c=1, i=1).broadcast_to([P, HALF // 2, PACK, 2])
@@ -211,14 +210,25 @@ def tile_attend_gat_lse_kv_kernel(tc, qT, kT, vT, doT, lse, delta, rw, qm, dom, 
             nc.vector.tensor_tensor(woven(pw0_grouped[h][:], 2), planes_woven(p0[h][:], 2), gates0, ALU.mult)
         for h in range(2):
             quantise(pw0, pw0_grouped[h][:], h * HALF)
-        dv0 = products("grad", dom0, pw0)
+        dv0 = [new_bank("grad%d" % j) for j in range(PACK)]
+        for j in range(2):
+            product_into(dv0[j][:], dom0[0], j, pw0, slice(0, W))
 
         q1_grouped = new_grouped("raw5")
         cast_dealt(q1_grouped[:], q1_raw[:])
-        do1_raw = load_rows(doT[1], "raw1")
+        qm0_raw = load_rows(qm[0], "raw1")
+        do1_raw = load_rows(doT[1], "g3")
         nc.vector.tensor_copy(pair_words(k1_grouped[:], 1), k_pairs[1][:].indirect(lists[1]))
-        k1 = quantised(k1_grouped, E4, "e")
+        k1 = new_operand(E4, "e", codes_tag="k0_1")
+        quantise(k1, k1_grouped[:])
+        dom0_tail = new_grouped("k0_0", P)
+        nc.vector.tensor_copy(woven(dom0_tail[:], 4), planes_woven(dom0_raw[2][:], 4))
+        dom0.append(new_operand(E5, "c2"))
+        quantise(dom0[1], dom0_grouped[1][:, 0:W])
+        quantise(dom0[1], dom0_tail[:], P)
         q1 = quantised(q1_grouped, E4, "f")
+        for j in range(2):
+            product_into(dv0[2 + j][:], dom0[1], j, pw0, slice(0, W))
         neg_rw_delta = [work.tile([P, PACK], F32, name="neg_rw_delta", tag="after_centred%d" % b, align_bytes=64) for b in range(B)]
         for b in range(B):
             nc.vector.scalar_tensor_tensor(neg_rw_delta[b][:], rw_sb[:, b, :], -1.0, delta_sb[:, b, :], ALU.mult, ALU.mult)
@@ -237,8 +247,6 @@ def tile_attend_gat_lse_kv_kernel(tc, qT, kT, vT, doT, lse, delta, rw, qm, dom, 
         put(dv0[3], 3, 0, tag="codes_dom1")
         pw1_grouped = new_grouped("g1")
         cast_plain_gpsimd(pw1_grouped[:], pw1_planes[:])
-        qm0_grouped = new_grouped("raw2")
-        cast_plain_gpsimd(qm0_grouped[:], qm0_raw[:])
         v_pairs = [work.tile([P, T], U32, name="pairs", tag="after_exp1", align_bytes=64), new_pairs(1)]
         for n in range(4):
             cast_pairs(v_pairs[n // 2], v_rows[n // 2][:, :, (n % 2) * (T // 2) : (n % 2 + 1) * (T // 2)], (n % 2) * (T // 2))
@@ -250,57 +258,62 @@ def tile_attend_gat_lse_kv_kernel(tc, qT, kT, vT, doT, lse, delta, rw, qm, dom, 
         v0_gathered = work.tile([P, 2, W], U32, name="v0_gathered", tag="gathered", align_bytes=64)
         for u in range(2):
             nc.vector.tensor_copy(v0_gathered[:, u, :], v_pairs[u][:].indirect(lists[0]))
-        qm0 = quantised(qm0_grouped, E4, "c")
-        after_v_casts = new_grouped("part2", W + HALF)
-        put(dv1[0], 0, 1, out=out_1, staged=after_v_casts[:, PACK * W :].bitcast(F32))
-        do0_grouped = after_v_casts[:, 0 : PACK * W]
-        cast_dealt(do0_grouped, do0_raw[:])
-        v0_grouped = new_grouped("part1")
-        weave_pairs(v0_grouped[:], v0_gathered[:])
+        do0_grouped = new_grouped("part2")
+        cast_dealt(do0_grouped[:], do0_raw[:])
         do0 = quantised(do0_grouped, E5, "e")
+        after_do0 = new_grouped("part1", W + HALF)
+        put(dv1[0], 0, 1, out=out_1, staged=after_do0[:, PACK * W :].bitcast(F32))
+        v0_grouped = after_do0[:, 0 : PACK * W]
+        weave_pairs(v0_grouped, v0_gathered[:])
         v0 = quantised(v0_grouped, E4, "f")
-        v1_gathered = work.tile([P, 2, W], U32, name="v1_gathered", tag="gathered", align_bytes=64)
+        do1_grouped = new_grouped("gathered")
+        cast_dealt(do1_grouped[:], do1_raw[:])
+        do1 = quantised(do1_grouped, E5, "a")
+        after_do1 = work.tile([P, 3 * W], U32, name="after_do1", tag="g3", align_bytes=64)
+        v1_gathered = after_do1[:, 0 : 2 * W].rearrange("p (u c) -> p u c", u=2)
         for u in range(2):
-            nc.vector.tensor_copy(v1_gathered[:, u, :], v_pairs[u][:].indirect(lists[1]))
-        put(dv1[1], 1, 1, tag="part1", out=out_1)
+            nc.vector.tensor_copy(after_do1[:, u * W : (u + 1) * W], v_pairs[u][:].indirect(lists[1]))
+        put(dv1[1], 1, 1, out=out_1, staged=after_do1[:, 2 * W : 3 * W].bitcast(F32))
         dp0 = products("score", do0, v0)
         g0 = [new_planes("g0_%d" % h, HALF) for h in range(2)]
-        ds0_planes = [new_planes("ds0_%d" % h, HALF) for h in range(2)]
+        ds0_planes = new_planes("ds0_0", HALF)
         for h in range(2):
             centred(g0[h], dp0, h, neg_rw_delta[0], rw_sb[:, 0, :])
-            nc.gpsimd.tensor_tensor(ds0_planes[h][:], g0[h][:], p0[h][:], ALU.mult)
-        dp1_inputs = new_grouped("after_centred0", 2 * W + HALF)
-        put(dv1[2], 2, 1, out=out_1, staged=dp1_inputs[:, 2 * PACK * W :].bitcast(F32))
-        ds0_grouped = new_grouped("g0")
+        nc.gpsimd.tensor_tensor(ds0_planes[:], g0[0][:], p0[0][:], ALU.mult)
+        put(dv1[2], 2, 1, tag="after_centred0", out=out_1)
+        ds0_grouped = [new_grouped("g0", HALF), new_grouped("after_centred0", HALF)]
+        cast_plain(ds0_grouped[0][:], ds0_planes[:])
+        nc.vector.tensor_tensor(woven(ds0_grouped[1][:], 2), planes_woven(g0[1][:], 2), planes_woven(p0[1][:], 2), ALU.mult)
+        after_ds0 = new_grouped("g0_0", 2 * W)
+        v1_grouped = after_ds0[:, 0 : PACK * W]
+        qm0_grouped = after_ds0[:, PACK * W : 2 * PACK * W]
+        cast_plain(qm0_grouped, qm0_raw[:])
+        weave_pairs(v1_grouped, v1_gathered)
+        ds0 = new_operand(E5, "d")
         for h in range(2):
-            cast_plain(ds0_grouped[:, h * 2 * W : (h + 1) * 2 * W], ds0_planes[h][:])
-        v1_grouped = dp1_inputs[:, 0 : PACK * W]
-        do1_grouped = dp1_inputs[:, PACK * W : 2 * PACK * W]
-        weave_pairs(v1_grouped, v1_gathered[:])
-        for h in range(2):
-            cast_dealt(do1_grouped, do1_raw[:, :, h * HALF : (h + 1) * HALF], h * (P // 2))
-        ds0 = quantised(ds0_grouped, E5, "d")
-        do1 = quantised(do1_grouped, E5, "e")
+            quantise(ds0, ds0_grouped[h][:], h * HALF)
+        qm0 = quantised(qm0_grouped, E4, "c")
         v1 = quantised(v1_grouped, E4, "f")
-        put(dv1[3], 3, 1, tag="ds0_1", out=out_1)
+        put(dv1[3], 3, 1, tag="g3", out=out_1)
         dk0 = products("grad", qm0, ds0)
 
         put(dk0[0], 0, 0)
         dp1 = products("score", do1, v1)
-        g1 = [new_planes("g0_%d" % h, HALF) for h in range(2)]
+        g1_planes = new_planes("g0")
+        g1 = [g1_planes[:, :, h * HALF : (h + 1) * HALF] for h in range(2)]
         ds1_planes = [new_planes("p0_%d" % h, HALF) for h in range(2)]
         for h in range(2):
             centred(g1[h], dp1, h, neg_rw_delta[1], rw_sb[:, 1, :])
-            nc.gpsimd.tensor_tensor(ds1_planes[h][:], g1[h][:], p1[:, :, h * HALF : (h + 1) * HALF], ALU.mult)
+            nc.gpsimd.tensor_tensor(ds1_planes[h][:], g1[h], p1[:, :, h * HALF : (h + 1) * HALF], ALU.mult)
         put(dk0[1], 1, 0)
         put(dk0[2], 2, 0)
-        ds1_grouped = new_grouped("g0")
+        ds1_grouped = new_grouped("g1")
         for h in range(2):
             cast_plain(ds1_grouped[:, h * 2 * W : (h + 1) * 2 * W], ds1_planes[h][:])
         qm1_grouped = new_grouped("after_centred1")
         for h in range(2):
             cast_plain(qm1_grouped[:, h * 2 * W : (h + 1) * 2 * W], qm1_raw[:, :, h * HALF : (h + 1) * HALF])
-        qm1 = quantised(qm1_grouped, E4, "a")
+        qm1 = quantised(qm1_grouped, E4, "e")
         ds1 = quantised(ds1_grouped, E5, "b")
         put(dk0[3], 3, 0, tag="p0_1")
         dk1 = products("grad", qm1, ds1)

@@ -75,6 +75,22 @@ def tile_attend_gat_lse_kv_kernel(tc, qT, kT, vT, doT, lse, delta, rw, qm, dom, 
                 in_=rows.rearrange("p j (s t) -> p s j t", t=PACK),
             )
 
+        def cast_dealt_pair(grouped, rows, t0):
+            nc.scalar.copy(
+                out=grouped.rearrange("p (t s j) -> p s j t", t=2, j=PACK),
+                in_=rows.rearrange("p j (s t) -> p s j t", t=PACK)[:, :, :, t0 : t0 + 2],
+            )
+
+        def cast_dealt_pair_gpsimd(grouped, rows, t0):
+            nc.gpsimd.tensor_scalar(
+                grouped.rearrange("p (t s j) -> p t s j", t=2, j=PACK),
+                rows.rearrange("p j (s t) -> p t s j", t=PACK)[:, t0 : t0 + 2, :, :],
+                1.0,
+                0.0,
+                ALU.mult,
+                ALU.add,
+            )
+
         def woven(grouped, run):
             return grouped.rearrange("p (c i j) -> p c j i", i=run, j=PACK)
 
@@ -247,6 +263,8 @@ def tile_attend_gat_lse_kv_kernel(tc, qT, kT, vT, doT, lse, delta, rw, qm, dom, 
         put(dv0[3], 3, 0, tag="codes_dom1")
         pw1_grouped = new_grouped("g1")
         cast_plain_gpsimd(pw1_grouped[:], pw1_planes[:])
+        do0_grouped = [new_grouped("raw2", HALF)]
+        cast_dealt_pair_gpsimd(do0_grouped[0][:], do0_raw[:], 0)
         v_pairs = [work.tile([P, T], U32, name="pairs", tag="after_exp1", align_bytes=64), new_pairs(1)]
         for n in range(4):
             cast_pairs(v_pairs[n // 2], v_rows[n // 2][:, :, (n % 2) * (T // 2) : (n % 2 + 1) * (T // 2)], (n % 2) * (T // 2))
@@ -258,43 +276,48 @@ def tile_attend_gat_lse_kv_kernel(tc, qT, kT, vT, doT, lse, delta, rw, qm, dom, 
         v0_gathered = work.tile([P, 2, W], U32, name="v0_gathered", tag="gathered", align_bytes=64)
         for u in range(2):
             nc.vector.tensor_copy(v0_gathered[:, u, :], v_pairs[u][:].indirect(lists[0]))
-        do0_grouped = new_grouped("part2")
-        cast_dealt(do0_grouped[:], do0_raw[:])
-        do0 = quantised(do0_grouped, E5, "e")
-        after_do0 = new_grouped("part1", W + HALF)
-        put(dv1[0], 0, 1, out=out_1, staged=after_do0[:, PACK * W :].bitcast(F32))
+        do0_grouped.append(new_grouped("part2", HALF))
+        cast_dealt_pair(do0_grouped[1][:], do0_raw[:], 2)
+        do0 = new_operand(E5, "e")
+        for h in range(2):
+            quantise(do0, do0_grouped[h][:], h * HALF)
+        qm0_grouped = [new_grouped("part2", HALF)]
+        cast_plain_gpsimd(qm0_grouped[0][:], qm0_raw[:, :, 0:HALF])
+        after_do0 = new_grouped("part1", 2 * W + HALF)
+        put(dv1[0], 0, 1, out=out_1, staged=after_do0[:, 2 * PACK * W :].bitcast(F32))
+        do1_grouped = after_do0[:, PACK * W : 2 * PACK * W]
+        cast_dealt(do1_grouped, do1_raw[:, :, 0:HALF])
         v0_grouped = after_do0[:, 0 : PACK * W]
         weave_pairs(v0_grouped, v0_gathered[:])
         v0 = quantised(v0_grouped, E4, "f")
-        do1_grouped = new_grouped("gathered")
-        cast_dealt(do1_grouped[:], do1_raw[:])
+        qm0 = new_operand(E4, "c")
+        quantise(qm0, qm0_grouped[0][:])
+        cast_dealt(do1_grouped, do1_raw[:, :, HALF:W], P // 2)
         do1 = quantised(do1_grouped, E5, "a")
-        after_do1 = work.tile([P, 3 * W], U32, name="after_do1", tag="g3", align_bytes=64)
+        qm0_grouped.append(new_grouped("gathered", HALF))
+        cast_plain(qm0_grouped[1][:], qm0_raw[:, :, HALF:W])
+        quantise(qm0, qm0_grouped[1][:], HALF)
+        after_do1 = work.tile([P, 3 * W], U32, name="after_do1", tag="raw1", align_bytes=64)
         v1_gathered = after_do1[:, 0 : 2 * W].rearrange("p (u c) -> p u c", u=2)
         for u in range(2):
             nc.vector.tensor_copy(after_do1[:, u * W : (u + 1) * W], v_pairs[u][:].indirect(lists[1]))
         put(dv1[1], 1, 1, out=out_1, staged=after_do1[:, 2 * W : 3 * W].bitcast(F32))
         dp0 = products("score", do0, v0)
         g0 = [new_planes("g0_%d" % h, HALF) for h in range(2)]
-        ds0_planes = new_planes("ds0_0", HALF)
+        ds0_planes = [new_planes(("ds0_0", "raw0")[h], HALF) for h in range(2)]
         for h in range(2):
             centred(g0[h], dp0, h, neg_rw_delta[0], rw_sb[:, 0, :])
-        nc.gpsimd.tensor_tensor(ds0_planes[:], g0[0][:], p0[0][:], ALU.mult)
-        put(dv1[2], 2, 1, tag="after_centred0", out=out_1)
-        ds0_grouped = [new_grouped("g0", HALF), new_grouped("after_centred0", HALF)]
-        cast_plain(ds0_grouped[0][:], ds0_planes[:])
-        nc.vector.tensor_tensor(woven(ds0_grouped[1][:], 2), planes_woven(g0[1][:], 2), planes_woven(p0[1][:], 2), ALU.mult)
-        after_ds0 = new_grouped("g0_0", 2 * W)
-        v1_grouped = after_ds0[:, 0 : PACK * W]
-        qm0_grouped = after_ds0[:, PACK * W : 2 * PACK * W]
-        cast_plain(qm0_grouped, qm0_raw[:])
+            nc.gpsimd.tensor_tensor(ds0_planes[h][:], g0[h][:], p0[h][:], ALU.mult)
+        after_centred = new_grouped("after_centred0", W + HALF)
+        put(dv1[2], 2, 1, out=out_1, staged=after_centred[:, PACK * W :].bitcast(F32))
+        v1_grouped = after_centred[:, 0 : PACK * W]
         weave_pairs(v1_grouped, v1_gathered)
-        ds0 = new_operand(E5, "d")
-        for h in range(2):
-            quantise(ds0, ds0_grouped[h][:], h * HALF)
-        qm0 = quantised(qm0_grouped, E4, "c")
+        ds0_grouped = new_grouped("g0")
+        cast_plain(ds0_grouped[:, 0 : 2 * W], ds0_planes[0][:])
+        cast_plain(ds0_grouped[:, 2 * W : 4 * W], ds0_planes[1][:])
         v1 = quantised(v1_grouped, E4, "f")
-        put(dv1[3], 3, 1, tag="g3", out=out_1)
+        ds0 = quantised(ds0_grouped, E5, "d")
+        put(dv1[3], 3, 1, tag="raw0", out=out_1)
         dk0 = products("grad", qm0, ds0)
 
         put(dk0[0], 0, 0)

@@ -167,16 +167,16 @@ def tile_attend_gat_lse_kv_kernel(tc, qT, kT, vT, doT, lse, delta, rw, qm, dom, 
         k_parts = [load_pair_part(kT, 0, 0, T // 2, "part0")]
         nc.sync.dma_start(offsets[:], offs)
         k_parts.append(load_pair_part(kT, 0, T // 2, T, "part1"))
-        q0_raw = load_rows(qT[0], "raw0")
         k_parts.append(load_pair_part(kT, 1, 0, T // 2, "part2"))
         k_parts.append(load_pair_part(kT, 1, T // 2, 3 * T // 4, "part3"))
         k_parts.append(load_pair_part(kT, 1, 3 * T // 4, T, "part4"))
+        q0_raw = [load_rows(qT[0], "q0_raw%d" % h, h * HALF, (h + 1) * HALF) for h in range(2)]
         lse_sb = load_per_row(lse, "lse_sb")
-        dom0_raw = [load_rows(dom[0], "raw4", 0, HALF), load_rows(dom[0], "raw5", HALF, HALF + P)]
+        dom0_raw = [load_rows(dom[0], "raw5", 0, HALF)]
         rw_sb = load_per_row(rw, "rw_sb")
         delta_sb = load_per_row(delta, "delta_sb")
         q1_raw = load_rows(qT[1], "raw1")
-        dom0_raw.append(load_rows(dom[0], "dom0_tail_raw", HALF + P, W))
+        dom0_raw.append(load_rows(dom[0], "raw4", HALF, W))
         dom1_raw = load_rows(dom[1], "raw2")
 
         windows = [keep.tile([P, T], F32, name="window%d" % j) for j in range(PACK)]
@@ -187,29 +187,36 @@ def tile_attend_gat_lse_kv_kernel(tc, qT, kT, vT, doT, lse, delta, rw, qm, dom, 
         for h in range(2):
             cast_pairs_shared(k_pairs[0], k_parts[h], h * (T // 2), 672)
         k0_grouped = [new_grouped("k0_%d" % h, HALF) for h in range(2)]
-        k1_grouped = new_grouped("g1")
-        half_lists = [offsets[:, h * (LIST_COLS // 2) : (h + 1) * (LIST_COLS // 2)] for h in range(2)]
+        k1_grouped = [new_grouped("g1", HALF)]
+        half_lists = [offsets[:, h * (LIST_COLS // 2) : (h + 1) * (LIST_COLS // 2)] for h in range(2 * B)]
         for h in range(2):
             nc.vector.tensor_copy(pair_words(k0_grouped[h][:], 0), k_pairs[0][:].indirect(half_lists[h]))
-        nc.vector.tensor_copy(pair_words(k1_grouped[:], 0), k_pairs[0][:].indirect(lists[1]))
-        q0_grouped = new_grouped("g0")
-        cast_dealt(q0_grouped[:], q0_raw[:])
-        q0 = quantised(q0_grouped, E4, "a")
-        cast_pairs_shared(k_pairs[1], k_parts[2], 0, 256)
+        nc.vector.tensor_copy(pair_words(k1_grouped[0][:], 0), k_pairs[0][:].indirect(half_lists[2]))
+        cast_pairs(k_pairs[1], k_parts[2][:], 0)
         cast_pairs(k_pairs[1], k_parts[3][:], T // 2, on_vector=True)
         cast_pairs_shared(k_pairs[1], k_parts[4], 3 * T // 4, 352)
-        neg_lse1 = work.tile([P, PACK], F32, name="neg_lse1", tag="after_exp1", align_bytes=64)
-        nc.scalar.mul(neg_lse1[:], lse_sb[:, 1, :], -1.0)
-        dom0_grouped = [new_grouped("g2", HALF), new_grouped("g3", HALF)]
-        cast_plain(dom0_grouped[0][:], dom0_raw[0][:])
-        cast_plain(dom0_grouped[1][:, 0:W], dom0_raw[1][:])
-        neg_lse0 = work.tile([P, PACK], F32, name="neg_lse0", tag="raw5", align_bytes=64)
-        nc.scalar.mul(neg_lse0[:], lse_sb[:, 0, :], -1.0)
         k0 = new_operand(E4, "b")
-        p0 = [new_planes("p0_%d" % h, HALF) for h in range(2)]
         for h in range(2):
             nc.vector.tensor_copy(pair_words(k0_grouped[h][:], 1), k_pairs[1][:].indirect(half_lists[h]))
             quantise(k0, k0_grouped[h][:], h * HALF)
+        nc.vector.tensor_copy(pair_words(k1_grouped[0][:], 1), k_pairs[1][:].indirect(half_lists[2]))
+        q0_grouped = new_grouped("g0")
+        for h in range(2):
+            cast_dealt(q0_grouped[:], q0_raw[h][:], h * (P // 2))
+        q0 = new_operand(E4, "a")
+        for h in range(2):
+            quantise(q0, q0_grouped[:, h * 2 * W : (h + 1) * 2 * W], h * HALF)
+        k1_grouped.append(new_grouped("g0", HALF))
+        for u in range(2):
+            nc.vector.tensor_copy(pair_words(k1_grouped[1][:], u), k_pairs[u][:].indirect(half_lists[3]))
+        neg_lse1 = work.tile([P, PACK], F32, name="neg_lse1", tag="after_exp1", align_bytes=64)
+        nc.scalar.mul(neg_lse1[:], lse_sb[:, 1, :], -1.0)
+        dom0_grouped = [new_grouped("g2", HALF)]
+        cast_plain(dom0_grouped[0][:], dom0_raw[0][:])
+        neg_lse0 = work.tile([P, PACK], F32, name="neg_lse0", tag="raw5", align_bytes=64)
+        nc.scalar.mul(neg_lse0[:], lse_sb[:, 0, :], -1.0)
+        p0 = [new_planes("p0_%d" % h, HALF) for h in range(2)]
+        for h in range(2):
             for t in range(PACK):
                 bank = psum.tile([P, HALF], F32, name="half_bank", tag="%s%d" % (("score", "grad")[h], t))
                 product_into(bank[:], q0, t, k0, slice(h * HALF, (h + 1) * HALF))
@@ -233,15 +240,14 @@ def tile_attend_gat_lse_kv_kernel(tc, qT, kT, vT, doT, lse, delta, rw, qm, dom, 
         q1_grouped = new_grouped("raw5")
         cast_dealt(q1_grouped[:], q1_raw[:])
         qm0_raw = load_rows(qm[0], "raw1")
-        do1_raw = load_rows(doT[1], "g3")
-        nc.vector.tensor_copy(pair_words(k1_grouped[:], 1), k_pairs[1][:].indirect(lists[1]))
+        dom0_grouped.append(new_grouped("k0_0", HALF))
+        nc.vector.tensor_copy(woven(dom0_grouped[1][:], 4), planes_woven(dom0_raw[1][:], 4))
+        do1_raw = load_rows(doT[1], "raw4")
         k1 = new_operand(E4, "e", codes_tag="k0_1")
-        quantise(k1, k1_grouped[:])
-        dom0_tail = new_grouped("k0_0", P)
-        nc.vector.tensor_copy(woven(dom0_tail[:], 4), planes_woven(dom0_raw[2][:], 4))
+        for h in range(2):
+            quantise(k1, k1_grouped[h][:], h * HALF)
         dom0.append(new_operand(E5, "c2"))
-        quantise(dom0[1], dom0_grouped[1][:, 0:W])
-        quantise(dom0[1], dom0_tail[:], P)
+        quantise(dom0[1], dom0_grouped[1][:])
         q1 = quantised(q1_grouped, E4, "f")
         for j in range(2):
             product_into(dv0[2 + j][:], dom0[1], j, pw0, slice(0, W))
@@ -304,7 +310,7 @@ def tile_attend_gat_lse_kv_kernel(tc, qT, kT, vT, doT, lse, delta, rw, qm, dom, 
         put(dv1[1], 1, 1, out=out_1, staged=after_do1[:, 2 * W : 3 * W].bitcast(F32))
         dp0 = products("score", do0, v0)
         g0 = [new_planes("g0_%d" % h, HALF) for h in range(2)]
-        ds0_planes = [new_planes(("ds0_0", "raw0")[h], HALF) for h in range(2)]
+        ds0_planes = [new_planes(("ds0_0", "q0_raw0")[h], HALF) for h in range(2)]
         for h in range(2):
             centred(g0[h], dp0, h, neg_rw_delta[0], rw_sb[:, 0, :])
             nc.gpsimd.tensor_tensor(ds0_planes[h][:], g0[h][:], p0[h][:], ALU.mult)
@@ -317,7 +323,7 @@ def tile_attend_gat_lse_kv_kernel(tc, qT, kT, vT, doT, lse, delta, rw, qm, dom, 
         cast_plain(ds0_grouped[:, 2 * W : 4 * W], ds0_planes[1][:])
         v1 = quantised(v1_grouped, E4, "f")
         ds0 = quantised(ds0_grouped, E5, "d")
-        put(dv1[3], 3, 1, tag="raw0", out=out_1)
+        put(dv1[3], 3, 1, tag="q0_raw0", out=out_1)
         dk0 = products("grad", qm0, ds0)
 
         put(dk0[0], 0, 0)

@@ -20,6 +20,15 @@ PACK = 4
 W = 512
 HALF = W // 2
 LIST_COLS = N // 16
+HALVES = [slice(0, HALF), slice(HALF, W)]
+WHOLE = slice(0, W)
+KB = 1024
+K0, K1, K2, K3, V0, V1, V2, V3 = (8 * KB * n for n in range(8))
+Q0A, Q0B, DOM0A, DOM0B = (64 * KB + 4 * KB * n for n in range(4))
+Q1, DOM1, DO0, QM0, DO1, QM1 = (80 * KB + 8 * KB * n for n in range(6))
+SCALES = 128 * KB
+X = 136 * KB
+Y = 166 * KB
 
 
 def tile_attend_gat_lse_kv_kernel(tc, qT, kT, vT, doT, lse, delta, rw, qm, dom, offs, out_0, out_1):
@@ -30,32 +39,37 @@ def tile_attend_gat_lse_kv_kernel(tc, qT, kT, vT, doT, lse, delta, rw, qm, dom, 
         psum = ctx.enter_context(tc.psum_pool(name="psum", bufs=1))
 
         offsets = keep.tile([P, B * LIST_COLS], U16, name="offsets")
-        lists = [offsets[:, b * LIST_COLS : (b + 1) * LIST_COLS] for b in range(B)]
 
-        def load_rows(x, tag, c0=0, c1=W):
-            rows = work.tile([P, PACK, c1 - c0], F32, name="rows", tag=tag, align_bytes=64)
-            nc.sync.dma_start(rows[:], x.rearrange("(p j) w -> p j w", j=PACK)[:, :, c0:c1])
+        def listed(b, slots=WHOLE):
+            return offsets[:, (b * N + slots.start) // 16 : (b * N + slots.stop) // 16]
+
+        def load_rows(x, name, at, cols=WHOLE):
+            rows = work.tile([P, PACK, cols.stop - cols.start], F32, name=name, offset=at, align_bytes=64)
+            nc.sync.dma_start(rows[:], x.rearrange("(p j) w -> p j w", j=PACK)[:, :, cols])
             return rows
 
-        def load_pair_part(pool_t, u, t0, t1, tag):
-            part = work.tile([P, 2, t1 - t0], F32, name="part", tag=tag, align_bytes=64)
-            nc.sync.dma_start(part[:], pool_t.rearrange("(p j) t -> p j t", j=PACK)[:, 2 * u : 2 * u + 2, t0:t1])
-            return part
+        def load_plane(pool_t, j, name, at):
+            plane = work.tile([P, T], F32, name=name, offset=at, align_bytes=64)
+            nc.sync.dma_start(plane[:], pool_t.rearrange("(p j) t -> p j t", j=PACK)[:, j, :])
+            return plane
 
         def load_per_row(x, name):
             col = keep.tile([P, B, PACK], F32, name=name)
             nc.sync.dma_start(col[:], x.rearrange("b (p t) o -> p b (t o)", t=PACK))
             return col
 
-        def new_grouped(tag, columns=W):
-            return work.tile([P, columns * PACK], BF16, name="grouped", tag=tag, align_bytes=64)
+        def new_grouped(name, at, columns=W):
+            return work.tile([P, columns * PACK], BF16, name=name, offset=at, align_bytes=64)
 
-        def new_planes(tag, columns=W):
-            return work.tile([P, PACK, columns], F32, name="planes", tag=tag, align_bytes=64)
+        def new_planes(name, at, dtype, columns=W, planes=PACK):
+            return work.tile([P, planes, columns], dtype, name=name, offset=at, align_bytes=64)
 
-        def new_operand(fmt, tag, codes_tag=None):
-            codes = work.tile([P, W], U32, name="codes", tag=codes_tag or "codes_" + tag, align_bytes=64)
-            scales = work.tile([P, W], U8, name="scales", tag="scales_" + tag, align_bytes=64)
+        operands = []
+
+        def new_operand(fmt, name, at):
+            codes = work.tile([P, W], U32, name=name + "_codes", offset=at, align_bytes=64)
+            scales = work.tile([P, W], U8, name=name + "_scales", offset=SCALES + W * len(operands), align_bytes=64)
+            operands.append(name)
             return codes, scales, fmt
 
         def quantise(operand, grouped, c0=0):
@@ -63,55 +77,70 @@ def tile_attend_gat_lse_kv_kernel(tc, qT, kT, vT, doT, lse, delta, rw, qm, dom, 
             c1 = c0 + grouped.shape[1] // PACK
             nc.vector.quantize_mx(out=codes[:, c0:c1].bitcast(fmt), scales=scales[:, c0:c1], in_=grouped)
 
-        def quantised(grouped, fmt, tag):
-            operand = new_operand(fmt, tag)
+        def quantised(grouped, fmt, name, at):
+            operand = new_operand(fmt, name, at)
             quantise(operand, grouped[:])
             return operand
 
-        def cast_dealt(grouped, rows, s0=0):
+        def copy_on(engine, out, in_):
+            if engine is nc.vector:
+                nc.vector.tensor_copy(out, in_)
+            elif engine is nc.scalar:
+                nc.scalar.copy(out=out, in_=in_)
+            else:
+                nc.gpsimd.tensor_scalar(out, in_, 1.0, 0.0, ALU.mult, ALU.add)
+
+        def deal(engine, grouped, rows, s0=0):
             s1 = s0 + rows.shape[2] // PACK
-            nc.scalar.copy(
-                out=grouped.rearrange("p (t s j) -> p s j t", t=PACK, j=PACK)[:, s0:s1, :, :],
-                in_=rows.rearrange("p j (s t) -> p s j t", t=PACK),
-            )
+            if engine is nc.gpsimd:
+                for t0 in range(0, PACK, 2):
+                    copy_on(
+                        engine,
+                        grouped.rearrange("p (t s j) -> p t s j", t=PACK, j=PACK)[:, t0 : t0 + 2, s0:s1, :],
+                        rows.rearrange("p j (s t) -> p t s j", t=PACK)[:, t0 : t0 + 2, :, :],
+                    )
+            else:
+                copy_on(
+                    engine,
+                    grouped.rearrange("p (t s j) -> p s j t", t=PACK, j=PACK)[:, s0:s1, :, :],
+                    rows.rearrange("p j (s t) -> p s j t", t=PACK),
+                )
 
-        def cast_dealt_pair(grouped, rows, t0):
-            nc.scalar.copy(
-                out=grouped.rearrange("p (t s j) -> p s j t", t=2, j=PACK),
-                in_=rows.rearrange("p j (s t) -> p s j t", t=PACK)[:, :, :, t0 : t0 + 2],
-            )
+        def deal_half(engine, grouped, rows, h):
+            if engine is nc.gpsimd:
+                copy_on(
+                    engine,
+                    grouped.rearrange("p (t s j) -> p t s j", t=2, j=PACK),
+                    rows.rearrange("p j (s t) -> p t s j", t=PACK)[:, 2 * h : 2 * h + 2, :, :],
+                )
+            else:
+                copy_on(
+                    engine,
+                    grouped.rearrange("p (t s j) -> p s j t", t=2, j=PACK),
+                    rows.rearrange("p j (s t) -> p s j t", t=PACK)[:, :, :, 2 * h : 2 * h + 2],
+                )
 
-        def cast_dealt_pair_gpsimd(grouped, rows, t0):
-            nc.gpsimd.tensor_scalar(
-                grouped.rearrange("p (t s j) -> p t s j", t=2, j=PACK),
-                rows.rearrange("p j (s t) -> p t s j", t=PACK)[:, t0 : t0 + 2, :, :],
-                1.0,
-                0.0,
-                ALU.mult,
-                ALU.add,
-            )
+        def weave(engine, grouped, planes):
+            if engine is nc.gpsimd:
+                copy_on(engine, grouped.rearrange("p (c j) -> p c j", j=PACK), planes.rearrange("p j c -> p c j"))
+            else:
+                copy_on(
+                    engine,
+                    grouped.rearrange("p (c i j) -> p c j i", i=4, j=PACK),
+                    planes.rearrange("p j (c i) -> p c j i", i=4),
+                )
 
-        def woven(grouped, run):
-            return grouped.rearrange("p (c i j) -> p c j i", i=run, j=PACK)
+        def gather_plane(out, plane, slots):
+            nc.scalar.activation(out=out, in_=plane[:].indirect(slots), func=ACT.Copy)
 
-        def planes_woven(planes, run):
-            return planes.rearrange("p j (c i) -> p c j i", i=run)
+        def gather_into_place(grouped, j, plane, slots):
+            nc.vector.tensor_copy(grouped.rearrange("p (n j) -> p n j", j=PACK)[:, :, j], plane[:].indirect(slots))
 
-        def cast_plain(grouped, rows):
-            nc.scalar.copy(out=woven(grouped, 4), in_=planes_woven(rows, 4))
-
-        def cast_plain_gpsimd(grouped, rows):
-            nc.gpsimd.tensor_scalar(
-                grouped.rearrange("p (c j) -> p c j", j=PACK), rows.rearrange("p j c -> p c j"), 1.0, 0.0, ALU.mult, ALU.add
-            )
-
-        def new_bank(tag):
-            return psum.tile([P, W], F32, name="bank", tag=tag)
-
-        def product_into(out, stationary, j, moving, slots):
+        def product(tag, stationary, j, moving, slots=WHOLE):
+            bank = psum.tile([P, slots.stop - slots.start], F32, name="bank", tag=tag)
             cols = slice(j * P, (j + 1) * P)
             nc.tensor.matmul_mx(
-                out=out,
+                out=bank[:],
                 lhsT=stationary[0][:, cols].bitcast(stationary[2]),
                 lhsT_scale=stationary[1][:, cols],
                 rhs=moving[0][:, slots].bitcast(moving[2]),
@@ -119,232 +148,236 @@ def tile_attend_gat_lse_kv_kernel(tc, qT, kT, vT, doT, lse, delta, rw, qm, dom, 
                 start=True,
                 stop=True,
             )
+            return bank
 
-        def products(kind, stationary, moving):
-            banks = [new_bank("%s%d" % (kind, j)) for j in range(PACK)]
-            for j in range(PACK):
-                product_into(banks[j][:], stationary, j, moving, slice(0, W))
-            return banks
+        def stage(engine, bank, name, at):
+            staged = work.tile([P, bank.shape[1]], F32, name=name, offset=at, align_bytes=64)
+            copy_on(engine, staged[:], bank)
+            return staged
 
-        def put(bank, j, b, tag=None, out=None, staged=None):
-            if staged is None:
-                staged = work.tile([P, W], F32, name="staged", tag=tag or "staged%d" % j, align_bytes=64)
-            nc.scalar.copy(out=staged[:], in_=bank[:])
-            nc.vector.tensor_copy(windows[j][:].indirect(lists[b]), staged[:])
-            if out is not None:
-                nc.sync.dma_start(out[j * P : (j + 1) * P, :], windows[j][:])
-
-        def cast_pairs(pairs, part, t0, on_vector=False):
-            dst = pairs[:, t0 : t0 + part.shape[2]].bitcast(BF16).rearrange("p (c i j) -> p c j i", i=4, j=2)
-            src = part.rearrange("p j (c i) -> p c j i", i=4)
-            if on_vector:
-                nc.vector.tensor_copy(dst, src)
+        def scatter(engine, window, staged, b, slots=WHOLE):
+            if engine is nc.vector:
+                nc.vector.tensor_copy(window[:].indirect(listed(b, slots)), staged)
             else:
-                nc.scalar.activation(out=dst, in_=src, func=ACT.Copy)
+                for c0 in range(slots.start, slots.stop, HALF):
+                    piece = slice(c0, c0 + HALF)
+                    nc.scalar.activation(
+                        out=window[:].indirect(listed(b, piece)), in_=staged[:, c0 - slots.start : c0 - slots.start + HALF], func=ACT.Copy
+                    )
 
-        def cast_pairs_shared(pairs, part, t0, on_vector):
-            cast_pairs(pairs, part[:, :, 0:on_vector], t0, on_vector=True)
-            cast_pairs(pairs, part[:, :, on_vector:], t0 + on_vector)
+        def store(out, j, window):
+            nc.sync.dma_start(out[j * P : (j + 1) * P, :], window[:])
 
-        def new_pairs(u):
-            return work.tile([P, T], U32, name="pairs", tag="pairs%d" % u)
-
-        def pair_words(grouped, u):
-            return grouped.bitcast(U32).rearrange("p (n u) -> p n u", u=2)[:, :, u]
-
-        def weave_pairs(grouped, gathered):
-            nc.scalar.copy(
-                out=grouped.bitcast(U32).rearrange("p (c i u) -> p c u i", i=4, u=2),
-                in_=gathered.rearrange("p u (c i) -> p c u i", i=4),
-            )
-
-        def centred(g, banks, h, bias, scale):
+        def weights(planes, banks, neg_lse):
             for t in range(PACK):
-                nc.scalar.activation(
-                    out=g[:, t, :], in_=banks[t][:, h * HALF : (h + 1) * HALF], func=ACT.Identity, bias=bias[:, t : t + 1], scale=scale[:, t : t + 1]
-                )
+                nc.scalar.activation(out=planes[:, t, :], in_=banks[t][:], func=ACT.Exp, bias=neg_lse[:, t : t + 1])
 
-        k_parts = [load_pair_part(kT, 0, 0, T // 2, "part0")]
+        def negated(name, at, column):
+            neg = work.tile([P, PACK], F32, name=name, offset=at, align_bytes=64)
+            nc.scalar.mul(neg[:], column, -1.0)
+            return neg
+
+        def gate(gated, planes, b):
+            for t in range(PACK):
+                nc.vector.tensor_scalar(gated[:, t, :], planes[:, t, :], rw_sb[:, b, t : t + 1], None, ALU.mult)
+
+        def score_gradient(planes, banks, pw, b, cols):
+            for t in range(PACK):
+                nc.vector.scalar_tensor_tensor(planes[:, t, :], banks[t][:, cols], delta_sb[:, b, t : t + 1], pw[:, t, :], ALU.subtract, ALU.mult)
+
+        V, S, G = nc.vector, nc.scalar, nc.gpsimd
+
+        k_planes = [load_plane(kT, 0, "k_plane0", K0)]
         nc.sync.dma_start(offsets[:], offs)
-        k_parts.append(load_pair_part(kT, 0, T // 2, T, "part1"))
-        k_parts.append(load_pair_part(kT, 1, 0, T // 2, "part2"))
-        k_parts.append(load_pair_part(kT, 1, T // 2, 3 * T // 4, "part3"))
-        k_parts.append(load_pair_part(kT, 1, 3 * T // 4, T, "part4"))
-        q0_raw = [load_rows(qT[0], "q0_raw%d" % h, h * HALF, (h + 1) * HALF) for h in range(2)]
+        k_planes.extend(load_plane(kT, j, "k_plane%d" % j, (K0, K1, K2, K3)[j]) for j in range(1, PACK))
+        q0_raw = [load_rows(qT[0], "q0_raw%d" % h, (Q0A, Q0B)[h], HALVES[h]) for h in range(2)]
         lse_sb = load_per_row(lse, "lse_sb")
-        dom0_raw = [load_rows(dom[0], "raw5", 0, HALF)]
+        dom0_raw = [load_rows(dom[0], "dom0_raw0", DOM0A, HALVES[0])]
         rw_sb = load_per_row(rw, "rw_sb")
+        dom0_raw.append(load_rows(dom[0], "dom0_raw1", DOM0B, HALVES[1]))
+        q1_raw = load_rows(qT[1], "q1_raw", Q1)
+        dom1_raw = load_rows(dom[1], "dom1_raw", DOM1)
+        do0_raw = load_rows(doT[0], "do0_raw", DO0)
+        v_planes = [load_plane(vT, j, "v_plane%d" % j, (V0, V1, V2, V3)[j]) for j in range(PACK)]
         delta_sb = load_per_row(delta, "delta_sb")
-        q1_raw = load_rows(qT[1], "raw1")
-        dom0_raw.append(load_rows(dom[0], "raw4", HALF, W))
-        dom1_raw = load_rows(dom[1], "raw2")
+        qm0_raw = load_rows(qm[0], "qm0_raw", QM0)
+        do1_raw = load_rows(doT[1], "do1_raw", DO1)
+        qm1_raw = load_rows(qm[1], "qm1_raw", QM1)
 
-        windows = [keep.tile([P, T], F32, name="window%d" % j) for j in range(PACK)]
-        for window in windows:
+        dv_windows = [keep.tile([P, T], F32, name="window%d" % j) for j in range(PACK)]
+        for window in dv_windows:
             nc.vector.memset(window[:], 0.0)
 
-        k_pairs = [new_pairs(0), new_pairs(1)]
-        for h in range(2):
-            cast_pairs_shared(k_pairs[0], k_parts[h], h * (T // 2), 672)
-        k0_grouped = [new_grouped("k0_%d" % h, HALF) for h in range(2)]
-        k1_grouped = [new_grouped("g1", HALF)]
-        half_lists = [offsets[:, h * (LIST_COLS // 2) : (h + 1) * (LIST_COLS // 2)] for h in range(2 * B)]
-        for h in range(2):
-            nc.vector.tensor_copy(pair_words(k0_grouped[h][:], 0), k_pairs[0][:].indirect(half_lists[h]))
-        nc.vector.tensor_copy(pair_words(k1_grouped[0][:], 0), k_pairs[0][:].indirect(half_lists[2]))
-        cast_pairs(k_pairs[1], k_parts[2][:], 0)
-        cast_pairs(k_pairs[1], k_parts[3][:], T // 2, on_vector=True)
-        cast_pairs_shared(k_pairs[1], k_parts[4], 3 * T // 4, 352)
-        k0 = new_operand(E4, "b")
-        for h in range(2):
-            nc.vector.tensor_copy(pair_words(k0_grouped[h][:], 1), k_pairs[1][:].indirect(half_lists[h]))
-            quantise(k0, k0_grouped[h][:], h * HALF)
-        nc.vector.tensor_copy(pair_words(k1_grouped[0][:], 1), k_pairs[1][:].indirect(half_lists[2]))
-        q0_grouped = new_grouped("g0")
-        for h in range(2):
-            cast_dealt(q0_grouped[:], q0_raw[h][:], h * (P // 2))
-        q0 = new_operand(E4, "a")
+        k0_low = new_planes("k0_low", X, BF16, N, 2)
+        k1_gathered = new_planes("k1_gathered", X + 2 * KB, BF16)
+        k0_grouped = new_grouped("k0_grouped", X + 6 * KB)
+        k1_grouped = new_grouped("k1_grouped", X + 10 * KB)
+        for j in range(2):
+            gather_plane(k0_low[:, j, :], k_planes[j], listed(0))
+            gather_plane(k1_gathered[:, j, :], k_planes[j], listed(1))
+        nc.scalar.copy(
+            out=k0_grouped[:].rearrange("p (n j) -> p n j", j=PACK)[:, :, 0:2],
+            in_=k0_low[:].rearrange("p j n -> p n j"),
+        )
+        for j in range(2, PACK):
+            gather_into_place(k0_grouped[:], j, k_planes[j], listed(0))
+            gather_plane(k1_gathered[:, j, :], k_planes[j], listed(1))
+        spare_window = work.tile([P, T], F32, name="spare_window", offset=K0, align_bytes=64)
+        nc.gpsimd.memset(spare_window[:], 0.0)
+        dk_windows = [dv_windows[0], spare_window, dv_windows[3], dv_windows[1]]
+        q0_grouped = new_grouped("q0_grouped", X + 14 * KB)
+        deal(V, q0_grouped[:], q0_raw[0][:])
+        k0 = quantised(k0_grouped, E4, "k0", X + 18 * KB)
+        deal(V, q0_grouped[:], q0_raw[1][:], P // 2)
+        weave(S, k1_grouped[:], k1_gathered[:])
+        neg_lse1 = negated("neg_lse1", X + 29 * KB, lse_sb[:, 1, :])
+        neg_lse0 = negated("neg_lse0", X + 6 * KB, lse_sb[:, 0, :])
+        q0 = new_operand(E4, "q0", X + 20 * KB)
         for h in range(2):
             quantise(q0, q0_grouped[:, h * 2 * W : (h + 1) * 2 * W], h * HALF)
-        k1_grouped.append(new_grouped("g0", HALF))
-        for u in range(2):
-            nc.vector.tensor_copy(pair_words(k1_grouped[1][:], u), k_pairs[u][:].indirect(half_lists[3]))
-        neg_lse1 = work.tile([P, PACK], F32, name="neg_lse1", tag="after_exp1", align_bytes=64)
-        nc.scalar.mul(neg_lse1[:], lse_sb[:, 1, :], -1.0)
-        dom0_grouped = [new_grouped("g2", HALF)]
-        cast_plain(dom0_grouped[0][:], dom0_raw[0][:])
-        neg_lse0 = work.tile([P, PACK], F32, name="neg_lse0", tag="raw5", align_bytes=64)
-        nc.scalar.mul(neg_lse0[:], lse_sb[:, 0, :], -1.0)
-        p0 = [new_planes("p0_%d" % h, HALF) for h in range(2)]
+        dom0_grouped = new_grouped("dom0_grouped", X + 14 * KB)
+        weave(V, dom0_grouped[:, 0 : 2 * W], dom0_raw[0][:])
+        k1 = quantised(k1_grouped, E4, "k1", Q0B)
+        weave(V, dom0_grouped[:, 2 * W : 4 * W], dom0_raw[1][:])
+        pw0_planes = [new_planes("pw0_planes%d" % h, Y + 4 * KB * h, F32, HALF) for h in range(2)]
         for h in range(2):
-            for t in range(PACK):
-                bank = psum.tile([P, HALF], F32, name="half_bank", tag="%s%d" % (("score", "grad")[h], t))
-                product_into(bank[:], q0, t, k0, slice(h * HALF, (h + 1) * HALF))
-                nc.scalar.activation(out=p0[h][:, t, :], in_=bank[:], func=ACT.Exp, bias=neg_lse0[:, t : t + 1])
-        v_rows = [load_pair_part(vT, u, 0, T, "part%d" % (2 * u)) for u in range(2)]
-        do0_raw = load_rows(doT[0], "part1")
+            banks = [product("bank%d" % (4 * h + t), q0, t, k0, HALVES[h]) for t in range(PACK)]
+            weights(pw0_planes[h], banks, neg_lse0)
+        pw0 = new_operand(E4, "pw0", X + 24 * KB)
+        pw0_grouped = [new_grouped("pw0_grouped%d" % h, Q0A + 2 * KB * h, HALF) for h in range(2)]
+        gate(pw0_planes[0], pw0_planes[0], 0)
+        dom0 = quantised(dom0_grouped, E5, "dom0", X + 22 * KB)
+        weave(V, pw0_grouped[0][:], pw0_planes[0][:])
+        q1_grouped = new_grouped("q1_grouped", X + 6 * KB)
+        deal(S, q1_grouped[:], q1_raw[:])
+        gate(pw0_planes[1], pw0_planes[1], 0)
+        quantise(pw0, pw0_grouped[0][:], 0)
+        b0 = [product("bank0", dom0, 1, pw0, HALVES[0])]
+        a0 = [product("bank1", dom0, 0, pw0, HALVES[0])]
+        weave(V, pw0_grouped[1][:], pw0_planes[1][:])
+        staged_b0 = [stage(S, b0[0][:], "staged_b0_0", Q1)]
+        staged_a0 = [stage(S, a0[0][:], "staged_a0_0", Q1 + KB)]
+        q1 = new_operand(E4, "q1", X + 18 * KB)
+        quantise(q1, q1_grouped[:, 0 : 2 * W], 0)
+        quantise(pw0, pw0_grouped[1][:], HALF)
+        quantise(q1, q1_grouped[:, 2 * W : 4 * W], HALF)
+        a0.append(product("bank2", dom0, 0, pw0, HALVES[1]))
+        scores1 = [product("bank%d" % (4 + t), q1, t, k1) for t in range(PACK)]
+        b0.append(product("bank3", dom0, 1, pw0, HALVES[1]))
+        c0 = product("bank0", dom0, 2, pw0)
+        d0 = product("bank1", dom0, 3, pw0)
+        scatter(S, dv_windows[1], staged_b0[0][:], 0, HALVES[0])
+        dom1_grouped = new_grouped("dom1_grouped", X + 6 * KB)
+        weave(G, dom1_grouped[:], dom1_raw[:])
+        scatter(V, dv_windows[0], staged_a0[0][:], 0, HALVES[0])
+        staged_a0.append(stage(V, a0[1][:], "staged_a0_1", X + 28 * KB))
+        scatter(V, dv_windows[0], staged_a0[1][:], 0, HALVES[1])
+        p1 = new_planes("p1", K1, F32)
+        weights(p1, scores1, neg_lse1)
 
-        dom0 = [new_operand(E5, "c")]
-        quantise(dom0[0], dom0_grouped[0][:])
-        pw0 = new_operand(E4, "d")
-        pw0_grouped = [new_grouped("k0_%d" % h, HALF) for h in range(2)]
-        gates0 = rw_sb[:, 0, :].rearrange("p (c j i) -> p c j i", c=1, i=1).broadcast_to([P, HALF // 2, PACK, 2])
+        staged_c0 = stage(V, c0[:], "staged_c0", DOM1 + 2 * KB)
+        dom1 = quantised(dom1_grouped, E5, "dom1", X + 20 * KB)
+        pw1_planes = [new_planes("pw1_planes%d" % h, (DOM1 + 4 * KB, X + 6 * KB)[h], F32, HALF) for h in range(2)]
+        gate(pw1_planes[0], p1[:, :, HALVES[0]], 1)
+        gate(pw1_planes[1], p1[:, :, HALVES[1]], 1)
+        pw1_grouped = new_grouped("pw1_grouped", K1)
         for h in range(2):
-            nc.vector.tensor_tensor(woven(pw0_grouped[h][:], 2), planes_woven(p0[h][:], 2), gates0, ALU.mult)
-        for h in range(2):
-            quantise(pw0, pw0_grouped[h][:], h * HALF)
-        dv0 = [new_bank("grad%d" % j) for j in range(PACK)]
-        for j in range(2):
-            product_into(dv0[j][:], dom0[0], j, pw0, slice(0, W))
-
-        q1_grouped = new_grouped("raw5")
-        cast_dealt(q1_grouped[:], q1_raw[:])
-        qm0_raw = load_rows(qm[0], "raw1")
-        dom0_grouped.append(new_grouped("k0_0", HALF))
-        nc.vector.tensor_copy(woven(dom0_grouped[1][:], 4), planes_woven(dom0_raw[1][:], 4))
-        do1_raw = load_rows(doT[1], "raw4")
-        k1 = new_operand(E4, "e", codes_tag="k0_1")
-        for h in range(2):
-            quantise(k1, k1_grouped[h][:], h * HALF)
-        dom0.append(new_operand(E5, "c2"))
-        quantise(dom0[1], dom0_grouped[1][:])
-        q1 = quantised(q1_grouped, E4, "f")
-        for j in range(2):
-            product_into(dv0[2 + j][:], dom0[1], j, pw0, slice(0, W))
-        neg_rw_delta = [work.tile([P, PACK], F32, name="neg_rw_delta", tag="after_centred%d" % b, align_bytes=64) for b in range(B)]
-        for b in range(B):
-            nc.vector.scalar_tensor_tensor(neg_rw_delta[b][:], rw_sb[:, b, :], -1.0, delta_sb[:, b, :], ALU.mult, ALU.mult)
-        dom1_grouped = new_grouped("raw5")
-        cast_plain_gpsimd(dom1_grouped[:], dom1_raw[:])
-
-        put(dv0[0], 0, 0)
-        put(dv0[1], 1, 0)
-        scores1 = products("score", q1, k1)
-        p1 = new_planes("p1")
-        pw1_planes = new_planes("raw2")
-        for t in range(PACK):
-            nc.scalar.activation(out=p1[:, t, :], in_=scores1[t][:], func=ACT.Exp, bias=neg_lse1[:, t : t + 1])
-            nc.gpsimd.tensor_scalar(pw1_planes[:, t, :], p1[:, t, :], rw_sb[:, 1, t : t + 1], 0.0, ALU.mult, ALU.add)
-        put(dv0[2], 2, 0)
-        put(dv0[3], 3, 0, tag="codes_dom1")
-        pw1_grouped = new_grouped("g1")
-        cast_plain_gpsimd(pw1_grouped[:], pw1_planes[:])
-        do0_grouped = [new_grouped("raw2", HALF)]
-        cast_dealt_pair_gpsimd(do0_grouped[0][:], do0_raw[:], 0)
-        v_pairs = [work.tile([P, T], U32, name="pairs", tag="after_exp1", align_bytes=64), new_pairs(1)]
-        for n in range(4):
-            cast_pairs(v_pairs[n // 2], v_rows[n // 2][:, :, (n % 2) * (T // 2) : (n % 2 + 1) * (T // 2)], (n % 2) * (T // 2))
-        qm1_raw = load_rows(qm[1], "part0")
-        pw1 = quantised(pw1_grouped, E4, "a")
-        dom1 = quantised(dom1_grouped, E5, "dom1")
-        dv1 = products("grad", dom1, pw1)
-
-        v0_gathered = work.tile([P, 2, W], U32, name="v0_gathered", tag="gathered", align_bytes=64)
-        for u in range(2):
-            nc.vector.tensor_copy(v0_gathered[:, u, :], v_pairs[u][:].indirect(lists[0]))
-        do0_grouped.append(new_grouped("part2", HALF))
-        cast_dealt_pair(do0_grouped[1][:], do0_raw[:], 2)
-        do0 = new_operand(E5, "e")
-        for h in range(2):
-            quantise(do0, do0_grouped[h][:], h * HALF)
-        qm0_grouped = [new_grouped("part2", HALF)]
-        cast_plain_gpsimd(qm0_grouped[0][:], qm0_raw[:, :, 0:HALF])
-        after_do0 = new_grouped("part1", 2 * W + HALF)
-        put(dv1[0], 0, 1, out=out_1, staged=after_do0[:, 2 * PACK * W :].bitcast(F32))
-        do1_grouped = after_do0[:, PACK * W : 2 * PACK * W]
-        cast_dealt(do1_grouped, do1_raw[:, :, 0:HALF])
-        v0_grouped = after_do0[:, 0 : PACK * W]
-        weave_pairs(v0_grouped, v0_gathered[:])
-        v0 = quantised(v0_grouped, E4, "f")
-        qm0 = new_operand(E4, "c")
-        quantise(qm0, qm0_grouped[0][:])
-        cast_dealt(do1_grouped, do1_raw[:, :, HALF:W], P // 2)
-        do1 = quantised(do1_grouped, E5, "a")
-        qm0_grouped.append(new_grouped("gathered", HALF))
-        cast_plain(qm0_grouped[1][:], qm0_raw[:, :, HALF:W])
-        quantise(qm0, qm0_grouped[1][:], HALF)
-        after_do1 = work.tile([P, 3 * W], U32, name="after_do1", tag="raw1", align_bytes=64)
-        v1_gathered = after_do1[:, 0 : 2 * W].rearrange("p (u c) -> p u c", u=2)
-        for u in range(2):
-            nc.vector.tensor_copy(after_do1[:, u * W : (u + 1) * W], v_pairs[u][:].indirect(lists[1]))
-        put(dv1[1], 1, 1, out=out_1, staged=after_do1[:, 2 * W : 3 * W].bitcast(F32))
-        dp0 = products("score", do0, v0)
-        g0 = [new_planes("g0_%d" % h, HALF) for h in range(2)]
-        ds0_planes = [new_planes(("ds0_0", "q0_raw0")[h], HALF) for h in range(2)]
-        for h in range(2):
-            centred(g0[h], dp0, h, neg_rw_delta[0], rw_sb[:, 0, :])
-            nc.gpsimd.tensor_tensor(ds0_planes[h][:], g0[h][:], p0[h][:], ALU.mult)
-        after_centred = new_grouped("after_centred0", W + HALF)
-        put(dv1[2], 2, 1, out=out_1, staged=after_centred[:, PACK * W :].bitcast(F32))
-        v1_grouped = after_centred[:, 0 : PACK * W]
-        weave_pairs(v1_grouped, v1_gathered)
-        ds0_grouped = new_grouped("g0")
-        cast_plain(ds0_grouped[:, 0 : 2 * W], ds0_planes[0][:])
-        cast_plain(ds0_grouped[:, 2 * W : 4 * W], ds0_planes[1][:])
-        v1 = quantised(v1_grouped, E4, "f")
-        ds0 = quantised(ds0_grouped, E5, "d")
-        put(dv1[3], 3, 1, tag="q0_raw0", out=out_1)
-        dk0 = products("grad", qm0, ds0)
-
-        put(dk0[0], 0, 0)
-        dp1 = products("score", do1, v1)
-        g1_planes = new_planes("g0")
-        g1 = [g1_planes[:, :, h * HALF : (h + 1) * HALF] for h in range(2)]
-        ds1_planes = [new_planes("p0_%d" % h, HALF) for h in range(2)]
-        for h in range(2):
-            centred(g1[h], dp1, h, neg_rw_delta[1], rw_sb[:, 1, :])
-            nc.gpsimd.tensor_tensor(ds1_planes[h][:], g1[h], p1[:, :, h * HALF : (h + 1) * HALF], ALU.mult)
-        put(dk0[1], 1, 0)
-        put(dk0[2], 2, 0)
-        ds1_grouped = new_grouped("g1")
-        for h in range(2):
-            cast_plain(ds1_grouped[:, h * 2 * W : (h + 1) * 2 * W], ds1_planes[h][:])
-        qm1_grouped = new_grouped("after_centred1")
-        for h in range(2):
-            cast_plain(qm1_grouped[:, h * 2 * W : (h + 1) * 2 * W], qm1_raw[:, :, h * HALF : (h + 1) * HALF])
-        qm1 = quantised(qm1_grouped, E4, "e")
-        ds1 = quantised(ds1_grouped, E5, "b")
-        put(dk0[3], 3, 0, tag="p0_1")
-        dk1 = products("grad", qm1, ds1)
+            weave(G, pw1_grouped[:, h * 2 * W : (h + 1) * 2 * W], pw1_planes[h][:])
+        scatter(V, dv_windows[2], staged_c0[:], 0)
+        v_gathered = [new_planes("v_gathered%d" % b, K2 + 4 * KB * b, BF16) for b in range(B)]
         for j in range(PACK):
-            put(dk1[j], j, 1, out=out_0)
+            for b in range(B):
+                gather_plane(v_gathered[b][:, j, :], v_planes[j], listed(b))
+        pw1 = quantised(pw1_grouped, E4, "pw1", X + 26 * KB)
+        dv1 = [product("bank%d" % (0, 4, 2, 5)[j], dom1, j, pw1) for j in range(PACK)]
+        do0_grouped = new_grouped("do0_grouped", K1)
+        deal(V, do0_grouped[:], do0_raw[:])
+        v0_grouped = new_grouped("v0_grouped", K3)
+        weave(V, v0_grouped[:], v_gathered[0][:])
+        do0 = quantised(do0_grouped, E5, "do0", X + 18 * KB)
+        staged_a1 = [stage(V, dv1[0][:, HALVES[0]], "staged_a1_0", K2)]
+        v0 = quantised(v0_grouped, E4, "v0", Q0B)
+        staged_b0.append(stage(S, b0[1][:], "staged_b0_1", V3))
+        staged_d0 = stage(S, d0[:], "staged_d0", V3 + 6 * KB)
+        dp0 = [product("bank%d" % (6, 7, 3, 1)[t], do0, t, v0) for t in range(PACK)]
+        qm0_grouped = new_grouped("qm0_grouped", K3)
+        weave(G, qm0_grouped[:], qm0_raw[:])
+        scatter(V, dv_windows[0], staged_a1[0][:], 1, HALVES[0])
+        scatter(S, dv_windows[3], staged_d0[:, HALVES[0]], 0, HALVES[0])
+        scatter(S, dv_windows[1], staged_b0[1][:], 0, HALVES[1])
+        scatter(S, dv_windows[3], staged_d0[:, HALVES[1]], 0, HALVES[1])
+        staged_b1 = [stage(S, dv1[1][:, HALVES[0]], "staged_b1_0", V3 + 2 * KB)]
+        staged_d1 = [stage(S, dv1[3][:, HALVES[0]], "staged_d1_0", V3 + 4 * KB)]
+        ds0_planes = [new_planes("ds0_planes%d" % h, DOM0A + 2 * KB * h, BF16, HALF) for h in range(2)]
+        ds0_grouped = new_grouped("ds0_grouped", Q0A)
+        score_gradient(ds0_planes[0], dp0, pw0_planes[0], 0, HALVES[0])
+        staged_a1.append(stage(V, dv1[0][:, HALVES[1]], "staged_a1_1", Y))
+        score_gradient(ds0_planes[1], dp0, pw0_planes[1], 0, HALVES[1])
+        for h in range(2):
+            weave(G, ds0_grouped[:, h * 2 * W : (h + 1) * 2 * W], ds0_planes[h][:])
+        scatter(V, dv_windows[0], staged_a1[1][:], 1, HALVES[1])
+        store(out_1, 0, dv_windows[0])
+        scatter(S, dv_windows[1], staged_b1[0][:], 1, HALVES[0])
+        staged_b1.append(stage(S, dv1[1][:, HALVES[1]], "staged_b1_1", Y))
+        scatter(S, dv_windows[3], staged_d1[0][:], 1, HALVES[0])
+        scatter(S, dv_windows[1], staged_b1[1][:], 1, HALVES[1])
+        store(out_1, 1, dv_windows[1])
+        ds0 = quantised(ds0_grouped, E5, "ds0", X + 22 * KB)
+        do1_grouped = [None, new_grouped("do1_grouped1", DOM0A + 3 * KB, HALF)]
+        deal_half(V, do1_grouped[1][:], do1_raw[:], 1)
+        qm0 = quantised(qm0_grouped, E4, "qm0", DOM0A + KB)
+        staged_c1 = [stage(V, dv1[2][:, HALVES[0]], "staged_c1_0", K3 + 2 * KB)]
+        dk0 = [product("bank%d" % (0, 6, 7, 1)[j], qm0, j, ds0) for j in range(PACK)]
+        do1_grouped[0] = new_grouped("do1_grouped0", K3, HALF)
+        deal_half(G, do1_grouped[0][:], do1_raw[:], 0)
+        staged_d1.append(stage(S, dv1[3][:, HALVES[1]], "staged_d1_1", Q0A))
+        staged_c1.append(stage(S, dv1[2][:, HALVES[1]], "staged_c1_1", V3 + KB))
+        scatter(S, dv_windows[3], staged_d1[1][:], 1, HALVES[1])
+        store(out_1, 3, dv_windows[3])
+        scatter(V, dv_windows[2], staged_c1[0][:], 1, HALVES[0])
+        staged_f0 = stage(S, dk0[1][:], "staged_f0", V2)
+        scatter(S, dv_windows[2], staged_c1[1][:], 1, HALVES[1])
+        store(out_1, 2, dv_windows[2])
+        v1_grouped = new_grouped("v1_grouped", DO1)
+        weave(V, v1_grouped[:], v_gathered[1][:])
+        do1 = new_operand(E5, "do1", DO1 + 4 * KB)
+        for h in range(2):
+            quantise(do1, do1_grouped[h][:], h * HALF)
+        staged_e0 = [stage(V, dk0[0][:, HALVES[0]], "staged_e0_0", K2 + 4 * KB)]
+        v1 = quantised(v1_grouped, E4, "v1", Q0B)
+        dp1 = [product("bank%d" % (2, 3, 4, 5)[t], do1, t, v1) for t in range(PACK)]
+        qm1_grouped = new_grouped("qm1_grouped", DO1)
+        weave(G, qm1_grouped[:], qm1_raw[:])
+        scatter(V, dk_windows[0], staged_e0[0][:], 0, HALVES[0])
+        scatter(S, dk_windows[1], staged_f0[:, HALVES[0]], 0, HALVES[0])
+        staged_h0 = stage(S, dk0[3][:], "staged_h0", V2 + 2 * KB)
+        scatter(S, dk_windows[1], staged_f0[:, HALVES[1]], 0, HALVES[1])
+        ds1_planes = [new_planes("ds1_planes%d" % h, QM0 + 2 * KB * h, BF16, HALF) for h in range(2)]
+        ds1_grouped = new_grouped("ds1_grouped", QM0 + 4 * KB)
+        score_gradient(ds1_planes[0], dp1, pw1_planes[0], 1, HALVES[0])
+        staged_e0.append(stage(V, dk0[0][:, HALVES[1]], "staged_e0_1", DOM1 + 4 * KB))
+        score_gradient(ds1_planes[1], dp1, pw1_planes[1], 1, HALVES[1])
+        for h in range(2):
+            weave(G, ds1_grouped[:, h * 2 * W : (h + 1) * 2 * W], ds1_planes[h][:])
+        scatter(V, dk_windows[0], staged_e0[1][:], 0, HALVES[1])
+        scatter(S, dk_windows[3], staged_h0[:], 0)
+        qm1 = quantised(qm1_grouped, E4, "qm1", QM0 + 2 * KB)
+        ds1 = quantised(ds1_grouped, E5, "ds1", X + 24 * KB)
+        dk1 = [product("bank%d" % (2, 3, 4, 5)[j], qm1, j, ds1) for j in range(PACK)]
+        staged_g0 = stage(V, dk0[2][:], "staged_g0", DO1)
+        scatter(V, dk_windows[2], staged_g0[:, HALVES[0]], 0, HALVES[0])
+        staged_f1 = [stage(S, dk1[1][:, HALVES[h]], "staged_f1_%d" % h, V1 + KB + 4 * KB * h) for h in range(2)]
+        staged_e1 = stage(V, dk1[0][:], "staged_e1", V0)
+        scatter(S, dk_windows[1], staged_f1[0][:], 1, HALVES[0])
+        scatter(S, dk_windows[1], staged_f1[1][:], 1, HALVES[1])
+        staged_h1 = [stage(S, dk1[3][:, HALVES[h]], "staged_h1_%d" % h, V1 + KB * h + KB // 2) for h in range(2)]
+        store(out_0, 1, dk_windows[1])
+        scatter(V, dk_windows[0], staged_e1[:], 1)
+        store(out_0, 0, dk_windows[0])
+        scatter(S, dk_windows[3], staged_h1[0][:], 1, HALVES[0])
+        scatter(V, dk_windows[2], staged_g0[:, HALVES[1]], 0, HALVES[1])
+        staged_g1 = stage(V, dk1[2][:], "staged_g1", V1 - KB)
+        scatter(S, dk_windows[3], staged_h1[1][:], 1, HALVES[1])
+        store(out_0, 3, dk_windows[3])
+        scatter(V, dk_windows[2], staged_g1[:], 1)
+        store(out_0, 2, dk_windows[2])

@@ -28,7 +28,6 @@ Q0A, Q0B, DOM0A, DOM0B = (64 * KB + 4 * KB * n for n in range(4))
 Q1, DOM1, DO0, QM0, DO1, QM1 = (80 * KB + 8 * KB * n for n in range(6))
 SCALES = 128 * KB
 X = 136 * KB
-Y = 166 * KB
 
 
 def tile_attend_gat_lse_kv_kernel(tc, qT, kT, vT, doT, lse, delta, rw, qm, dom, offs, out_0, out_1):
@@ -206,40 +205,31 @@ def tile_attend_gat_lse_kv_kernel(tc, qT, kT, vT, doT, lse, delta, rw, qm, dom, 
 
         dv_windows = [keep.tile([P, T], F32, name="window%d" % j) for j in range(PACK)]
         for window in dv_windows:
-            nc.vector.memset(window[:], 0.0)
+            nc.vector.memset(window[:].bitcast(U32), 0)
 
-        k0_low = new_planes("k0_low", X, BF16, N, 2)
         k1_gathered = new_planes("k1_gathered", X + 2 * KB, BF16)
         k0_grouped = new_grouped("k0_grouped", X + 6 * KB)
-        k1_grouped = new_grouped("k1_grouped", X + 10 * KB)
-        for j in range(2):
-            gather_plane(k0_low[:, j, :], k_planes[j], listed(0))
-            gather_plane(k1_gathered[:, j, :], k_planes[j], listed(1))
-        nc.scalar.copy(
-            out=k0_grouped[:].rearrange("p (n j) -> p n j", j=PACK)[:, :, 0:2],
-            in_=k0_low[:].rearrange("p j n -> p n j"),
-        )
-        for j in range(2, PACK):
+        for j in range(PACK):
             gather_into_place(k0_grouped[:], j, k_planes[j], listed(0))
             gather_plane(k1_gathered[:, j, :], k_planes[j], listed(1))
-        spare_window = work.tile([P, T], F32, name="spare_window", offset=K0, align_bytes=64)
-        nc.gpsimd.memset(spare_window[:], 0.0)
-        dk_windows = [dv_windows[0], spare_window, dv_windows[3], dv_windows[1]]
+        dk_windows = [dv_windows[0], dv_windows[1], dv_windows[3], dv_windows[2]]
         q0_grouped = new_grouped("q0_grouped", X + 14 * KB)
-        deal(V, q0_grouped[:], q0_raw[0][:])
+        deal(S, q0_grouped[:], q0_raw[0][:])
         k0 = quantised(k0_grouped, E4, "k0", X + 18 * KB)
         deal(V, q0_grouped[:], q0_raw[1][:], P // 2)
-        weave(S, k1_grouped[:], k1_gathered[:])
-        neg_lse1 = negated("neg_lse1", X + 29 * KB, lse_sb[:, 1, :])
+        k1_grouped = new_grouped("k1_grouped", Q0A)
+        weave(S, k1_grouped[:, 0 : 3 * W], k1_gathered[:, :, 0:384])
         neg_lse0 = negated("neg_lse0", X + 6 * KB, lse_sb[:, 0, :])
+        neg_lse1 = negated("neg_lse1", X + 29 * KB, lse_sb[:, 1, :])
         q0 = new_operand(E4, "q0", X + 20 * KB)
         for h in range(2):
             quantise(q0, q0_grouped[:, h * 2 * W : (h + 1) * 2 * W], h * HALF)
         dom0_grouped = new_grouped("dom0_grouped", X + 14 * KB)
+        weave(V, k1_grouped[:, 3 * W : 4 * W], k1_gathered[:, :, 384:512])
         weave(V, dom0_grouped[:, 0 : 2 * W], dom0_raw[0][:])
         k1 = quantised(k1_grouped, E4, "k1", Q0B)
         weave(V, dom0_grouped[:, 2 * W : 4 * W], dom0_raw[1][:])
-        pw0_planes = [new_planes("pw0_planes%d" % h, Y + 4 * KB * h, F32, HALF) for h in range(2)]
+        pw0_planes = [new_planes("pw0_planes%d" % h, K0 + 4 * KB * h, F32, HALF) for h in range(2)]
         for h in range(2):
             banks = [product("bank%d" % (4 * h + t), q0, t, k0, HALVES[h]) for t in range(PACK)]
             weights(pw0_planes[h], banks, neg_lse0)
@@ -275,11 +265,11 @@ def tile_attend_gat_lse_kv_kernel(tc, qT, kT, vT, doT, lse, delta, rw, qm, dom, 
         p1 = new_planes("p1", K1, F32)
         weights(p1, scores1, neg_lse1)
 
-        staged_c0 = stage(V, c0[:], "staged_c0", DOM1 + 2 * KB)
         dom1 = quantised(dom1_grouped, E5, "dom1", X + 20 * KB)
         pw1_planes = [new_planes("pw1_planes%d" % h, (DOM1 + 4 * KB, X + 6 * KB)[h], F32, HALF) for h in range(2)]
         gate(pw1_planes[0], p1[:, :, HALVES[0]], 1)
         gate(pw1_planes[1], p1[:, :, HALVES[1]], 1)
+        staged_c0 = stage(V, c0[:], "staged_c0", K1 + 4 * KB)
         pw1_grouped = new_grouped("pw1_grouped", K1)
         for h in range(2):
             weave(G, pw1_grouped[:, h * 2 * W : (h + 1) * 2 * W], pw1_planes[h][:])
@@ -309,75 +299,74 @@ def tile_attend_gat_lse_kv_kernel(tc, qT, kT, vT, doT, lse, delta, rw, qm, dom, 
         staged_b1 = [stage(S, dv1[1][:, HALVES[0]], "staged_b1_0", V3 + 2 * KB)]
         staged_d1 = [stage(S, dv1[3][:, HALVES[0]], "staged_d1_0", V3 + 4 * KB)]
         ds0_planes = [new_planes("ds0_planes%d" % h, DOM0A + 2 * KB * h, BF16, HALF) for h in range(2)]
-        ds0_grouped = new_grouped("ds0_grouped", Q0A)
+        ds0_grouped = [new_grouped("ds0_grouped%d" % h, (Q0A, DOM0A)[h], HALF) for h in range(2)]
         score_gradient(ds0_planes[0], dp0, pw0_planes[0], 0, HALVES[0])
-        staged_a1.append(stage(V, dv1[0][:, HALVES[1]], "staged_a1_1", Y))
+        staged_a1.append(stage(V, dv1[0][:, HALVES[1]], "staged_a1_1", K0))
         score_gradient(ds0_planes[1], dp0, pw0_planes[1], 0, HALVES[1])
-        for h in range(2):
-            weave(G, ds0_grouped[:, h * 2 * W : (h + 1) * 2 * W], ds0_planes[h][:])
+        weave(G, ds0_grouped[0][:], ds0_planes[0][:])
         scatter(V, dv_windows[0], staged_a1[1][:], 1, HALVES[1])
         store(out_1, 0, dv_windows[0])
         scatter(S, dv_windows[1], staged_b1[0][:], 1, HALVES[0])
-        staged_b1.append(stage(S, dv1[1][:, HALVES[1]], "staged_b1_1", Y))
+        staged_b1.append(stage(S, dv1[1][:, HALVES[1]], "staged_b1_1", K0))
         scatter(S, dv_windows[3], staged_d1[0][:], 1, HALVES[0])
         scatter(S, dv_windows[1], staged_b1[1][:], 1, HALVES[1])
         store(out_1, 1, dv_windows[1])
-        ds0 = quantised(ds0_grouped, E5, "ds0", X + 22 * KB)
-        do1_grouped = [None, new_grouped("do1_grouped1", DOM0A + 3 * KB, HALF)]
-        deal_half(V, do1_grouped[1][:], do1_raw[:], 1)
-        qm0 = quantised(qm0_grouped, E4, "qm0", DOM0A + KB)
-        staged_c1 = [stage(V, dv1[2][:, HALVES[0]], "staged_c1_0", K3 + 2 * KB)]
+        weave(V, ds0_grouped[1][:], ds0_planes[1][:])
+        ds0 = new_operand(E5, "ds0", X + 22 * KB)
+        quantise(ds0, ds0_grouped[0][:], 0)
+        do1_grouped = new_grouped("do1_grouped", Q0A)
+        quantise(ds0, ds0_grouped[1][:], HALF)
+        deal(V, do1_grouped[:], do1_raw[:])
+        qm0 = quantised(qm0_grouped, E4, "qm0", DOM0A + 2 * KB)
         dk0 = [product("bank%d" % (0, 6, 7, 1)[j], qm0, j, ds0) for j in range(PACK)]
-        do1_grouped[0] = new_grouped("do1_grouped0", K3, HALF)
-        deal_half(G, do1_grouped[0][:], do1_raw[:], 0)
-        staged_d1.append(stage(S, dv1[3][:, HALVES[1]], "staged_d1_1", Q0A))
-        staged_c1.append(stage(S, dv1[2][:, HALVES[1]], "staged_c1_1", V3 + KB))
+        staged_d1.append(stage(S, dv1[3][:, HALVES[1]], "staged_d1_1", DOM0A))
+        staged_c1 = stage(S, dv1[2][:], "staged_c1", K3)
         scatter(S, dv_windows[3], staged_d1[1][:], 1, HALVES[1])
         store(out_1, 3, dv_windows[3])
-        scatter(V, dv_windows[2], staged_c1[0][:], 1, HALVES[0])
-        staged_f0 = stage(S, dk0[1][:], "staged_f0", V2)
-        scatter(S, dv_windows[2], staged_c1[1][:], 1, HALVES[1])
-        store(out_1, 2, dv_windows[2])
         v1_grouped = new_grouped("v1_grouped", DO1)
         weave(V, v1_grouped[:], v_gathered[1][:])
-        do1 = new_operand(E5, "do1", DO1 + 4 * KB)
-        for h in range(2):
-            quantise(do1, do1_grouped[h][:], h * HALF)
+        do1 = quantised(do1_grouped, E5, "do1", DO1 + 4 * KB)
         staged_e0 = [stage(V, dk0[0][:, HALVES[0]], "staged_e0_0", K2 + 4 * KB)]
         v1 = quantised(v1_grouped, E4, "v1", Q0B)
         dp1 = [product("bank%d" % (2, 3, 4, 5)[t], do1, t, v1) for t in range(PACK)]
         qm1_grouped = new_grouped("qm1_grouped", DO1)
         weave(G, qm1_grouped[:], qm1_raw[:])
         scatter(V, dk_windows[0], staged_e0[0][:], 0, HALVES[0])
-        scatter(S, dk_windows[1], staged_f0[:, HALVES[0]], 0, HALVES[0])
-        staged_h0 = stage(S, dk0[3][:], "staged_h0", V2 + 2 * KB)
-        scatter(S, dk_windows[1], staged_f0[:, HALVES[1]], 0, HALVES[1])
+        scatter(S, dv_windows[2], staged_c1[:, HALVES[0]], 1, HALVES[0])
+        staged_f0 = stage(S, dk0[1][:], "staged_f0", V2)
+        scatter(S, dv_windows[2], staged_c1[:, HALVES[1]], 1, HALVES[1])
+        store(out_1, 2, dv_windows[2])
         ds1_planes = [new_planes("ds1_planes%d" % h, QM0 + 2 * KB * h, BF16, HALF) for h in range(2)]
-        ds1_grouped = new_grouped("ds1_grouped", QM0 + 4 * KB)
+        ds1_grouped = [new_grouped("ds1_grouped%d" % h, (QM0 + 4 * KB, QM0)[h], HALF) for h in range(2)]
         score_gradient(ds1_planes[0], dp1, pw1_planes[0], 1, HALVES[0])
         staged_e0.append(stage(V, dk0[0][:, HALVES[1]], "staged_e0_1", DOM1 + 4 * KB))
         score_gradient(ds1_planes[1], dp1, pw1_planes[1], 1, HALVES[1])
-        for h in range(2):
-            weave(G, ds1_grouped[:, h * 2 * W : (h + 1) * 2 * W], ds1_planes[h][:])
+        weave(G, ds1_grouped[0][:], ds1_planes[0][:])
         scatter(V, dk_windows[0], staged_e0[1][:], 0, HALVES[1])
-        scatter(S, dk_windows[3], staged_h0[:], 0)
+        scatter(S, dk_windows[1], staged_f0[:], 0)
+        weave(V, ds1_grouped[1][:], ds1_planes[1][:])
+        ds1 = new_operand(E5, "ds1", X + 24 * KB)
+        quantise(ds1, ds1_grouped[0][:], 0)
         qm1 = quantised(qm1_grouped, E4, "qm1", QM0 + 2 * KB)
-        ds1 = quantised(ds1_grouped, E5, "ds1", X + 24 * KB)
-        dk1 = [product("bank%d" % (2, 3, 4, 5)[j], qm1, j, ds1) for j in range(PACK)]
+        quantise(ds1, ds1_grouped[1][:], HALF)
+        dk1 = {j: product("bank%d" % (2, 3, 4, 5)[j], qm1, j, ds1) for j in (1, 2, 0, 3)}
         staged_g0 = stage(V, dk0[2][:], "staged_g0", DO1)
-        scatter(V, dk_windows[2], staged_g0[:, HALVES[0]], 0, HALVES[0])
-        staged_f1 = [stage(S, dk1[1][:, HALVES[h]], "staged_f1_%d" % h, V1 + KB + 4 * KB * h) for h in range(2)]
-        staged_e1 = stage(V, dk1[0][:], "staged_e1", V0)
-        scatter(S, dk_windows[1], staged_f1[0][:], 1, HALVES[0])
-        scatter(S, dk_windows[1], staged_f1[1][:], 1, HALVES[1])
-        staged_h1 = [stage(S, dk1[3][:, HALVES[h]], "staged_h1_%d" % h, V1 + KB * h + KB // 2) for h in range(2)]
+        scatter(V, dk_windows[2], staged_g0[:], 0)
+        staged_f1 = stage(S, dk1[1][:], "staged_f1", V1)
+        scatter(S, dk_windows[1], staged_f1[:, HALVES[0]], 1, HALVES[0])
+        staged_h0 = stage(S, dk0[3][:], "staged_h0", X + 24 * KB)
+        scatter(S, dk_windows[1], staged_f1[:, HALVES[1]], 1, HALVES[1])
         store(out_0, 1, dk_windows[1])
-        scatter(V, dk_windows[0], staged_e1[:], 1)
-        store(out_0, 0, dk_windows[0])
-        scatter(S, dk_windows[3], staged_h1[0][:], 1, HALVES[0])
-        scatter(V, dk_windows[2], staged_g0[:, HALVES[1]], 0, HALVES[1])
-        staged_g1 = stage(V, dk1[2][:], "staged_g1", V1 - KB)
-        scatter(S, dk_windows[3], staged_h1[1][:], 1, HALVES[1])
-        store(out_0, 3, dk_windows[3])
+        staged_g1 = stage(V, dk1[2][:], "staged_g1", V0)
+        staged_e1 = stage(V, dk1[0][:], "staged_e1", V0 + 2 * KB)
         scatter(V, dk_windows[2], staged_g1[:], 1)
         store(out_0, 2, dk_windows[2])
+        scatter(S, dk_windows[3], staged_h0[:, HALVES[0]], 0, HALVES[0])
+        staged_h1 = [stage(S, dk1[3][:, HALVES[0]], "staged_h1_0", V1)]
+        scatter(S, dk_windows[3], staged_h0[:, HALVES[1]], 0, HALVES[1])
+        staged_h1.append(stage(S, dk1[3][:, HALVES[1]], "staged_h1_1", V0))
+        scatter(V, dk_windows[0], staged_e1[:], 1)
+        store(out_0, 0, dk_windows[0])
+        for h in range(2):
+            scatter(S, dk_windows[3], staged_h1[h][:], 1, HALVES[h])
+        store(out_0, 3, dk_windows[3])

@@ -28,6 +28,7 @@ Q0A, Q0B, DOM0A, DOM0B = (64 * KB + 4 * KB * n for n in range(4))
 Q1, DOM1, DO0, QM0, DO1, QM1 = (80 * KB + 8 * KB * n for n in range(6))
 SCALES = 128 * KB
 X = 136 * KB
+Y = 166 * KB
 
 
 def tile_attend_gat_lse_kv_kernel(tc, qT, kT, vT, doT, lse, delta, rw, qm, dom, offs, out_0, out_1):
@@ -164,8 +165,8 @@ def tile_attend_gat_lse_kv_kernel(tc, qT, kT, vT, doT, lse, delta, rw, qm, dom, 
                         out=window[:].indirect(listed(b, piece)), in_=staged[:, c0 - slots.start : c0 - slots.start + HALF], func=ACT.Copy
                     )
 
-        def store(out, j, window):
-            nc.sync.dma_start(out[j * P : (j + 1) * P, :], window[:])
+        def store(out, j, window, queue=nc.sync):
+            queue.dma_start(out[j * P : (j + 1) * P, :], window[:])
 
         def weights(planes, banks, neg_lse):
             for t in range(PACK):
@@ -180,8 +181,8 @@ def tile_attend_gat_lse_kv_kernel(tc, qT, kT, vT, doT, lse, delta, rw, qm, dom, 
             for t in range(PACK):
                 nc.vector.tensor_scalar(gated[:, t, :], planes[:, t, :], rw_sb[:, b, t : t + 1], None, ALU.mult)
 
-        def score_gradient(planes, banks, pw, b, cols):
-            for t in range(PACK):
+        def score_gradient(planes, banks, pw, b, cols, ts=range(PACK)):
+            for t in ts:
                 nc.vector.scalar_tensor_tensor(planes[:, t, :], banks[t][:, cols], delta_sb[:, b, t : t + 1], pw[:, t, :], ALU.subtract, ALU.mult)
 
         V, S, G = nc.vector, nc.scalar, nc.gpsimd
@@ -212,7 +213,9 @@ def tile_attend_gat_lse_kv_kernel(tc, qT, kT, vT, doT, lse, delta, rw, qm, dom, 
         for j in range(PACK):
             gather_into_place(k0_grouped[:], j, k_planes[j], listed(0))
             gather_plane(k1_gathered[:, j, :], k_planes[j], listed(1))
-        dk_windows = [dv_windows[0], dv_windows[1], dv_windows[3], dv_windows[2]]
+        spare_window = work.tile([P, T], F32, name="spare_window", offset=K0, align_bytes=64)
+        nc.gpsimd.memset(spare_window[:], 0.0)
+        dk_windows = [spare_window, dv_windows[1], dv_windows[0], dv_windows[3]]
         q0_grouped = new_grouped("q0_grouped", X + 14 * KB)
         deal(S, q0_grouped[:], q0_raw[0][:])
         k0 = quantised(k0_grouped, E4, "k0", X + 18 * KB)
@@ -221,15 +224,15 @@ def tile_attend_gat_lse_kv_kernel(tc, qT, kT, vT, doT, lse, delta, rw, qm, dom, 
         weave(S, k1_grouped[:, 0 : 3 * W], k1_gathered[:, :, 0:384])
         neg_lse0 = negated("neg_lse0", X + 6 * KB, lse_sb[:, 0, :])
         neg_lse1 = negated("neg_lse1", X + 29 * KB, lse_sb[:, 1, :])
+        weave(V, k1_grouped[:, 3 * W : 4 * W], k1_gathered[:, :, 384:512])
         q0 = new_operand(E4, "q0", X + 20 * KB)
         for h in range(2):
             quantise(q0, q0_grouped[:, h * 2 * W : (h + 1) * 2 * W], h * HALF)
         dom0_grouped = new_grouped("dom0_grouped", X + 14 * KB)
-        weave(V, k1_grouped[:, 3 * W : 4 * W], k1_gathered[:, :, 384:512])
         weave(V, dom0_grouped[:, 0 : 2 * W], dom0_raw[0][:])
         k1 = quantised(k1_grouped, E4, "k1", Q0B)
         weave(V, dom0_grouped[:, 2 * W : 4 * W], dom0_raw[1][:])
-        pw0_planes = [new_planes("pw0_planes%d" % h, K0 + 4 * KB * h, F32, HALF) for h in range(2)]
+        pw0_planes = [new_planes("pw0_planes%d" % h, Y + 4 * KB * h, F32, HALF) for h in range(2)]
         for h in range(2):
             banks = [product("bank%d" % (4 * h + t), q0, t, k0, HALVES[h]) for t in range(PACK)]
             weights(pw0_planes[h], banks, neg_lse0)
@@ -238,135 +241,145 @@ def tile_attend_gat_lse_kv_kernel(tc, qT, kT, vT, doT, lse, delta, rw, qm, dom, 
         gate(pw0_planes[0], pw0_planes[0], 0)
         dom0 = quantised(dom0_grouped, E5, "dom0", X + 22 * KB)
         weave(V, pw0_grouped[0][:], pw0_planes[0][:])
-        q1_grouped = new_grouped("q1_grouped", X + 6 * KB)
-        deal(S, q1_grouped[:], q1_raw[:])
+        q1_grouped = [new_grouped("q1_grouped%d" % h, (X + 6 * KB, X + 14 * KB)[h], HALF) for h in range(2)]
+        deal_half(S, q1_grouped[0][:], q1_raw[:], 0)
         gate(pw0_planes[1], pw0_planes[1], 0)
         quantise(pw0, pw0_grouped[0][:], 0)
         b0 = [product("bank0", dom0, 1, pw0, HALVES[0])]
         a0 = [product("bank1", dom0, 0, pw0, HALVES[0])]
+        deal_half(V, q1_grouped[1][:], q1_raw[:], 1)
         weave(V, pw0_grouped[1][:], pw0_planes[1][:])
         staged_b0 = [stage(S, b0[0][:], "staged_b0_0", Q1)]
         staged_a0 = [stage(S, a0[0][:], "staged_a0_0", Q1 + KB)]
         q1 = new_operand(E4, "q1", X + 18 * KB)
-        quantise(q1, q1_grouped[:, 0 : 2 * W], 0)
+        quantise(q1, q1_grouped[0][:], 0)
         quantise(pw0, pw0_grouped[1][:], HALF)
-        quantise(q1, q1_grouped[:, 2 * W : 4 * W], HALF)
+        quantise(q1, q1_grouped[1][:], HALF)
         a0.append(product("bank2", dom0, 0, pw0, HALVES[1]))
         scores1 = [product("bank%d" % (4 + t), q1, t, k1) for t in range(PACK)]
         b0.append(product("bank3", dom0, 1, pw0, HALVES[1]))
         c0 = product("bank0", dom0, 2, pw0)
         d0 = product("bank1", dom0, 3, pw0)
         scatter(S, dv_windows[1], staged_b0[0][:], 0, HALVES[0])
-        dom1_grouped = new_grouped("dom1_grouped", X + 6 * KB)
+        dom1_grouped = new_grouped("dom1_grouped", X + 14 * KB)
         weave(G, dom1_grouped[:], dom1_raw[:])
         scatter(V, dv_windows[0], staged_a0[0][:], 0, HALVES[0])
         staged_a0.append(stage(V, a0[1][:], "staged_a0_1", X + 28 * KB))
-        scatter(V, dv_windows[0], staged_a0[1][:], 0, HALVES[1])
         p1 = new_planes("p1", K1, F32)
         weights(p1, scores1, neg_lse1)
+        scatter(V, dv_windows[0], staged_a0[1][:], 0, HALVES[1])
 
         dom1 = quantised(dom1_grouped, E5, "dom1", X + 20 * KB)
-        pw1_planes = [new_planes("pw1_planes%d" % h, (DOM1 + 4 * KB, X + 6 * KB)[h], F32, HALF) for h in range(2)]
+        do0_grouped = new_grouped("do0_grouped", DOM1)
+        deal(V, do0_grouped[:], do0_raw[:])
+        pw1_planes = [new_planes("pw1_planes%d" % h, (DOM1 + 4 * KB, DO0)[h], F32, HALF) for h in range(2)]
         gate(pw1_planes[0], p1[:, :, HALVES[0]], 1)
+        do0 = quantised(do0_grouped, E5, "do0", X + 18 * KB)
         gate(pw1_planes[1], p1[:, :, HALVES[1]], 1)
-        staged_c0 = stage(V, c0[:], "staged_c0", K1 + 4 * KB)
         pw1_grouped = new_grouped("pw1_grouped", K1)
         for h in range(2):
             weave(G, pw1_grouped[:, h * 2 * W : (h + 1) * 2 * W], pw1_planes[h][:])
-        scatter(V, dv_windows[2], staged_c0[:], 0)
-        v_gathered = [new_planes("v_gathered%d" % b, K2 + 4 * KB * b, BF16) for b in range(B)]
-        for j in range(PACK):
-            for b in range(B):
-                gather_plane(v_gathered[b][:, j, :], v_planes[j], listed(b))
+        v_gathered = [new_planes("v_gathered%d" % b, (K2, X + 14 * KB)[b], BF16) for b in range(B)]
+        for j in range(PACK - 1):
+            nc.vector.tensor_copy(v_gathered[1][:, j, :], v_planes[j][:].indirect(listed(1)))
+        gather_plane(v_gathered[0][:, 0, :], v_planes[0], listed(0))
+        staged_c0 = [stage(S, c0[:, HALVES[0]], "staged_c0_0", X + 29 * KB)]
+        gather_plane(v_gathered[0][:, 1, :], v_planes[1], listed(0))
+        scatter(S, dv_windows[2], staged_c0[0][:], 0, HALVES[0])
+        for j in range(2, PACK):
+            gather_plane(v_gathered[0][:, j, :], v_planes[j], listed(0))
+        gather_plane(v_gathered[1][:, 3, :], v_planes[3], listed(1))
         pw1 = quantised(pw1_grouped, E4, "pw1", X + 26 * KB)
-        dv1 = [product("bank%d" % (0, 4, 2, 5)[j], dom1, j, pw1) for j in range(PACK)]
-        do0_grouped = new_grouped("do0_grouped", K1)
-        deal(V, do0_grouped[:], do0_raw[:])
-        v0_grouped = new_grouped("v0_grouped", K3)
-        weave(V, v0_grouped[:], v_gathered[0][:])
-        do0 = quantised(do0_grouped, E5, "do0", X + 18 * KB)
+        dv1 = [product("bank2", dom1, 0, pw1)]
+        v0_grouped = [new_grouped("v0_grouped%d" % h, (K3, K1)[h], HALF) for h in range(2)]
+        v0 = new_operand(E4, "v0", Q0B)
+        for h in range(2):
+            weave(V, v0_grouped[h][:], v_gathered[0][:, :, HALVES[h]])
+        quantise(v0, v0_grouped[0][:], 0)
         staged_a1 = [stage(V, dv1[0][:, HALVES[0]], "staged_a1_0", K2)]
-        v0 = quantised(v0_grouped, E4, "v0", Q0B)
+        quantise(v0, v0_grouped[1][:], HALF)
         staged_b0.append(stage(S, b0[1][:], "staged_b0_1", V3))
+        staged_c0.append(stage(S, c0[:, HALVES[1]], "staged_c0_1", V3 + KB))
         staged_d0 = stage(S, d0[:], "staged_d0", V3 + 6 * KB)
-        dp0 = [product("bank%d" % (6, 7, 3, 1)[t], do0, t, v0) for t in range(PACK)]
-        qm0_grouped = new_grouped("qm0_grouped", K3)
+        dv1.extend(product("bank%d" % (2, 3, 0, 1)[j], dom1, j, pw1) for j in range(1, PACK))
+        dp0 = [product("bank%d" % (4 + t), do0, t, v0) for t in range(PACK)]
+        qm0_grouped = new_grouped("qm0_grouped", K1)
         weave(G, qm0_grouped[:], qm0_raw[:])
         scatter(V, dv_windows[0], staged_a1[0][:], 1, HALVES[0])
-        scatter(S, dv_windows[3], staged_d0[:, HALVES[0]], 0, HALVES[0])
         scatter(S, dv_windows[1], staged_b0[1][:], 0, HALVES[1])
+        staged_b1 = stage(S, dv1[1][:], "staged_b1", V2)
+        scatter(S, dv_windows[2], staged_c0[1][:], 0, HALVES[1])
+        scatter(S, dv_windows[3], staged_d0[:, HALVES[0]], 0, HALVES[0])
+        scatter(S, dv_windows[1], staged_b1[:, HALVES[0]], 1, HALVES[0])
         scatter(S, dv_windows[3], staged_d0[:, HALVES[1]], 0, HALVES[1])
-        staged_b1 = [stage(S, dv1[1][:, HALVES[0]], "staged_b1_0", V3 + 2 * KB)]
-        staged_d1 = [stage(S, dv1[3][:, HALVES[0]], "staged_d1_0", V3 + 4 * KB)]
+        staged_d1 = stage(S, dv1[3][:], "staged_d1", V2 + 2 * KB)
         ds0_planes = [new_planes("ds0_planes%d" % h, DOM0A + 2 * KB * h, BF16, HALF) for h in range(2)]
         ds0_grouped = [new_grouped("ds0_grouped%d" % h, (Q0A, DOM0A)[h], HALF) for h in range(2)]
         score_gradient(ds0_planes[0], dp0, pw0_planes[0], 0, HALVES[0])
-        staged_a1.append(stage(V, dv1[0][:, HALVES[1]], "staged_a1_1", K0))
-        score_gradient(ds0_planes[1], dp0, pw0_planes[1], 0, HALVES[1])
+        score_gradient(ds0_planes[1], dp0, pw0_planes[1], 0, HALVES[1], range(0, 2))
+        staged_a1.append(stage(V, dv1[0][:, HALVES[1]], "staged_a1_1", Y))
+        score_gradient(ds0_planes[1], dp0, pw0_planes[1], 0, HALVES[1], range(2, PACK))
         weave(G, ds0_grouped[0][:], ds0_planes[0][:])
         scatter(V, dv_windows[0], staged_a1[1][:], 1, HALVES[1])
         store(out_1, 0, dv_windows[0])
-        scatter(S, dv_windows[1], staged_b1[0][:], 1, HALVES[0])
-        staged_b1.append(stage(S, dv1[1][:, HALVES[1]], "staged_b1_1", K0))
-        scatter(S, dv_windows[3], staged_d1[0][:], 1, HALVES[0])
-        scatter(S, dv_windows[1], staged_b1[1][:], 1, HALVES[1])
-        store(out_1, 1, dv_windows[1])
+        scatter(S, dv_windows[1], staged_b1[:, HALVES[1]], 1, HALVES[1])
+        scatter(S, dv_windows[3], staged_d1[:, HALVES[0]], 1, HALVES[0])
+        store(out_1, 1, dv_windows[1], S)
         weave(V, ds0_grouped[1][:], ds0_planes[1][:])
         ds0 = new_operand(E5, "ds0", X + 22 * KB)
         quantise(ds0, ds0_grouped[0][:], 0)
+        qm0 = quantised(qm0_grouped, E4, "qm0", DOM0A + 2 * KB)
         do1_grouped = new_grouped("do1_grouped", Q0A)
         quantise(ds0, ds0_grouped[1][:], HALF)
         deal(V, do1_grouped[:], do1_raw[:])
-        qm0 = quantised(qm0_grouped, E4, "qm0", DOM0A + 2 * KB)
-        dk0 = [product("bank%d" % (0, 6, 7, 1)[j], qm0, j, ds0) for j in range(PACK)]
-        staged_d1.append(stage(S, dv1[3][:, HALVES[1]], "staged_d1_1", DOM0A))
-        staged_c1 = stage(S, dv1[2][:], "staged_c1", K3)
-        scatter(S, dv_windows[3], staged_d1[1][:], 1, HALVES[1])
-        store(out_1, 3, dv_windows[3])
-        v1_grouped = new_grouped("v1_grouped", DO1)
+        dk0 = {j: product("bank%d" % (2, 3, 1)[j], qm0, j, ds0) for j in range(3)}
+        v1_grouped = new_grouped("v1_grouped", K1)
         weave(V, v1_grouped[:], v_gathered[1][:])
         do1 = quantised(do1_grouped, E5, "do1", DO1 + 4 * KB)
-        staged_e0 = [stage(V, dk0[0][:, HALVES[0]], "staged_e0_0", K2 + 4 * KB)]
+        staged_c1 = [stage(V, dv1[2][:, HALVES[0]], "staged_c1_0", X + 14 * KB)]
         v1 = quantised(v1_grouped, E4, "v1", Q0B)
-        dp1 = [product("bank%d" % (2, 3, 4, 5)[t], do1, t, v1) for t in range(PACK)]
-        qm1_grouped = new_grouped("qm1_grouped", DO1)
+        dp1 = [product("bank%d" % (4 + t), do1, t, v1) for t in range(PACK)]
+        qm1_grouped = new_grouped("qm1_grouped", K1)
         weave(G, qm1_grouped[:], qm1_raw[:])
-        scatter(V, dk_windows[0], staged_e0[0][:], 0, HALVES[0])
-        scatter(S, dv_windows[2], staged_c1[:, HALVES[0]], 1, HALVES[0])
-        staged_f0 = stage(S, dk0[1][:], "staged_f0", V2)
-        scatter(S, dv_windows[2], staged_c1[:, HALVES[1]], 1, HALVES[1])
-        store(out_1, 2, dv_windows[2])
+        scatter(V, dv_windows[2], staged_c1[0][:], 1, HALVES[0])
+        staged_e0 = stage(S, dk0[0][:], "staged_e0", V3)
+        scatter(S, dv_windows[3], staged_d1[:, HALVES[1]], 1, HALVES[1])
+        staged_f0 = stage(S, dk0[1][:], "staged_f0", V3 + 2 * KB)
+        scatter(S, dk_windows[0], staged_e0[:, HALVES[0]], 0, HALVES[0])
+        store(out_1, 3, dv_windows[3], S)
+        scatter(S, dk_windows[1], staged_f0[:, HALVES[0]], 0, HALVES[0])
         ds1_planes = [new_planes("ds1_planes%d" % h, QM0 + 2 * KB * h, BF16, HALF) for h in range(2)]
-        ds1_grouped = [new_grouped("ds1_grouped%d" % h, (QM0 + 4 * KB, QM0)[h], HALF) for h in range(2)]
+        ds1_grouped = [new_grouped("ds1_grouped%d" % h, (DO1, QM0)[h], HALF) for h in range(2)]
         score_gradient(ds1_planes[0], dp1, pw1_planes[0], 1, HALVES[0])
-        staged_e0.append(stage(V, dk0[0][:, HALVES[1]], "staged_e0_1", DOM1 + 4 * KB))
-        score_gradient(ds1_planes[1], dp1, pw1_planes[1], 1, HALVES[1])
+        score_gradient(ds1_planes[1], dp1, pw1_planes[1], 1, HALVES[1], range(0, 2))
+        staged_c1.append(stage(V, dv1[2][:, HALVES[1]], "staged_c1_1", DOM1 + 4 * KB))
+        score_gradient(ds1_planes[1], dp1, pw1_planes[1], 1, HALVES[1], range(2, PACK))
+        dk0[3] = product("bank0", qm0, 3, ds0)
         weave(G, ds1_grouped[0][:], ds1_planes[0][:])
-        scatter(V, dk_windows[0], staged_e0[1][:], 0, HALVES[1])
-        scatter(S, dk_windows[1], staged_f0[:], 0)
+        scatter(V, dv_windows[2], staged_c1[1][:], 1, HALVES[1])
+        store(out_1, 2, dv_windows[2])
+        for j in range(2):
+            scatter(S, dk_windows[j], (staged_e0, staged_f0)[j][:, HALVES[1]], 0, HALVES[1])
         weave(V, ds1_grouped[1][:], ds1_planes[1][:])
         ds1 = new_operand(E5, "ds1", X + 24 * KB)
         quantise(ds1, ds1_grouped[0][:], 0)
         qm1 = quantised(qm1_grouped, E4, "qm1", QM0 + 2 * KB)
-        quantise(ds1, ds1_grouped[1][:], HALF)
-        dk1 = {j: product("bank%d" % (2, 3, 4, 5)[j], qm1, j, ds1) for j in (1, 2, 0, 3)}
         staged_g0 = stage(V, dk0[2][:], "staged_g0", DO1)
+        quantise(ds1, ds1_grouped[1][:], HALF)
+        dk1 = {j: product("bank%d" % (4 + j), qm1, j, ds1) for j in (2, 0, 3, 1)}
         scatter(V, dk_windows[2], staged_g0[:], 0)
-        staged_f1 = stage(S, dk1[1][:], "staged_f1", V1)
-        scatter(S, dk_windows[1], staged_f1[:, HALVES[0]], 1, HALVES[0])
-        staged_h0 = stage(S, dk0[3][:], "staged_h0", X + 24 * KB)
-        scatter(S, dk_windows[1], staged_f1[:, HALVES[1]], 1, HALVES[1])
-        store(out_0, 1, dk_windows[1])
+        staged_1 = [stage(S, dk1[j][:], "staged_dk1_%d" % j, V1 + 2 * KB * j) for j in range(2)]
+        staged_h = work.tile([P, B * N], F32, name="staged_h", offset=K1, align_bytes=64)
         staged_g1 = stage(V, dk1[2][:], "staged_g1", V0)
-        staged_e1 = stage(V, dk1[0][:], "staged_e1", V0 + 2 * KB)
+        copy_on(V, staged_h[:, 0:N], dk0[3][:])
         scatter(V, dk_windows[2], staged_g1[:], 1)
         store(out_0, 2, dk_windows[2])
-        scatter(S, dk_windows[3], staged_h0[:, HALVES[0]], 0, HALVES[0])
-        staged_h1 = [stage(S, dk1[3][:, HALVES[0]], "staged_h1_0", V1)]
-        scatter(S, dk_windows[3], staged_h0[:, HALVES[1]], 0, HALVES[1])
-        staged_h1.append(stage(S, dk1[3][:, HALVES[1]], "staged_h1_1", V0))
-        scatter(V, dk_windows[0], staged_e1[:], 1)
-        store(out_0, 0, dk_windows[0])
-        for h in range(2):
-            scatter(S, dk_windows[3], staged_h1[h][:], 1, HALVES[h])
+        scatter(S, dk_windows[0], staged_1[0][:, HALVES[0]], 1, HALVES[0])
+        copy_on(S, staged_h[:, N : 2 * N], dk1[3][:])
+        scatter(S, dk_windows[0], staged_1[0][:, HALVES[1]], 1, HALVES[1])
+        scatter(S, dk_windows[1], staged_1[1][:, HALVES[0]], 1, HALVES[0])
+        store(out_0, 0, dk_windows[0], S)
+        scatter(S, dk_windows[1], staged_1[1][:, HALVES[1]], 1, HALVES[1])
+        store(out_0, 1, dk_windows[1], S)
+        nc.vector.tensor_copy(dk_windows[3][:].indirect(offsets[:]), staged_h[:])
         store(out_0, 3, dk_windows[3])

@@ -27,8 +27,8 @@ K0, K1, K2, K3, V0, V1, V2, V3 = (8 * KB * n for n in range(8))
 Q0A, Q0B, DOM0A, DOM0B = (64 * KB + 4 * KB * n for n in range(4))
 Q1, DOM1, DO0, QM0, DO1, QM1 = (80 * KB + 8 * KB * n for n in range(6))
 SCALES = 128 * KB
-X = 136 * KB
-Y = 166 * KB
+X = 137 * KB
+Y = 167 * KB
 
 
 def tile_attend_gat_lse_kv_kernel(tc, qT, kT, vT, doT, lse, delta, rw, qm, dom, offs, out_0, out_1):
@@ -190,11 +190,10 @@ def tile_attend_gat_lse_kv_kernel(tc, qT, kT, vT, doT, lse, delta, rw, qm, dom, 
         k_planes = [load_plane(kT, 0, "k_plane0", K0)]
         nc.sync.dma_start(offsets[:], offs)
         k_planes.extend(load_plane(kT, j, "k_plane%d" % j, (K0, K1, K2, K3)[j]) for j in range(1, PACK))
-        q0_raw = [load_rows(qT[0], "q0_raw%d" % h, (Q0A, Q0B)[h], HALVES[h]) for h in range(2)]
+        q0_raw = load_rows(qT[0], "q0_raw", Q0A)
         lse_sb = load_per_row(lse, "lse_sb")
-        dom0_raw = [load_rows(dom[0], "dom0_raw0", DOM0A, HALVES[0])]
+        dom0_raw = load_rows(dom[0], "dom0_raw", DOM0A)
         rw_sb = load_per_row(rw, "rw_sb")
-        dom0_raw.append(load_rows(dom[0], "dom0_raw1", DOM0B, HALVES[1]))
         q1_raw = load_rows(qT[1], "q1_raw", Q1)
         dom1_raw = load_rows(dom[1], "dom1_raw", DOM1)
         do0_raw = load_rows(doT[0], "do0_raw", DO0)
@@ -216,52 +215,53 @@ def tile_attend_gat_lse_kv_kernel(tc, qT, kT, vT, doT, lse, delta, rw, qm, dom, 
         spare_window = work.tile([P, T], F32, name="spare_window", offset=K0, align_bytes=64)
         nc.gpsimd.memset(spare_window[:], 0.0)
         dk_windows = [spare_window, dv_windows[1], dv_windows[0], dv_windows[3]]
-        q0_grouped = new_grouped("q0_grouped", X + 14 * KB)
-        deal(S, q0_grouped[:], q0_raw[0][:])
-        k0 = quantised(k0_grouped, E4, "k0", X + 18 * KB)
-        deal(V, q0_grouped[:], q0_raw[1][:], P // 2)
-        k1_grouped = new_grouped("k1_grouped", Q0A)
-        weave(S, k1_grouped[:, 0 : 3 * W], k1_gathered[:, :, 0:384])
+        k1_grouped = [new_grouped("k1_grouped%d" % h, (X + 10 * KB, Q0A)[h], HALF) for h in range(2)]
+        weave(S, k1_grouped[0][:, 0:W], k1_gathered[:, :, 0:128])
+        q0_grouped = [new_grouped("q0_grouped%d" % h, X + 14 * KB + 2 * KB * h, HALF) for h in range(2)]
+        k0 = [new_operand(E4, "k0_%d" % h, (X + 18 * KB, Q0A + 2 * KB)[h]) for h in range(2)]
+        quantise(k0[0], k0_grouped[:, 0 : 2 * W])
+        for h in range(2):
+            deal_half((V, S)[h], q0_grouped[h][:], q0_raw[:], h)
         neg_lse0 = negated("neg_lse0", X + 6 * KB, lse_sb[:, 0, :])
         neg_lse1 = negated("neg_lse1", X + 29 * KB, lse_sb[:, 1, :])
-        weave(V, k1_grouped[:, 3 * W : 4 * W], k1_gathered[:, :, 384:512])
+        weave(V, k1_grouped[0][:, W : 2 * W], k1_gathered[:, :, 128:256])
         q0 = new_operand(E4, "q0", X + 20 * KB)
         for h in range(2):
-            quantise(q0, q0_grouped[:, h * 2 * W : (h + 1) * 2 * W], h * HALF)
+            quantise(q0, q0_grouped[h][:], h * HALF)
+        quantise(k0[1], k0_grouped[:, 2 * W : 4 * W])
+        k1 = new_operand(E4, "k1", Q0B)
+        quantise(k1, k1_grouped[0][:], 0)
+        weave(S, k1_grouped[1][:], k1_gathered[:, :, HALVES[1]])
         dom0_grouped = new_grouped("dom0_grouped", X + 14 * KB)
-        weave(V, dom0_grouped[:, 0 : 2 * W], dom0_raw[0][:])
-        k1 = quantised(k1_grouped, E4, "k1", Q0B)
-        weave(V, dom0_grouped[:, 2 * W : 4 * W], dom0_raw[1][:])
+        weave(V, dom0_grouped[:], dom0_raw[:])
+        quantise(k1, k1_grouped[1][:], HALF)
         pw0_planes = [new_planes("pw0_planes%d" % h, Y + 4 * KB * h, F32, HALF) for h in range(2)]
         for h in range(2):
-            banks = [product("bank%d" % (4 * h + t), q0, t, k0, HALVES[h]) for t in range(PACK)]
+            banks = [product("bank%d" % (4 * h + t), q0, t, k0[h], HALVES[0]) for t in range(PACK)]
             weights(pw0_planes[h], banks, neg_lse0)
         pw0 = new_operand(E4, "pw0", X + 24 * KB)
-        pw0_grouped = [new_grouped("pw0_grouped%d" % h, Q0A + 2 * KB * h, HALF) for h in range(2)]
+        pw0_grouped = [new_grouped("pw0_grouped%d" % h, X + 10 * KB + 2 * KB * h, HALF) for h in range(2)]
         gate(pw0_planes[0], pw0_planes[0], 0)
         dom0 = quantised(dom0_grouped, E5, "dom0", X + 22 * KB)
         weave(V, pw0_grouped[0][:], pw0_planes[0][:])
-        q1_grouped = [new_grouped("q1_grouped%d" % h, (X + 6 * KB, X + 14 * KB)[h], HALF) for h in range(2)]
-        deal_half(S, q1_grouped[0][:], q1_raw[:], 0)
+        q1_grouped = new_grouped("q1_grouped", X + 6 * KB)
+        deal(S, q1_grouped[:], q1_raw[:])
         gate(pw0_planes[1], pw0_planes[1], 0)
         quantise(pw0, pw0_grouped[0][:], 0)
         b0 = [product("bank0", dom0, 1, pw0, HALVES[0])]
         a0 = [product("bank1", dom0, 0, pw0, HALVES[0])]
-        deal_half(V, q1_grouped[1][:], q1_raw[:], 1)
         weave(V, pw0_grouped[1][:], pw0_planes[1][:])
-        staged_b0 = [stage(S, b0[0][:], "staged_b0_0", Q1)]
         staged_a0 = [stage(S, a0[0][:], "staged_a0_0", Q1 + KB)]
-        q1 = new_operand(E4, "q1", X + 18 * KB)
-        quantise(q1, q1_grouped[0][:], 0)
+        staged_b0 = [stage(S, b0[0][:], "staged_b0_0", Q1)]
         quantise(pw0, pw0_grouped[1][:], HALF)
-        quantise(q1, q1_grouped[1][:], HALF)
+        q1 = quantised(q1_grouped, E4, "q1", X + 18 * KB)
         a0.append(product("bank2", dom0, 0, pw0, HALVES[1]))
         scores1 = [product("bank%d" % (4 + t), q1, t, k1) for t in range(PACK)]
         b0.append(product("bank3", dom0, 1, pw0, HALVES[1]))
         c0 = product("bank0", dom0, 2, pw0)
         d0 = product("bank1", dom0, 3, pw0)
         scatter(S, dv_windows[1], staged_b0[0][:], 0, HALVES[0])
-        dom1_grouped = new_grouped("dom1_grouped", X + 14 * KB)
+        dom1_grouped = new_grouped("dom1_grouped", X + 6 * KB)
         weave(G, dom1_grouped[:], dom1_raw[:])
         scatter(V, dv_windows[0], staged_a0[0][:], 0, HALVES[0])
         staged_a0.append(stage(V, a0[1][:], "staged_a0_1", X + 28 * KB))
@@ -279,7 +279,7 @@ def tile_attend_gat_lse_kv_kernel(tc, qT, kT, vT, doT, lse, delta, rw, qm, dom, 
         pw1_grouped = new_grouped("pw1_grouped", K1)
         for h in range(2):
             weave(G, pw1_grouped[:, h * 2 * W : (h + 1) * 2 * W], pw1_planes[h][:])
-        v_gathered = [new_planes("v_gathered%d" % b, (K2, X + 14 * KB)[b], BF16) for b in range(B)]
+        v_gathered = [new_planes("v_gathered%d" % b, (K2, X + 6 * KB)[b], BF16) for b in range(B)]
         for j in range(PACK - 1):
             nc.vector.tensor_copy(v_gathered[1][:, j, :], v_planes[j][:].indirect(listed(1)))
         gather_plane(v_gathered[0][:, 0, :], v_planes[0], listed(0))
@@ -336,7 +336,7 @@ def tile_attend_gat_lse_kv_kernel(tc, qT, kT, vT, doT, lse, delta, rw, qm, dom, 
         v1_grouped = new_grouped("v1_grouped", K1)
         weave(V, v1_grouped[:], v_gathered[1][:])
         do1 = quantised(do1_grouped, E5, "do1", DO1 + 4 * KB)
-        staged_c1 = [stage(V, dv1[2][:, HALVES[0]], "staged_c1_0", X + 14 * KB)]
+        staged_c1 = [stage(V, dv1[2][:, HALVES[0]], "staged_c1_0", X + 6 * KB)]
         v1 = quantised(v1_grouped, E4, "v1", Q0B)
         dp1 = [product("bank%d" % (4 + t), do1, t, v1) for t in range(PACK)]
         qm1_grouped = new_grouped("qm1_grouped", K1)
@@ -368,10 +368,10 @@ def tile_attend_gat_lse_kv_kernel(tc, qT, kT, vT, doT, lse, delta, rw, qm, dom, 
         quantise(ds1, ds1_grouped[1][:], HALF)
         dk1 = {j: product("bank%d" % (4 + j), qm1, j, ds1) for j in (2, 0, 3, 1)}
         scatter(V, dk_windows[2], staged_g0[:], 0)
-        staged_1 = [stage(S, dk1[j][:], "staged_dk1_%d" % j, V1 + 2 * KB * j) for j in range(2)]
         staged_h = work.tile([P, B * N], F32, name="staged_h", offset=K1, align_bytes=64)
+        copy_on(S, staged_h[:, 0:N], dk0[3][:])
+        staged_1 = [stage(S, dk1[j][:], "staged_dk1_%d" % j, V1 + 2 * KB * j) for j in range(2)]
         staged_g1 = stage(V, dk1[2][:], "staged_g1", V0)
-        copy_on(V, staged_h[:, 0:N], dk0[3][:])
         scatter(V, dk_windows[2], staged_g1[:], 1)
         store(out_0, 2, dk_windows[2])
         scatter(S, dk_windows[0], staged_1[0][:, HALVES[0]], 1, HALVES[0])

@@ -19,6 +19,7 @@ P = 128
 PACK = 4
 W = 512
 HALF = W // 2
+QUARTER = W // 4
 LIST_COLS = N // 16
 HALVES = [slice(0, HALF), slice(HALF, W)]
 WHOLE = slice(0, W)
@@ -177,8 +178,8 @@ def tile_attend_gat_lse_kv_kernel(tc, qT, kT, vT, doT, lse, delta, rw, qm, dom, 
             nc.scalar.mul(neg[:], column, -1.0)
             return neg
 
-        def gate(gated, planes, b):
-            for t in range(PACK):
+        def gate(gated, planes, b, ts=range(PACK)):
+            for t in ts:
                 nc.vector.tensor_scalar(gated[:, t, :], planes[:, t, :], rw_sb[:, b, t : t + 1], None, ALU.mult)
 
         def score_gradient(planes, banks, pw, b, cols, ts=range(PACK)):
@@ -272,13 +273,18 @@ def tile_attend_gat_lse_kv_kernel(tc, qT, kT, vT, doT, lse, delta, rw, qm, dom, 
         dom1 = quantised(dom1_grouped, E5, "dom1", X + 20 * KB)
         do0_grouped = new_grouped("do0_grouped", DOM1)
         deal(V, do0_grouped[:], do0_raw[:])
-        pw1_planes = [new_planes("pw1_planes%d" % h, (DOM1 + 4 * KB, DO0)[h], F32, HALF) for h in range(2)]
-        gate(pw1_planes[0], p1[:, :, HALVES[0]], 1)
-        do0 = quantised(do0_grouped, E5, "do0", X + 18 * KB)
+        pw1_planes = [new_planes("pw1_planes%d" % h, (DO0, DOM1 + 4 * KB)[h], F32, HALF) for h in range(2)]
         gate(pw1_planes[1], p1[:, :, HALVES[1]], 1)
-        pw1_grouped = new_grouped("pw1_grouped", K1)
-        for h in range(2):
-            weave(G, pw1_grouped[:, h * 2 * W : (h + 1) * 2 * W], pw1_planes[h][:])
+        do0 = quantised(do0_grouped, E5, "do0", X + 18 * KB)
+        pw1_last = new_grouped("pw1_last", Q1 + 2 * KB, QUARTER)
+        weave(V, pw1_last[:], pw1_planes[1][:, :, QUARTER:HALF])
+        gate(pw1_planes[0], p1[:, :, HALVES[0]], 1, range(0, 2))
+        pw1 = new_operand(E4, "pw1", X + 26 * KB)
+        quantise(pw1, pw1_last[:], W - QUARTER)
+        gate(pw1_planes[0], p1[:, :, HALVES[0]], 1, range(2, PACK))
+        pw1_grouped = new_grouped("pw1_grouped", K1, W - QUARTER)
+        weave(G, pw1_grouped[:, 0 : 2 * W], pw1_planes[0][:])
+        weave(G, pw1_grouped[:, 2 * W : 3 * W], pw1_planes[1][:, :, 0:QUARTER])
         v_gathered = [new_planes("v_gathered%d" % b, (K2, X + 6 * KB)[b], BF16) for b in range(B)]
         for j in range(PACK - 1):
             nc.vector.tensor_copy(v_gathered[1][:, j, :], v_planes[j][:].indirect(listed(1)))
@@ -289,7 +295,8 @@ def tile_attend_gat_lse_kv_kernel(tc, qT, kT, vT, doT, lse, delta, rw, qm, dom, 
         for j in range(2, PACK):
             gather_plane(v_gathered[0][:, j, :], v_planes[j], listed(0))
         gather_plane(v_gathered[1][:, 3, :], v_planes[3], listed(1))
-        pw1 = quantised(pw1_grouped, E4, "pw1", X + 26 * KB)
+        quantise(pw1, pw1_grouped[:, 0 : 2 * W], 0)
+        quantise(pw1, pw1_grouped[:, 2 * W : 3 * W], HALF)
         dv1 = [product("bank2", dom1, 0, pw1)]
         v0_grouped = [new_grouped("v0_grouped%d" % h, (K3, K1)[h], HALF) for h in range(2)]
         v0 = new_operand(E4, "v0", Q0B)
@@ -352,7 +359,7 @@ def tile_attend_gat_lse_kv_kernel(tc, qT, kT, vT, doT, lse, delta, rw, qm, dom, 
         ds1_grouped = [new_grouped("ds1_grouped%d" % h, (DO1, QM0)[h], HALF) for h in range(2)]
         score_gradient(ds1_planes[0], dp1, pw1_planes[0], 1, HALVES[0])
         score_gradient(ds1_planes[1], dp1, pw1_planes[1], 1, HALVES[1], range(0, 2))
-        staged_c1.append(stage(V, dv1[2][:, HALVES[1]], "staged_c1_1", DOM1 + 4 * KB))
+        staged_c1.append(stage(V, dv1[2][:, HALVES[1]], "staged_c1_1", DO0))
         score_gradient(ds1_planes[1], dp1, pw1_planes[1], 1, HALVES[1], range(2, PACK))
         dk0[3] = product("bank0", qm0, 3, ds0)
         weave(G, ds1_grouped[0][:], ds1_planes[0][:])
@@ -370,8 +377,8 @@ def tile_attend_gat_lse_kv_kernel(tc, qT, kT, vT, doT, lse, delta, rw, qm, dom, 
         scatter(V, dk_windows[2], staged_g0[:], 0)
         staged_h = work.tile([P, B * N], F32, name="staged_h", offset=K1, align_bytes=64)
         copy_on(S, staged_h[:, 0:N], dk0[3][:])
+        staged_g1 = stage(S, dk1[2][:], "staged_g1", V0)
         staged_1 = [stage(S, dk1[j][:], "staged_dk1_%d" % j, V1 + 2 * KB * j) for j in range(2)]
-        staged_g1 = stage(V, dk1[2][:], "staged_g1", V0)
         scatter(V, dk_windows[2], staged_g1[:], 1)
         store(out_0, 2, dk_windows[2])
         scatter(S, dk_windows[0], staged_1[0][:, HALVES[0]], 1, HALVES[0])

@@ -25,11 +25,10 @@ HALVES = [slice(0, HALF), slice(HALF, W)]
 WHOLE = slice(0, W)
 KB = 1024
 K0, K1, K2, K3, V0, V1, V2, V3 = (8 * KB * n for n in range(8))
-Q0A, Q0B, DOM0A, DOM0B = (64 * KB + 4 * KB * n for n in range(4))
-Q1, DOM1, DO0, QM0, DO1, QM1 = (80 * KB + 8 * KB * n for n in range(6))
+Q0, DOM0, Q1, DOM1, DO0, QM0, DO1, QM1 = (64 * KB + 8 * KB * n for n in range(8))
 SCALES = 128 * KB
-X = 137 * KB
-Y = 167 * KB
+CODES = 137 * KB
+X = 171 * KB
 
 
 def tile_attend_gat_lse_kv_kernel(tc, qT, kT, vT, doT, lse, delta, rw, qm, dom, offs, out_0, out_1):
@@ -67,9 +66,9 @@ def tile_attend_gat_lse_kv_kernel(tc, qT, kT, vT, doT, lse, delta, rw, qm, dom, 
 
         operands = []
 
-        def new_operand(fmt, name, at):
-            codes = work.tile([P, W], U32, name=name + "_codes", offset=at, align_bytes=64)
-            scales = work.tile([P, W], U8, name=name + "_scales", offset=SCALES + W * len(operands), align_bytes=64)
+        def new_operand(fmt, name, scales_at=None):
+            codes = work.tile([P, W], U32, name=name + "_codes", offset=CODES + 2 * KB * len(operands), align_bytes=64)
+            scales = work.tile([P, W], U8, name=name + "_scales", offset=scales_at or SCALES + W * len(operands), align_bytes=64)
             operands.append(name)
             return codes, scales, fmt
 
@@ -78,8 +77,8 @@ def tile_attend_gat_lse_kv_kernel(tc, qT, kT, vT, doT, lse, delta, rw, qm, dom, 
             c1 = c0 + grouped.shape[1] // PACK
             nc.vector.quantize_mx(out=codes[:, c0:c1].bitcast(fmt), scales=scales[:, c0:c1], in_=grouped)
 
-        def quantised(grouped, fmt, name, at):
-            operand = new_operand(fmt, name, at)
+        def quantised(grouped, fmt, name, scales_at=None):
+            operand = new_operand(fmt, name, scales_at)
             quantise(operand, grouped[:])
             return operand
 
@@ -91,34 +90,20 @@ def tile_attend_gat_lse_kv_kernel(tc, qT, kT, vT, doT, lse, delta, rw, qm, dom, 
             else:
                 nc.gpsimd.tensor_scalar(out, in_, 1.0, 0.0, ALU.mult, ALU.add)
 
-        def deal(engine, grouped, rows, s0=0):
-            s1 = s0 + rows.shape[2] // PACK
+        def deal(engine, grouped, rows, ts=range(PACK)):
+            n = len(ts)
             if engine is nc.gpsimd:
-                for t0 in range(0, PACK, 2):
+                for t0 in range(0, n, 2):
                     copy_on(
                         engine,
-                        grouped.rearrange("p (t s j) -> p t s j", t=PACK, j=PACK)[:, t0 : t0 + 2, s0:s1, :],
-                        rows.rearrange("p j (s t) -> p t s j", t=PACK)[:, t0 : t0 + 2, :, :],
+                        grouped.rearrange("p (t s j) -> p t s j", t=n, j=PACK)[:, t0 : t0 + 2, :, :],
+                        rows.rearrange("p j (s t) -> p t s j", t=PACK)[:, ts[t0] : ts[t0] + 2, :, :],
                     )
             else:
                 copy_on(
                     engine,
-                    grouped.rearrange("p (t s j) -> p s j t", t=PACK, j=PACK)[:, s0:s1, :, :],
-                    rows.rearrange("p j (s t) -> p s j t", t=PACK),
-                )
-
-        def deal_half(engine, grouped, rows, h):
-            if engine is nc.gpsimd:
-                copy_on(
-                    engine,
-                    grouped.rearrange("p (t s j) -> p t s j", t=2, j=PACK),
-                    rows.rearrange("p j (s t) -> p t s j", t=PACK)[:, 2 * h : 2 * h + 2, :, :],
-                )
-            else:
-                copy_on(
-                    engine,
-                    grouped.rearrange("p (t s j) -> p s j t", t=2, j=PACK),
-                    rows.rearrange("p j (s t) -> p s j t", t=PACK)[:, :, :, 2 * h : 2 * h + 2],
+                    grouped.rearrange("p (t s j) -> p s j t", t=n, j=PACK),
+                    rows.rearrange("p j (s t) -> p s j t", t=PACK)[:, :, :, ts[0] : ts[0] + n],
                 )
 
         def weave(engine, grouped, planes):
@@ -131,8 +116,11 @@ def tile_attend_gat_lse_kv_kernel(tc, qT, kT, vT, doT, lse, delta, rw, qm, dom, 
                     planes.rearrange("p j (c i) -> p c j i", i=4),
                 )
 
-        def gather_plane(out, plane, slots):
-            nc.scalar.activation(out=out, in_=plane[:].indirect(slots), func=ACT.Copy)
+        def gather_plane(engine, out, plane, slots):
+            if engine is nc.vector:
+                nc.vector.tensor_copy(out, plane[:].indirect(slots))
+            else:
+                nc.scalar.activation(out=out, in_=plane[:].indirect(slots), func=ACT.Copy)
 
         def gather_into_place(grouped, j, plane, slots):
             nc.vector.tensor_copy(grouped.rearrange("p (n j) -> p n j", j=PACK)[:, :, j], plane[:].indirect(slots))
@@ -191,14 +179,14 @@ def tile_attend_gat_lse_kv_kernel(tc, qT, kT, vT, doT, lse, delta, rw, qm, dom, 
         k_planes = [load_plane(kT, 0, "k_plane0", K0)]
         nc.sync.dma_start(offsets[:], offs)
         k_planes.extend(load_plane(kT, j, "k_plane%d" % j, (K0, K1, K2, K3)[j]) for j in range(1, PACK))
-        q0_raw = load_rows(qT[0], "q0_raw", Q0A)
+        q0_raw = load_rows(qT[0], "q0_raw", Q0)
         lse_sb = load_per_row(lse, "lse_sb")
-        dom0_raw = load_rows(dom[0], "dom0_raw", DOM0A)
+        dom0_raw = load_rows(dom[0], "dom0_raw", DOM0)
         rw_sb = load_per_row(rw, "rw_sb")
         q1_raw = load_rows(qT[1], "q1_raw", Q1)
         dom1_raw = load_rows(dom[1], "dom1_raw", DOM1)
-        do0_raw = load_rows(doT[0], "do0_raw", DO0)
         v_planes = [load_plane(vT, j, "v_plane%d" % j, (V0, V1, V2, V3)[j]) for j in range(PACK)]
+        do0_raw = load_rows(doT[0], "do0_raw", DO0)
         delta_sb = load_per_row(delta, "delta_sb")
         qm0_raw = load_rows(qm[0], "qm0_raw", QM0)
         do1_raw = load_rows(doT[1], "do1_raw", DO1)
@@ -208,185 +196,163 @@ def tile_attend_gat_lse_kv_kernel(tc, qT, kT, vT, doT, lse, delta, rw, qm, dom, 
         for window in dv_windows:
             nc.vector.memset(window[:].bitcast(U32), 0)
 
-        k1_gathered = new_planes("k1_gathered", X + 2 * KB, BF16)
-        k0_grouped = new_grouped("k0_grouped", X + 6 * KB)
+        k0_grouped = new_grouped("k0_grouped", X)
+        k1_gathered = new_planes("k1_gathered", X + 4 * KB, BF16)
+        spare = []
         for j in range(PACK):
             gather_into_place(k0_grouped[:], j, k_planes[j], listed(0))
-            gather_plane(k1_gathered[:, j, :], k_planes[j], listed(1))
-        spare_window = work.tile([P, T], F32, name="spare_window", offset=K0, align_bytes=64)
-        nc.gpsimd.memset(spare_window[:], 0.0)
-        dk_windows = [spare_window, dv_windows[1], dv_windows[0], dv_windows[3]]
-        k1_grouped = [new_grouped("k1_grouped%d" % h, (X + 10 * KB, Q0A)[h], HALF) for h in range(2)]
-        weave(S, k1_grouped[0][:, 0:W], k1_gathered[:, :, 0:128])
-        q0_grouped = [new_grouped("q0_grouped%d" % h, X + 14 * KB + 2 * KB * h, HALF) for h in range(2)]
-        k0 = [new_operand(E4, "k0_%d" % h, (X + 18 * KB, Q0A + 2 * KB)[h]) for h in range(2)]
+            gather_plane(S, k1_gathered[:, j, :], k_planes[j], listed(1))
+            if j < 2:
+                spare.append(work.tile([P, T], F32, name="spare%d" % j, offset=(K0, K1)[j], align_bytes=64))
+                nc.gpsimd.memset(spare[j][:], 0.0)
+        dk_windows = [spare[0], spare[1], dv_windows[1], dv_windows[0]]
+        k1_parts = [slice(0, QUARTER), slice(QUARTER, HALF), HALVES[1]]
+        k1_grouped = [new_grouped("k1_grouped%d" % n, (X + 8 * KB, Q0 + 2 * KB, Q0)[n], c.stop - c.start) for n, c in enumerate(k1_parts)]
+        weave(S, k1_grouped[0][:], k1_gathered[:, :, k1_parts[0]])
+        q0_grouped = [new_grouped("q0_grouped%d" % h, X + 12 * KB + 2 * KB * h, HALF) for h in range(2)]
+        k0 = [new_operand(E4, "k0_%d" % h) for h in range(2)]
         quantise(k0[0], k0_grouped[:, 0 : 2 * W])
         for h in range(2):
-            deal_half((V, S)[h], q0_grouped[h][:], q0_raw[:], h)
-        neg_lse0 = negated("neg_lse0", X + 6 * KB, lse_sb[:, 0, :])
-        neg_lse1 = negated("neg_lse1", X + 29 * KB, lse_sb[:, 1, :])
-        weave(V, k1_grouped[0][:, W : 2 * W], k1_gathered[:, :, 128:256])
-        q0 = new_operand(E4, "q0", X + 20 * KB)
+            deal((V, S)[h], q0_grouped[h][:], q0_raw[:], range(2 * h, 2 * h + 2))
+        quantise(k0[1], k0_grouped[:, 2 * W : 4 * W])
+        neg_lse0 = negated("neg_lse0", X + 2 * KB, lse_sb[:, 0, :])
+        neg_lse1 = negated("neg_lse1", X + 33 * KB, lse_sb[:, 1, :])
+        weave(S, k1_grouped[1][:], k1_gathered[:, :, k1_parts[1]])
+        q0 = new_operand(E4, "q0")
         for h in range(2):
             quantise(q0, q0_grouped[h][:], h * HALF)
-        quantise(k0[1], k0_grouped[:, 2 * W : 4 * W])
-        k1 = new_operand(E4, "k1", Q0B)
-        quantise(k1, k1_grouped[0][:], 0)
-        weave(S, k1_grouped[1][:], k1_gathered[:, :, HALVES[1]])
-        dom0_grouped = new_grouped("dom0_grouped", X + 14 * KB)
+        weave(V, k1_grouped[2][:], k1_gathered[:, :, k1_parts[2]])
+        dom0_grouped = new_grouped("dom0_grouped", X + 16 * KB)
         weave(V, dom0_grouped[:], dom0_raw[:])
-        quantise(k1, k1_grouped[1][:], HALF)
-        pw0_planes = [new_planes("pw0_planes%d" % h, Y + 4 * KB * h, F32, HALF) for h in range(2)]
+        pw0_planes = [new_planes("pw0_planes%d" % h, X + 20 * KB + 4 * KB * h, F32, HALF) for h in range(2)]
         for h in range(2):
             banks = [product("bank%d" % (4 * h + t), q0, t, k0[h], HALVES[0]) for t in range(PACK)]
             weights(pw0_planes[h], banks, neg_lse0)
-        pw0 = new_operand(E4, "pw0", X + 24 * KB)
-        pw0_grouped = [new_grouped("pw0_grouped%d" % h, X + 10 * KB + 2 * KB * h, HALF) for h in range(2)]
+        pw0 = new_operand(E4, "pw0")
+        pw0_grouped = [new_grouped("pw0_grouped%d" % h, X + 28 * KB + 2 * KB * h, HALF) for h in range(2)]
+        k1 = new_operand(E4, "k1", X + 28 * KB)
         gate(pw0_planes[0], pw0_planes[0], 0)
-        dom0 = quantised(dom0_grouped, E5, "dom0", X + 22 * KB)
+        dom0 = quantised(dom0_grouped, E5, "dom0")
         weave(V, pw0_grouped[0][:], pw0_planes[0][:])
-        q1_grouped = new_grouped("q1_grouped", X + 6 * KB)
-        deal(S, q1_grouped[:], q1_raw[:])
         gate(pw0_planes[1], pw0_planes[1], 0)
         quantise(pw0, pw0_grouped[0][:], 0)
-        b0 = [product("bank0", dom0, 1, pw0, HALVES[0])]
-        a0 = [product("bank1", dom0, 0, pw0, HALVES[0])]
         weave(V, pw0_grouped[1][:], pw0_planes[1][:])
-        staged_a0 = [stage(S, a0[0][:], "staged_a0_0", Q1 + KB)]
-        staged_b0 = [stage(S, b0[0][:], "staged_b0_0", Q1)]
+        quantise(k1, k1_grouped[2][:], HALF)
         quantise(pw0, pw0_grouped[1][:], HALF)
-        q1 = quantised(q1_grouped, E4, "q1", X + 18 * KB)
+        for n in range(2):
+            quantise(k1, k1_grouped[n][:], n * QUARTER)
+        q1_grouped = new_grouped("q1_grouped", X + 2 * KB)
+        deal(S, q1_grouped[:], q1_raw[:])
+        q1 = quantised(q1_grouped, E4, "q1", X + 30 * KB)
+        a0 = [product("bank0", dom0, 0, pw0, HALVES[0])]
+        a1 = [product("bank1", dom0, 1, pw0, HALVES[0])]
         a0.append(product("bank2", dom0, 0, pw0, HALVES[1]))
         scores1 = [product("bank%d" % (4 + t), q1, t, k1) for t in range(PACK)]
-        b0.append(product("bank3", dom0, 1, pw0, HALVES[1]))
-        c0 = product("bank0", dom0, 2, pw0)
-        d0 = product("bank1", dom0, 3, pw0)
-        scatter(S, dv_windows[1], staged_b0[0][:], 0, HALVES[0])
-        dom1_grouped = new_grouped("dom1_grouped", X + 6 * KB)
+        a1.append(product("bank5", dom0, 1, pw0, HALVES[1]))
+        a2 = product("bank6", dom0, 2, pw0)
+        a3 = product("bank7", dom0, 3, pw0)
+        staged_a0 = [stage(S, a0[0][:], "staged_a0_0", Q1)]
+        staged_a1 = [stage(S, a1[0][:], "staged_a1_0", Q1 + KB)]
+
+        dom1_grouped = new_grouped("dom1_grouped", X + 5 * KB)
         weave(G, dom1_grouped[:], dom1_raw[:])
         scatter(V, dv_windows[0], staged_a0[0][:], 0, HALVES[0])
-        staged_a0.append(stage(V, a0[1][:], "staged_a0_1", X + 28 * KB))
-        p1 = new_planes("p1", K1, F32)
-        weights(p1, scores1, neg_lse1)
+        staged_a0.append(stage(V, a0[1][:], "staged_a0_1", X + 4 * KB))
         scatter(V, dv_windows[0], staged_a0[1][:], 0, HALVES[1])
-
-        dom1 = quantised(dom1_grouped, E5, "dom1", X + 20 * KB)
-        do0_grouped = new_grouped("do0_grouped", DOM1)
-        deal(V, do0_grouped[:], do0_raw[:])
-        pw1_planes = [new_planes("pw1_planes%d" % h, (DO0, DOM1 + 4 * KB)[h], F32, HALF) for h in range(2)]
-        gate(pw1_planes[1], p1[:, :, HALVES[1]], 1)
-        do0 = quantised(do0_grouped, E5, "do0", X + 18 * KB)
-        pw1_last = new_grouped("pw1_last", Q1 + 2 * KB, QUARTER)
-        weave(V, pw1_last[:], pw1_planes[1][:, :, QUARTER:HALF])
-        gate(pw1_planes[0], p1[:, :, HALVES[0]], 1, range(0, 2))
-        pw1 = new_operand(E4, "pw1", X + 26 * KB)
-        quantise(pw1, pw1_last[:], W - QUARTER)
-        gate(pw1_planes[0], p1[:, :, HALVES[0]], 1, range(2, PACK))
-        pw1_grouped = new_grouped("pw1_grouped", K1, W - QUARTER)
-        weave(G, pw1_grouped[:, 0 : 2 * W], pw1_planes[0][:])
-        weave(G, pw1_grouped[:, 2 * W : 3 * W], pw1_planes[1][:, :, 0:QUARTER])
-        v_gathered = [new_planes("v_gathered%d" % b, (K2, X + 6 * KB)[b], BF16) for b in range(B)]
-        for j in range(PACK - 1):
-            nc.vector.tensor_copy(v_gathered[1][:, j, :], v_planes[j][:].indirect(listed(1)))
-        gather_plane(v_gathered[0][:, 0, :], v_planes[0], listed(0))
-        staged_c0 = [stage(S, c0[:, HALVES[0]], "staged_c0_0", X + 29 * KB)]
-        gather_plane(v_gathered[0][:, 1, :], v_planes[1], listed(0))
-        scatter(S, dv_windows[2], staged_c0[0][:], 0, HALVES[0])
-        for j in range(2, PACK):
-            gather_plane(v_gathered[0][:, j, :], v_planes[j], listed(0))
-        gather_plane(v_gathered[1][:, 3, :], v_planes[3], listed(1))
-        quantise(pw1, pw1_grouped[:, 0 : 2 * W], 0)
-        quantise(pw1, pw1_grouped[:, 2 * W : 3 * W], HALF)
-        dv1 = [product("bank2", dom1, 0, pw1)]
-        v0_grouped = [new_grouped("v0_grouped%d" % h, (K3, K1)[h], HALF) for h in range(2)]
-        v0 = new_operand(E4, "v0", Q0B)
+        scatter(S, dv_windows[1], staged_a1[0][:], 0, HALVES[0])
+        p1 = new_planes("p1", K2, F32)
+        weights(p1, scores1, neg_lse1)
+        staged_a1.append(stage(S, a1[1][:], "staged_a1_1", Q0 + 3 * KB))
+        staged_a2 = stage(S, a2[:], "staged_a2", Q0 + 4 * KB)
+        scatter(S, dv_windows[1], staged_a1[1][:], 0, HALVES[1])
+        pw1_planes = new_planes("pw1_planes", DOM1, F32)
+        gate(pw1_planes, p1, 1)
+        dom1 = quantised(dom1_grouped, E5, "dom1")
+        pw1_grouped = new_grouped("pw1_grouped", X + 14 * KB)
+        weave(G, pw1_grouped[:], pw1_planes[:])
+        v_gathered = [new_planes("v_gathered%d" % b, (K2, X + 12 * KB)[b], BF16) for b in range(B)]
+        for j in range(PACK):
+            gather_plane((S, V, V, V)[j], v_gathered[0][:, j, :], v_planes[j], listed(0))
+        staged_a3 = stage(S, a3[:], "staged_a3", Q0 + 6 * KB)
         for h in range(2):
-            weave(V, v0_grouped[h][:], v_gathered[0][:, :, HALVES[h]])
-        quantise(v0, v0_grouped[0][:], 0)
-        staged_a1 = [stage(V, dv1[0][:, HALVES[0]], "staged_a1_0", K2)]
-        quantise(v0, v0_grouped[1][:], HALF)
-        staged_b0.append(stage(S, b0[1][:], "staged_b0_1", V3))
-        staged_c0.append(stage(S, c0[:, HALVES[1]], "staged_c0_1", V3 + KB))
-        staged_d0 = stage(S, d0[:], "staged_d0", V3 + 6 * KB)
-        dv1.extend(product("bank%d" % (2, 3, 0, 1)[j], dom1, j, pw1) for j in range(1, PACK))
-        dp0 = [product("bank%d" % (4 + t), do0, t, v0) for t in range(PACK)]
-        qm0_grouped = new_grouped("qm0_grouped", K1)
+            scatter(S, dv_windows[2], staged_a2[:, HALVES[h]], 0, HALVES[h])
+            scatter(S, dv_windows[3], staged_a3[:, HALVES[h]], 0, HALVES[h])
+        do0_grouped = new_grouped("do0_grouped", X + 10 * KB)
+        deal(V, do0_grouped[:], do0_raw[:])
+        pw1 = quantised(pw1_grouped, E4, "pw1", DO0)
+        do0 = quantised(do0_grouped, E5, "do0")
+        dv1 = {j: product("bank%d" % j, dom1, j, pw1) for j in range(PACK)}
+        v0_grouped = new_grouped("v0_grouped", X + 8 * KB)
+        weave(G, v0_grouped[:], v_gathered[0][:])
+        qm0_grouped = new_grouped("qm0_grouped", K2)
         weave(G, qm0_grouped[:], qm0_raw[:])
-        scatter(V, dv_windows[0], staged_a1[0][:], 1, HALVES[0])
-        scatter(S, dv_windows[1], staged_b0[1][:], 0, HALVES[1])
-        staged_b1 = stage(S, dv1[1][:], "staged_b1", V2)
-        scatter(S, dv_windows[2], staged_c0[1][:], 0, HALVES[1])
-        scatter(S, dv_windows[3], staged_d0[:, HALVES[0]], 0, HALVES[0])
-        scatter(S, dv_windows[1], staged_b1[:, HALVES[0]], 1, HALVES[0])
-        scatter(S, dv_windows[3], staged_d0[:, HALVES[1]], 0, HALVES[1])
-        staged_d1 = stage(S, dv1[3][:], "staged_d1", V2 + 2 * KB)
-        ds0_planes = [new_planes("ds0_planes%d" % h, DOM0A + 2 * KB * h, BF16, HALF) for h in range(2)]
-        ds0_grouped = [new_grouped("ds0_grouped%d" % h, (Q0A, DOM0A)[h], HALF) for h in range(2)]
-        score_gradient(ds0_planes[0], dp0, pw0_planes[0], 0, HALVES[0])
-        score_gradient(ds0_planes[1], dp0, pw0_planes[1], 0, HALVES[1], range(0, 2))
-        staged_a1.append(stage(V, dv1[0][:, HALVES[1]], "staged_a1_1", Y))
-        score_gradient(ds0_planes[1], dp0, pw0_planes[1], 0, HALVES[1], range(2, PACK))
-        weave(G, ds0_grouped[0][:], ds0_planes[0][:])
-        scatter(V, dv_windows[0], staged_a1[1][:], 1, HALVES[1])
-        store(out_1, 0, dv_windows[0])
-        scatter(S, dv_windows[1], staged_b1[:, HALVES[1]], 1, HALVES[1])
-        scatter(S, dv_windows[3], staged_d1[:, HALVES[0]], 1, HALVES[0])
-        store(out_1, 1, dv_windows[1], S)
-        weave(V, ds0_grouped[1][:], ds0_planes[1][:])
-        ds0 = new_operand(E5, "ds0", X + 22 * KB)
-        quantise(ds0, ds0_grouped[0][:], 0)
-        qm0 = quantised(qm0_grouped, E4, "qm0", DOM0A + 2 * KB)
-        do1_grouped = new_grouped("do1_grouped", Q0A)
-        quantise(ds0, ds0_grouped[1][:], HALF)
+        staged_b = {}
+
+        def stage_pair(pair, at):
+            for h in range(2):
+                for j in (pair, pair + 1):
+                    staged_b[j, h] = stage(V, dv1[j][:, HALVES[h]], "staged_b%d_%d" % (j, h), at + KB * (2 * h + j - pair))
+
+        for j in range(PACK):
+            gather_plane(V, v_gathered[1][:, j, :], v_planes[j], listed(1))
+            if j == 0:
+                stage_pair(0, X + 14 * KB + 2 * KB)
+        v0 = quantised(v0_grouped, E4, "v0", QM0 + 4 * KB)
+        dp0 = [product("bank%d" % (4 + t), do0, t, v0) for t in range(PACK)]
+        v1_grouped = new_grouped("v1_grouped", X + 6 * KB)
+        weave(G, v1_grouped[:], v_gathered[1][:])
+        stage_pair(2, QM0)
+        for pair in range(0, PACK, 2):
+            for h in range(2):
+                for j in (pair, pair + 1):
+                    scatter(S, dv_windows[j], staged_b[j, h][:], 1, HALVES[h])
+            store(out_1, pair, dv_windows[pair])
+            store(out_1, pair + 1, dv_windows[pair + 1])
+        ds0_planes = new_planes("ds0_planes", Q1 + 2 * KB, BF16)
+        for t in range(PACK):
+            for h in range(2):
+                score_gradient(ds0_planes[:, :, HALVES[h]], dp0, pw0_planes[h], 0, HALVES[h], range(t, t + 1))
+        do1_grouped = new_grouped("do1_grouped", X + 12 * KB)
         deal(V, do1_grouped[:], do1_raw[:])
-        dk0 = {j: product("bank%d" % (2, 3, 1)[j], qm0, j, ds0) for j in range(3)}
-        v1_grouped = new_grouped("v1_grouped", K1)
-        weave(V, v1_grouped[:], v_gathered[1][:])
-        do1 = quantised(do1_grouped, E5, "do1", DO1 + 4 * KB)
-        staged_c1 = [stage(V, dv1[2][:, HALVES[0]], "staged_c1_0", X + 6 * KB)]
-        v1 = quantised(v1_grouped, E4, "v1", Q0B)
+        v1 = quantised(v1_grouped, E4, "v1")
+        do1 = quantised(do1_grouped, E5, "do1")
         dp1 = [product("bank%d" % (4 + t), do1, t, v1) for t in range(PACK)]
-        qm1_grouped = new_grouped("qm1_grouped", K1)
+        ds0_grouped = new_grouped("ds0_grouped", DO1)
+        weave(V, ds0_grouped[:], ds0_planes[:])
+        qm0 = quantised(qm0_grouped, E4, "qm0", X + 12 * KB)
+        ds0 = quantised(ds0_grouped, E5, "ds0")
+        dk0 = {j: product("bank%d" % (0, 5, 1, 2)[j], qm0, j, ds0) for j in (0, 2, 1, 3)}
+        qm1_grouped = new_grouped("qm1_grouped", DO1)
         weave(G, qm1_grouped[:], qm1_raw[:])
-        scatter(V, dv_windows[2], staged_c1[0][:], 1, HALVES[0])
-        staged_e0 = stage(S, dk0[0][:], "staged_e0", V3)
-        scatter(S, dv_windows[3], staged_d1[:, HALVES[1]], 1, HALVES[1])
-        staged_f0 = stage(S, dk0[1][:], "staged_f0", V3 + 2 * KB)
-        scatter(S, dk_windows[0], staged_e0[:, HALVES[0]], 0, HALVES[0])
-        store(out_1, 3, dv_windows[3], S)
-        scatter(S, dk_windows[1], staged_f0[:, HALVES[0]], 0, HALVES[0])
-        ds1_planes = [new_planes("ds1_planes%d" % h, QM0 + 2 * KB * h, BF16, HALF) for h in range(2)]
-        ds1_grouped = [new_grouped("ds1_grouped%d" % h, (DO1, QM0)[h], HALF) for h in range(2)]
-        score_gradient(ds1_planes[0], dp1, pw1_planes[0], 1, HALVES[0])
-        score_gradient(ds1_planes[1], dp1, pw1_planes[1], 1, HALVES[1], range(0, 2))
-        staged_c1.append(stage(V, dv1[2][:, HALVES[1]], "staged_c1_1", DO0))
-        score_gradient(ds1_planes[1], dp1, pw1_planes[1], 1, HALVES[1], range(2, PACK))
-        dk0[3] = product("bank0", qm0, 3, ds0)
-        weave(G, ds1_grouped[0][:], ds1_planes[0][:])
-        scatter(V, dv_windows[2], staged_c1[1][:], 1, HALVES[1])
-        store(out_1, 2, dv_windows[2])
-        for j in range(2):
-            scatter(S, dk_windows[j], (staged_e0, staged_f0)[j][:, HALVES[1]], 0, HALVES[1])
-        weave(V, ds1_grouped[1][:], ds1_planes[1][:])
-        ds1 = new_operand(E5, "ds1", X + 24 * KB)
-        quantise(ds1, ds1_grouped[0][:], 0)
-        qm1 = quantised(qm1_grouped, E4, "qm1", QM0 + 2 * KB)
-        staged_g0 = stage(V, dk0[2][:], "staged_g0", DO1)
-        quantise(ds1, ds1_grouped[1][:], HALF)
-        dk1 = {j: product("bank%d" % (4 + j), qm1, j, ds1) for j in (2, 0, 3, 1)}
-        scatter(V, dk_windows[2], staged_g0[:], 0)
-        staged_h = work.tile([P, B * N], F32, name="staged_h", offset=K1, align_bytes=64)
-        copy_on(S, staged_h[:, 0:N], dk0[3][:])
-        staged_g1 = stage(S, dk1[2][:], "staged_g1", V0)
-        staged_1 = [stage(S, dk1[j][:], "staged_dk1_%d" % j, V1 + 2 * KB * j) for j in range(2)]
-        scatter(V, dk_windows[2], staged_g1[:], 1)
-        store(out_0, 2, dk_windows[2])
-        scatter(S, dk_windows[0], staged_1[0][:, HALVES[0]], 1, HALVES[0])
-        copy_on(S, staged_h[:, N : 2 * N], dk1[3][:])
-        scatter(S, dk_windows[0], staged_1[0][:, HALVES[1]], 1, HALVES[1])
-        scatter(S, dk_windows[1], staged_1[1][:, HALVES[0]], 1, HALVES[0])
+        ds1_planes = new_planes("ds1_planes", DO0, BF16)
+        score_gradient(ds1_planes[:], dp1, pw1_planes, 1, WHOLE)
+        staged_c = {1: stage(V, dk0[1][:], "staged_c1", V3 + 2 * KB)}
+        ds1_grouped = new_grouped("ds1_grouped", DO0 + 4 * KB)
+        weave(G, ds1_grouped[:], ds1_planes[:])
+        scatter(V, dk_windows[1], staged_c[1][:], 0)
+        for j in (0, 2):
+            staged_c[j] = stage(S, dk0[j][:], "staged_c%d" % j, V3 + 2 * KB * j)
+        for j, h in ((0, 0), (2, 0), (0, 1)):
+            scatter(S, dk_windows[j], staged_c[j][:, HALVES[h]], 0, HALVES[h])
+        ds1 = quantised(ds1_grouped, E5, "ds1")
+        qm1 = new_operand(E4, "qm1", DO0 + 3 * KB + 512)
+        for h in range(2):
+            quantise(qm1, qm1_grouped[:, 2 * W * h : 2 * W * (h + 1)], h * HALF)
+        dk1 = {j: product("bank%d" % (4 + j), qm1, j, ds1) for j in (1, 0, 3, 2)}
+        staged_last = work.tile([P, B * N], F32, name="staged_last", offset=DO0 - KB, align_bytes=64)
+        copy_on(V, staged_last[:, 0:N], dk0[3][:])
+        staged_d = {1: stage(V, dk1[1][:], "staged_d1", V2 + 2 * KB)}
+        scatter(V, dk_windows[1], staged_d[1][:], 1)
+        store(out_0, 1, dk_windows[1])
+        scatter(S, dk_windows[2], staged_c[2][:, HALVES[1]], 0, HALVES[1])
+        staged_d[0] = stage(S, dk1[0][:], "staged_d0", V2)
+        copy_on(S, staged_last[:, N : 2 * N], dk1[3][:])
+        staged_d[2] = stage(S, dk1[2][:], "staged_d2", V3 + 4 * KB)
+        scatter(S, dk_windows[0], staged_d[0][:, HALVES[0]], 1, HALVES[0])
+        scatter(S, dk_windows[2], staged_d[2][:, HALVES[0]], 1, HALVES[0])
+        scatter(S, dk_windows[0], staged_d[0][:, HALVES[1]], 1, HALVES[1])
         store(out_0, 0, dk_windows[0], S)
-        scatter(S, dk_windows[1], staged_1[1][:, HALVES[1]], 1, HALVES[1])
-        store(out_0, 1, dk_windows[1], S)
-        nc.vector.tensor_copy(dk_windows[3][:].indirect(offsets[:]), staged_h[:])
+        scatter(S, dk_windows[2], staged_d[2][:, HALVES[1]], 1, HALVES[1])
+        store(out_0, 2, dk_windows[2], S)
+        nc.vector.tensor_copy(dk_windows[3][:].indirect(offsets[:]), staged_last[:])
         store(out_0, 3, dk_windows[3])

@@ -172,7 +172,7 @@ def tile_attend_gat_lse_kv_kernel(tc, qT, kT, vT, doT, lse, delta, rw, qm, dom, 
 
         def score_gradient(planes, banks, pw, b, cols, ts=range(PACK)):
             for t in ts:
-                nc.vector.scalar_tensor_tensor(planes[:, t, :], banks[t][:, cols], delta_sb[:, b, t : t + 1], pw[:, t, :], ALU.subtract, ALU.mult)
+                nc.vector.scalar_tensor_tensor(planes[:, t, :], banks[t][:, cols], neg_delta[:, b, t : t + 1], pw[:, t, :], ALU.add, ALU.mult)
 
         V, S, G = nc.vector, nc.scalar, nc.gpsimd
 
@@ -186,8 +186,9 @@ def tile_attend_gat_lse_kv_kernel(tc, qT, kT, vT, doT, lse, delta, rw, qm, dom, 
         q1_raw = load_rows(qT[1], "q1_raw", Q1)
         dom1_raw = load_rows(dom[1], "dom1_raw", DOM1)
         v_planes = [load_plane(vT, j, "v_plane%d" % j, (V0, V1, V2, V3)[j]) for j in range(PACK)]
+        delta_raw = work.tile([P, B, PACK], F32, name="delta_raw", offset=X + 34 * KB, align_bytes=64)
+        nc.sync.dma_start(delta_raw[:], delta.rearrange("b (p t) o -> p b (t o)", t=PACK))
         do0_raw = load_rows(doT[0], "do0_raw", DO0)
-        delta_sb = load_per_row(delta, "delta_sb")
         qm0_raw = load_rows(qm[0], "qm0_raw", QM0)
         do1_raw = load_rows(doT[1], "do1_raw", DO1)
         qm1_raw = load_rows(qm[1], "qm1_raw", QM1)
@@ -270,19 +271,18 @@ def tile_attend_gat_lse_kv_kernel(tc, qT, kT, vT, doT, lse, delta, rw, qm, dom, 
         dom1 = quantised(dom1_grouped, E5, "dom1")
         pw1_grouped = new_grouped("pw1_grouped", X + 14 * KB)
         weave(G, pw1_grouped[:], pw1_planes[:])
-        v_gathered = [new_planes("v_gathered%d" % b, (K2, X + 12 * KB)[b], BF16) for b in range(B)]
+        v_gathered = [new_planes("v_gathered%d" % b, (K2, X + 16 * KB)[b], BF16) for b in range(B)]
         for j in range(PACK):
             gather_plane((S, V, V, V)[j], v_gathered[0][:, j, :], v_planes[j], listed(0))
         staged_a3 = stage(S, a3[:], "staged_a3", Q0 + 6 * KB)
         for h in range(2):
             scatter(S, dv_windows[2], staged_a2[:, HALVES[h]], 0, HALVES[h])
             scatter(S, dv_windows[3], staged_a3[:, HALVES[h]], 0, HALVES[h])
-        do0_grouped = new_grouped("do0_grouped", X + 10 * KB)
-        deal(V, do0_grouped[:], do0_raw[:])
-        pw1 = quantised(pw1_grouped, E4, "pw1", DO0)
-        do0 = quantised(do0_grouped, E5, "do0")
+        neg_delta = work.tile([P, B, PACK], F32, name="neg_delta", offset=K2 + 7 * KB, align_bytes=64)
+        nc.gpsimd.tensor_scalar(neg_delta[:], delta_raw[:], -1.0, 0.0, ALU.mult, ALU.add)
+        pw1 = quantised(pw1_grouped, E4, "pw1", X + 34 * KB)
         dv1 = {j: product("bank%d" % j, dom1, j, pw1) for j in range(PACK)}
-        v0_grouped = new_grouped("v0_grouped", X + 8 * KB)
+        v0_grouped = new_grouped("v0_grouped", X + 12 * KB)
         weave(G, v0_grouped[:], v_gathered[0][:])
         qm0_grouped = new_grouped("qm0_grouped", K2)
         weave(G, qm0_grouped[:], qm0_raw[:])
@@ -296,12 +296,15 @@ def tile_attend_gat_lse_kv_kernel(tc, qT, kT, vT, doT, lse, delta, rw, qm, dom, 
         for j in range(PACK):
             gather_plane(V, v_gathered[1][:, j, :], v_planes[j], listed(1))
             if j == 0:
-                stage_pair(0, X + 14 * KB + 2 * KB)
+                stage_pair(0, X + 5 * KB)
+        do0_grouped = new_grouped("do0_grouped", QM0)
+        deal(V, do0_grouped[:], do0_raw[:])
         v0 = quantised(v0_grouped, E4, "v0", QM0 + 4 * KB)
+        do0 = quantised(do0_grouped, E5, "do0")
         dp0 = [product("bank%d" % (4 + t), do0, t, v0) for t in range(PACK)]
-        v1_grouped = new_grouped("v1_grouped", X + 6 * KB)
+        v1_grouped = new_grouped("v1_grouped", QM0)
         weave(G, v1_grouped[:], v_gathered[1][:])
-        stage_pair(2, QM0)
+        stage_pair(2, X + 12 * KB)
         for pair in range(0, PACK, 2):
             for h in range(2):
                 for j in (pair, pair + 1):
@@ -312,16 +315,16 @@ def tile_attend_gat_lse_kv_kernel(tc, qT, kT, vT, doT, lse, delta, rw, qm, dom, 
         for t in range(PACK):
             for h in range(2):
                 score_gradient(ds0_planes[:, :, HALVES[h]], dp0, pw0_planes[h], 0, HALVES[h], range(t, t + 1))
-        do1_grouped = new_grouped("do1_grouped", X + 12 * KB)
+        do1_grouped = new_grouped("do1_grouped", X + 16 * KB)
         deal(V, do1_grouped[:], do1_raw[:])
         v1 = quantised(v1_grouped, E4, "v1")
         do1 = quantised(do1_grouped, E5, "do1")
         dp1 = [product("bank%d" % (4 + t), do1, t, v1) for t in range(PACK)]
         ds0_grouped = new_grouped("ds0_grouped", DO1)
         weave(V, ds0_grouped[:], ds0_planes[:])
-        qm0 = quantised(qm0_grouped, E4, "qm0", X + 12 * KB)
+        qm0 = quantised(qm0_grouped, E4, "qm0", X + 16 * KB)
         ds0 = quantised(ds0_grouped, E5, "ds0")
-        dk0 = {j: product("bank%d" % (0, 5, 1, 2)[j], qm0, j, ds0) for j in (0, 2, 1, 3)}
+        dk0 = {j: product("bank%d" % (0, 4, 1, 2)[j], qm0, j, ds0) for j in (0, 2, 1, 3)}
         qm1_grouped = new_grouped("qm1_grouped", DO1)
         weave(G, qm1_grouped[:], qm1_raw[:])
         ds1_planes = new_planes("ds1_planes", DO0, BF16)
@@ -338,19 +341,19 @@ def tile_attend_gat_lse_kv_kernel(tc, qT, kT, vT, doT, lse, delta, rw, qm, dom, 
         qm1 = new_operand(E4, "qm1", DO0 + 3 * KB + 512)
         for h in range(2):
             quantise(qm1, qm1_grouped[:, 2 * W * h : 2 * W * (h + 1)], h * HALF)
-        dk1 = {j: product("bank%d" % (4 + j), qm1, j, ds1) for j in (1, 0, 3, 2)}
+        dk1 = {j: product("bank%d" % (4 + j), qm1, j, ds1) for j in (1, 3, 0, 2)}
         staged_last = work.tile([P, B * N], F32, name="staged_last", offset=DO0 - KB, align_bytes=64)
         copy_on(V, staged_last[:, 0:N], dk0[3][:])
         staged_d = {1: stage(V, dk1[1][:], "staged_d1", V2 + 2 * KB)}
+        copy_on(V, staged_last[:, N : 2 * N], dk1[3][:])
         scatter(V, dk_windows[1], staged_d[1][:], 1)
         store(out_0, 1, dk_windows[1])
         scatter(S, dk_windows[2], staged_c[2][:, HALVES[1]], 0, HALVES[1])
-        staged_d[0] = stage(S, dk1[0][:], "staged_d0", V2)
-        copy_on(S, staged_last[:, N : 2 * N], dk1[3][:])
-        staged_d[2] = stage(S, dk1[2][:], "staged_d2", V3 + 4 * KB)
-        scatter(S, dk_windows[0], staged_d[0][:, HALVES[0]], 1, HALVES[0])
+        staged_d[0] = [stage(S, dk1[0][:, HALVES[h]], "staged_d0_%d" % h, V2 + KB * h) for h in range(2)]
+        scatter(S, dk_windows[0], staged_d[0][0][:], 1, HALVES[0])
+        staged_d[2] = stage(S, dk1[2][:], "staged_d2", V2 - KB)
+        scatter(S, dk_windows[0], staged_d[0][1][:], 1, HALVES[1])
         scatter(S, dk_windows[2], staged_d[2][:, HALVES[0]], 1, HALVES[0])
-        scatter(S, dk_windows[0], staged_d[0][:, HALVES[1]], 1, HALVES[1])
         store(out_0, 0, dk_windows[0], S)
         scatter(S, dk_windows[2], staged_d[2][:, HALVES[1]], 1, HALVES[1])
         store(out_0, 2, dk_windows[2], S)

@@ -107,14 +107,12 @@ def tile_attend_gat_lse_kv_kernel(tc, qT, kT, vT, doT, lse, delta, rw, qm, dom, 
                 )
 
         def weave(engine, grouped, planes):
-            if engine is nc.gpsimd:
-                copy_on(engine, grouped.rearrange("p (c j) -> p c j", j=PACK), planes.rearrange("p j c -> p c j"))
-            else:
-                copy_on(
-                    engine,
-                    grouped.rearrange("p (c i j) -> p c j i", i=4, j=PACK),
-                    planes.rearrange("p j (c i) -> p c j i", i=4),
-                )
+            run = 2
+            copy_on(
+                engine,
+                grouped.rearrange("p (c i j) -> p c j i", i=run, j=PACK),
+                planes.rearrange("p j (c i) -> p c j i", i=run),
+            )
 
         def gather_plane(engine, out, plane, slots):
             if engine is nc.vector:
@@ -184,8 +182,9 @@ def tile_attend_gat_lse_kv_kernel(tc, qT, kT, vT, doT, lse, delta, rw, qm, dom, 
         dom0_raw = load_rows(dom[0], "dom0_raw", DOM0)
         rw_sb = load_per_row(rw, "rw_sb")
         q1_raw = load_rows(qT[1], "q1_raw", Q1)
+        v_planes = [load_plane(vT, 0, "v_plane0", V0)]
         dom1_raw = load_rows(dom[1], "dom1_raw", DOM1)
-        v_planes = [load_plane(vT, j, "v_plane%d" % j, (V0, V1, V2, V3)[j]) for j in range(PACK)]
+        v_planes.extend(load_plane(vT, j, "v_plane%d" % j, (V0, V1, V2, V3)[j]) for j in range(1, PACK))
         delta_raw = work.tile([P, B, PACK], F32, name="delta_raw", offset=X + 34 * KB, align_bytes=64)
         nc.sync.dma_start(delta_raw[:], delta.rearrange("b (p t) o -> p b (t o)", t=PACK))
         do0_raw = load_rows(doT[0], "do0_raw", DO0)
@@ -223,57 +222,63 @@ def tile_attend_gat_lse_kv_kernel(tc, qT, kT, vT, doT, lse, delta, rw, qm, dom, 
         for h in range(2):
             quantise(q0, q0_grouped[h][:], h * HALF)
         weave(V, k1_grouped[2][:], k1_gathered[:, :, k1_parts[2]])
-        dom0_grouped = new_grouped("dom0_grouped", X + 16 * KB)
-        weave(V, dom0_grouped[:], dom0_raw[:])
+        dom0_grouped = [new_grouped("dom0_grouped%d" % h, (X + 16 * KB, X + 2 * KB)[h], HALF) for h in range(2)]
+        weave(V, dom0_grouped[0][:], dom0_raw[:, :, HALVES[0]])
         pw0_planes = [new_planes("pw0_planes%d" % h, X + 20 * KB + 4 * KB * h, F32, HALF) for h in range(2)]
         for h in range(2):
             banks = [product("bank%d" % (4 * h + t), q0, t, k0[h], HALVES[0]) for t in range(PACK)]
             weights(pw0_planes[h], banks, neg_lse0)
         pw0 = new_operand(E4, "pw0")
-        pw0_grouped = [new_grouped("pw0_grouped%d" % h, X + 28 * KB + 2 * KB * h, HALF) for h in range(2)]
+        pw0_grouped = [new_grouped("pw0_grouped%d" % h, (X + 28 * KB, X + 16 * KB)[h], HALF) for h in range(2)]
         k1 = new_operand(E4, "k1", X + 28 * KB)
+        dom0 = new_operand(E5, "dom0")
         gate(pw0_planes[0], pw0_planes[0], 0)
-        dom0 = quantised(dom0_grouped, E5, "dom0")
+        quantise(dom0, dom0_grouped[0][:], 0)
         weave(V, pw0_grouped[0][:], pw0_planes[0][:])
         gate(pw0_planes[1], pw0_planes[1], 0)
         quantise(pw0, pw0_grouped[0][:], 0)
+        q1_grouped = [new_grouped("q1_grouped%d" % h, (X + 16 * KB, X + 2 * KB)[h], HALF) for h in range(2)]
+        deal(S, q1_grouped[1][:], q1_raw[:], range(2, PACK))
+        deal(V, q1_grouped[0][:], q1_raw[:], range(0, 2))
+        for n in (2, 0, 1):
+            quantise(k1, k1_grouped[n][:], k1_parts[n].start)
+        q1 = new_operand(E4, "q1")
+        for h in range(2):
+            quantise(q1, q1_grouped[h][:], h * HALF)
         weave(V, pw0_grouped[1][:], pw0_planes[1][:])
-        quantise(k1, k1_grouped[2][:], HALF)
+        weave(V, dom0_grouped[1][:], dom0_raw[:, :, HALVES[1]])
         quantise(pw0, pw0_grouped[1][:], HALF)
-        for n in range(2):
-            quantise(k1, k1_grouped[n][:], n * QUARTER)
-        q1_grouped = new_grouped("q1_grouped", X + 2 * KB)
-        deal(S, q1_grouped[:], q1_raw[:])
-        q1 = quantised(q1_grouped, E4, "q1", X + 30 * KB)
-        a0 = [product("bank0", dom0, 0, pw0, HALVES[0])]
+        quantise(dom0, dom0_grouped[1][:], HALF)
         a1 = [product("bank1", dom0, 1, pw0, HALVES[0])]
-        a0.append(product("bank2", dom0, 0, pw0, HALVES[1]))
+        a0 = [product("bank0", dom0, 0, pw0, HALVES[0])]
         scores1 = [product("bank%d" % (4 + t), q1, t, k1) for t in range(PACK)]
-        a1.append(product("bank5", dom0, 1, pw0, HALVES[1]))
+        a1.append(product("bank4", dom0, 1, pw0, HALVES[1]))
+        a0.append(product("bank5", dom0, 0, pw0, HALVES[1]))
         a2 = product("bank6", dom0, 2, pw0)
         a3 = product("bank7", dom0, 3, pw0)
-        staged_a0 = [stage(S, a0[0][:], "staged_a0_0", Q1)]
-        staged_a1 = [stage(S, a1[0][:], "staged_a1_0", Q1 + KB)]
-
-        dom1_grouped = new_grouped("dom1_grouped", X + 5 * KB)
-        weave(G, dom1_grouped[:], dom1_raw[:])
-        scatter(V, dv_windows[0], staged_a0[0][:], 0, HALVES[0])
-        staged_a0.append(stage(V, a0[1][:], "staged_a0_1", X + 4 * KB))
-        scatter(V, dv_windows[0], staged_a0[1][:], 0, HALVES[1])
+        staged_a1 = [stage(S, a1[0][:], "staged_a1_0", X + KB)]
+        staged_a0 = [stage(S, a0[0][:], "staged_a0_0", X)]
         scatter(S, dv_windows[1], staged_a1[0][:], 0, HALVES[0])
+
+        dom1_grouped = new_grouped("dom1_grouped", X + 3 * KB)
+        weave(G, dom1_grouped[:], dom1_raw[:])
+        v_gathered = [new_planes("v_gathered%d" % b, (DOM0 + 4 * KB, X + 16 * KB)[b], BF16) for b in range(B)]
+        scatter(V, dv_windows[0], staged_a0[0][:], 0, HALVES[0])
+        gather_plane(V, v_gathered[0][:, 0, :], v_planes[0], listed(0))
         p1 = new_planes("p1", K2, F32)
         weights(p1, scores1, neg_lse1)
         staged_a1.append(stage(S, a1[1][:], "staged_a1_1", Q0 + 3 * KB))
-        staged_a2 = stage(S, a2[:], "staged_a2", Q0 + 4 * KB)
+        staged_a0.append(stage(S, a0[1][:], "staged_a0_1", Q0 + 4 * KB))
         scatter(S, dv_windows[1], staged_a1[1][:], 0, HALVES[1])
+        scatter(S, dv_windows[0], staged_a0[1][:], 0, HALVES[1])
         pw1_planes = new_planes("pw1_planes", DOM1, F32)
         gate(pw1_planes, p1, 1)
         dom1 = quantised(dom1_grouped, E5, "dom1")
         pw1_grouped = new_grouped("pw1_grouped", X + 14 * KB)
         weave(G, pw1_grouped[:], pw1_planes[:])
-        v_gathered = [new_planes("v_gathered%d" % b, (K2, X + 16 * KB)[b], BF16) for b in range(B)]
-        for j in range(PACK):
-            gather_plane((S, V, V, V)[j], v_gathered[0][:, j, :], v_planes[j], listed(0))
+        for j in range(1, PACK):
+            gather_plane(V, v_gathered[0][:, j, :], v_planes[j], listed(0))
+        staged_a2 = stage(S, a2[:], "staged_a2", Q1)
         staged_a3 = stage(S, a3[:], "staged_a3", Q0 + 6 * KB)
         for h in range(2):
             scatter(S, dv_windows[2], staged_a2[:, HALVES[h]], 0, HALVES[h])
@@ -284,7 +289,7 @@ def tile_attend_gat_lse_kv_kernel(tc, qT, kT, vT, doT, lse, delta, rw, qm, dom, 
         dv1 = {j: product("bank%d" % j, dom1, j, pw1) for j in range(PACK)}
         v0_grouped = new_grouped("v0_grouped", X + 12 * KB)
         weave(G, v0_grouped[:], v_gathered[0][:])
-        qm0_grouped = new_grouped("qm0_grouped", K2)
+        qm0_grouped = new_grouped("qm0_grouped", DOM0 + 4 * KB)
         weave(G, qm0_grouped[:], qm0_raw[:])
         staged_b = {}
 
@@ -324,32 +329,30 @@ def tile_attend_gat_lse_kv_kernel(tc, qT, kT, vT, doT, lse, delta, rw, qm, dom, 
         weave(V, ds0_grouped[:], ds0_planes[:])
         qm0 = quantised(qm0_grouped, E4, "qm0", X + 16 * KB)
         ds0 = quantised(ds0_grouped, E5, "ds0")
-        dk0 = {j: product("bank%d" % (0, 4, 1, 2)[j], qm0, j, ds0) for j in (0, 2, 1, 3)}
+        dk0 = {j: product("bank%d" % j, qm0, j, ds0) for j in (1, 0, 2, 3)}
         qm1_grouped = new_grouped("qm1_grouped", DO1)
         weave(G, qm1_grouped[:], qm1_raw[:])
         ds1_planes = new_planes("ds1_planes", DO0, BF16)
         score_gradient(ds1_planes[:], dp1, pw1_planes, 1, WHOLE)
-        staged_c = {1: stage(V, dk0[1][:], "staged_c1", V3 + 2 * KB)}
+        staged_c = {j: stage(S, dk0[j][:], "staged_c%d" % j, V3 + 2 * KB * j) for j in (1, 0, 2)}
         ds1_grouped = new_grouped("ds1_grouped", DO0 + 4 * KB)
         weave(G, ds1_grouped[:], ds1_planes[:])
         scatter(V, dk_windows[1], staged_c[1][:], 0)
-        for j in (0, 2):
-            staged_c[j] = stage(S, dk0[j][:], "staged_c%d" % j, V3 + 2 * KB * j)
         for j, h in ((0, 0), (2, 0), (0, 1)):
             scatter(S, dk_windows[j], staged_c[j][:, HALVES[h]], 0, HALVES[h])
         ds1 = quantised(ds1_grouped, E5, "ds1")
         qm1 = new_operand(E4, "qm1", DO0 + 3 * KB + 512)
         for h in range(2):
             quantise(qm1, qm1_grouped[:, 2 * W * h : 2 * W * (h + 1)], h * HALF)
-        dk1 = {j: product("bank%d" % (4 + j), qm1, j, ds1) for j in (1, 3, 0, 2)}
+        dk1 = {j: product("bank%d" % (4 + j), qm1, j, ds1) for j in (1, 0, 3, 2)}
         staged_last = work.tile([P, B * N], F32, name="staged_last", offset=DO0 - KB, align_bytes=64)
         copy_on(V, staged_last[:, 0:N], dk0[3][:])
         staged_d = {1: stage(V, dk1[1][:], "staged_d1", V2 + 2 * KB)}
+        staged_d[0] = [stage(V, dk1[0][:, HALVES[h]], "staged_d0_%d" % h, V2 + KB * h) for h in range(2)]
         copy_on(V, staged_last[:, N : 2 * N], dk1[3][:])
         scatter(V, dk_windows[1], staged_d[1][:], 1)
         store(out_0, 1, dk_windows[1])
         scatter(S, dk_windows[2], staged_c[2][:, HALVES[1]], 0, HALVES[1])
-        staged_d[0] = [stage(S, dk1[0][:, HALVES[h]], "staged_d0_%d" % h, V2 + KB * h) for h in range(2)]
         scatter(S, dk_windows[0], staged_d[0][0][:], 1, HALVES[0])
         staged_d[2] = stage(S, dk1[2][:], "staged_d2", V2 - KB)
         scatter(S, dk_windows[0], staged_d[0][1][:], 1, HALVES[1])

@@ -107,7 +107,7 @@ def tile_attend_gat_lse_kv_kernel(tc, qT, kT, vT, doT, lse, delta, rw, qm, dom, 
                 )
 
         def weave(engine, grouped, planes):
-            run = 2
+            run = 2 if engine is nc.gpsimd else 4
             copy_on(
                 engine,
                 grouped.rearrange("p (c i j) -> p c j i", i=run, j=PACK),

from contextlib import ExitStack

import concourse.mybir as mybir

B, N, T, D, R = 2, 512, 2048, 512, 512
FLOPS = 4 * 2 * B * N * D * R

F32 = mybir.dt.float32
BF16 = mybir.dt.bfloat16
U32 = mybir.dt.uint32
U16 = mybir.dt.uint16
U8 = mybir.dt.uint8
E4 = mybir.dt.float8_e4m3fn_x4
E5 = mybir.dt.float8_e5m2_x4
ACT = mybir.ActivationFunctionType
ALU = mybir.AluOpType

P = 128
PACK = 4
W = 512
HALF = W // 2
QUARTER = W // 4
LIST_COLS = N // 16
HALVES = [slice(0, HALF), slice(HALF, W)]
WHOLE = slice(0, W)
KB = 1024
K0, K1, K2, K3, V0, V1, V2, V3 = (8 * KB * n for n in range(8))
Q0, DOM0, Q1, DOM1, DO0, QM0, DO1, QM1 = (64 * KB + 8 * KB * n for n in range(8))
SCALES = 128 * KB
CODES = 137 * KB
X = 171 * KB


def tile_attend_gat_lse_kv_kernel(tc, qT, kT, vT, doT, lse, delta, rw, qm, dom, offs, out_0, out_1):
    nc = tc.nc
    with ExitStack() as ctx:
        keep = ctx.enter_context(tc.tile_pool(name="keep", bufs=1))
        work = ctx.enter_context(tc.tile_pool(name="work", bufs=1))
        psum = ctx.enter_context(tc.psum_pool(name="psum", bufs=1))

        offsets = keep.tile([P, B * LIST_COLS], U16, name="offsets")

        def listed(b, slots=WHOLE):
            return offsets[:, (b * N + slots.start) // 16 : (b * N + slots.stop) // 16]

        def load_rows(x, name, at, cols=WHOLE):
            rows = work.tile([P, PACK, cols.stop - cols.start], F32, name=name, offset=at, align_bytes=64)
            nc.sync.dma_start(rows[:], x.rearrange("(p j) w -> p j w", j=PACK)[:, :, cols])
            return rows

        def load_plane(pool_t, j, name, at):
            plane = work.tile([P, T], F32, name=name, offset=at, align_bytes=64)
            nc.sync.dma_start(plane[:], pool_t.rearrange("(p j) t -> p j t", j=PACK)[:, j, :])
            return plane

        def load_per_row(x, name):
            col = keep.tile([P, B, PACK], F32, name=name)
            nc.sync.dma_start(col[:], x.rearrange("b (p t) o -> p b (t o)", t=PACK))
            return col

        def new_grouped(name, at, columns=W):
            return work.tile([P, columns * PACK], BF16, name=name, offset=at, align_bytes=64)

        def new_planes(name, at, dtype, columns=W, planes=PACK):
            return work.tile([P, planes, columns], dtype, name=name, offset=at, align_bytes=64)

        operands = []

        def new_operand(fmt, name, scales_at=None):
            codes = work.tile([P, W], U32, name=name + "_codes", offset=CODES + 2 * KB * len(operands), align_bytes=64)
            scales = work.tile([P, W], U8, name=name + "_scales", offset=scales_at or SCALES + W * len(operands), align_bytes=64)
            operands.append(name)
            return codes, scales, fmt

        def quantise(operand, grouped, c0=0):
            codes, scales, fmt = operand
            c1 = c0 + grouped.shape[1] // PACK
            nc.vector.quantize_mx(out=codes[:, c0:c1].bitcast(fmt), scales=scales[:, c0:c1], in_=grouped)

        def quantised(grouped, fmt, name, scales_at=None):
            operand = new_operand(fmt, name, scales_at)
            quantise(operand, grouped[:])
            return operand

        def copy_on(engine, out, in_):
            if engine is nc.vector:
                nc.vector.tensor_copy(out, in_)
            elif engine is nc.scalar:
                nc.scalar.copy(out=out, in_=in_)
            else:
                nc.gpsimd.tensor_scalar(out, in_, 1.0, 0.0, ALU.mult, ALU.add)

        def deal(engine, grouped, rows, ts=range(PACK)):
            n = len(ts)
            if engine is nc.gpsimd:
                for t0 in range(0, n, 2):
                    copy_on(
                        engine,
                        grouped.rearrange("p (t s j) -> p t s j", t=n, j=PACK)[:, t0 : t0 + 2, :, :],
                        rows.rearrange("p j (s t) -> p t s j", t=PACK)[:, ts[t0] : ts[t0] + 2, :, :],
                    )
            else:
                copy_on(
                    engine,
                    grouped.rearrange("p (t s j) -> p s j t", t=n, j=PACK),
                    rows.rearrange("p j (s t) -> p s j t", t=PACK)[:, :, :, ts[0] : ts[0] + n],
                )

        def weave(engine, grouped, planes):
            run = 2 if engine is nc.gpsimd else 4
            copy_on(
                engine,
                grouped.rearrange("p (c i j) -> p c j i", i=run, j=PACK),
                planes.rearrange("p j (c i) -> p c j i", i=run),
            )

        def gather_plane(engine, out, plane, slots):
            if engine is nc.vector:
                nc.vector.tensor_copy(out, plane[:].indirect(slots))
            else:
                nc.scalar.activation(out=out, in_=plane[:].indirect(slots), func=ACT.Copy)

        def gather_into_place(grouped, j, plane, slots):
            nc.vector.tensor_copy(grouped.rearrange("p (n j) -> p n j", j=PACK)[:, :, j], plane[:].indirect(slots))

        def product(tag, stationary, j, moving, slots=WHOLE):
            bank = psum.tile([P, slots.stop - slots.start], F32, name="bank", tag=tag)
            cols = slice(j * P, (j + 1) * P)
            nc.tensor.matmul_mx(
                out=bank[:],
                lhsT=stationary[0][:, cols].bitcast(stationary[2]),
                lhsT_scale=stationary[1][:, cols],
                rhs=moving[0][:, slots].bitcast(moving[2]),
                rhs_scale=moving[1][:, slots],
                start=True,
                stop=True,
            )
            return bank

        def stage(engine, bank, name, at):
            staged = work.tile([P, bank.shape[1]], F32, name=name, offset=at, align_bytes=64)
            copy_on(engine, staged[:], bank)
            return staged

        def scatter(engine, window, staged, b, slots=WHOLE):
            if engine is nc.vector:
                nc.vector.tensor_copy(window[:].indirect(listed(b, slots)), staged)
            else:
                for c0 in range(slots.start, slots.stop, HALF):
                    piece = slice(c0, c0 + HALF)
                    nc.scalar.activation(
                        out=window[:].indirect(listed(b, piece)), in_=staged[:, c0 - slots.start : c0 - slots.start + HALF], func=ACT.Copy
                    )

        def store(out, j, window, queue=nc.sync):
            queue.dma_start(out[j * P : (j + 1) * P, :], window[:])

        def weights(planes, banks, neg_lse):
            for t in range(PACK):
                nc.scalar.activation(out=planes[:, t, :], in_=banks[t][:], func=ACT.Exp, bias=neg_lse[:, t : t + 1])

        def negated(name, at, column):
            neg = work.tile([P, PACK], F32, name=name, offset=at, align_bytes=64)
            nc.scalar.mul(neg[:], column, -1.0)
            return neg

        def gate(gated, planes, b, ts=range(PACK)):
            for t in ts:
                nc.vector.tensor_scalar(gated[:, t, :], planes[:, t, :], rw_sb[:, b, t : t + 1], None, ALU.mult)

        def score_gradient(planes, banks, pw, b, cols, ts=range(PACK)):
            for t in ts:
                nc.vector.scalar_tensor_tensor(planes[:, t, :], banks[t][:, cols], neg_delta[:, b, t : t + 1], pw[:, t, :], ALU.add, ALU.mult)

        V, S, G = nc.vector, nc.scalar, nc.gpsimd

        k_planes = [load_plane(kT, 0, "k_plane0", K0)]
        nc.sync.dma_start(offsets[:], offs)
        k_planes.extend(load_plane(kT, j, "k_plane%d" % j, (K0, K1, K2, K3)[j]) for j in range(1, PACK))
        q0_raw = load_rows(qT[0], "q0_raw", Q0)
        lse_sb = load_per_row(lse, "lse_sb")
        dom0_raw = load_rows(dom[0], "dom0_raw", DOM0)
        rw_sb = load_per_row(rw, "rw_sb")
        q1_raw = load_rows(qT[1], "q1_raw", Q1)
        v_planes = [load_plane(vT, 0, "v_plane0", V0)]
        dom1_raw = load_rows(dom[1], "dom1_raw", DOM1)
        v_planes.extend(load_plane(vT, j, "v_plane%d" % j, (V0, V1, V2, V3)[j]) for j in range(1, PACK))
        delta_raw = work.tile([P, B, PACK], F32, name="delta_raw", offset=X + 34 * KB, align_bytes=64)
        nc.sync.dma_start(delta_raw[:], delta.rearrange("b (p t) o -> p b (t o)", t=PACK))
        do0_raw = load_rows(doT[0], "do0_raw", DO0)
        qm0_raw = load_rows(qm[0], "qm0_raw", QM0)
        do1_raw = load_rows(doT[1], "do1_raw", DO1)
        qm1_raw = load_rows(qm[1], "qm1_raw", QM1)

        dv_windows = [keep.tile([P, T], F32, name="window%d" % j) for j in range(PACK)]
        for window in dv_windows:
            nc.vector.memset(window[:].bitcast(U32), 0)

        k0_grouped = new_grouped("k0_grouped", X)
        k1_gathered = new_planes("k1_gathered", X + 4 * KB, BF16)
        spare = []
        for j in range(PACK):
            gather_into_place(k0_grouped[:], j, k_planes[j], listed(0))
            gather_plane(S, k1_gathered[:, j, :], k_planes[j], listed(1))
            if j < 2:
                spare.append(work.tile([P, T], F32, name="spare%d" % j, offset=(K0, K1)[j], align_bytes=64))
                nc.gpsimd.memset(spare[j][:], 0.0)
        dk_windows = [spare[0], spare[1], dv_windows[1], dv_windows[0]]
        k1_parts = [slice(0, QUARTER), slice(QUARTER, HALF), HALVES[1]]
        k1_grouped = [new_grouped("k1_grouped%d" % n, (X + 8 * KB, Q0 + 2 * KB, Q0)[n], c.stop - c.start) for n, c in enumerate(k1_parts)]
        weave(S, k1_grouped[0][:], k1_gathered[:, :, k1_parts[0]])
        q0_grouped = [new_grouped("q0_grouped%d" % h, X + 12 * KB + 2 * KB * h, HALF) for h in range(2)]
        k0 = [new_operand(E4, "k0_%d" % h) for h in range(2)]
        quantise(k0[0], k0_grouped[:, 0 : 2 * W])
        for h in range(2):
            deal((V, S)[h], q0_grouped[h][:], q0_raw[:], range(2 * h, 2 * h + 2))
        quantise(k0[1], k0_grouped[:, 2 * W : 4 * W])
        neg_lse0 = negated("neg_lse0", X + 2 * KB, lse_sb[:, 0, :])
        neg_lse1 = negated("neg_lse1", X + 33 * KB, lse_sb[:, 1, :])
        weave(S, k1_grouped[1][:], k1_gathered[:, :, k1_parts[1]])
        q0 = new_operand(E4, "q0")
        for h in range(2):
            quantise(q0, q0_grouped[h][:], h * HALF)
        weave(V, k1_grouped[2][:], k1_gathered[:, :, k1_parts[2]])
        dom0_grouped = [new_grouped("dom0_grouped%d" % h, (X + 16 * KB, X + 2 * KB)[h], HALF) for h in range(2)]
        weave(V, dom0_grouped[0][:], dom0_raw[:, :, HALVES[0]])
        pw0_planes = [new_planes("pw0_planes%d" % h, X + 20 * KB + 4 * KB * h, F32, HALF) for h in range(2)]
        for h in range(2):
            banks = [product("bank%d" % (4 * h + t), q0, t, k0[h], HALVES[0]) for t in range(PACK)]
            weights(pw0_planes[h], banks, neg_lse0)
        pw0 = new_operand(E4, "pw0")
        pw0_grouped = [new_grouped("pw0_grouped%d" % h, (X + 28 * KB, X + 16 * KB)[h], HALF) for h in range(2)]
        k1 = new_operand(E4, "k1", X + 28 * KB)
        dom0 = new_operand(E5, "dom0")
        gate(pw0_planes[0], pw0_planes[0], 0)
        quantise(dom0, dom0_grouped[0][:], 0)
        weave(V, pw0_grouped[0][:], pw0_planes[0][:])
        gate(pw0_planes[1], pw0_planes[1], 0)
        quantise(pw0, pw0_grouped[0][:], 0)
        q1_grouped = [new_grouped("q1_grouped%d" % h, (X + 16 * KB, X + 2 * KB)[h], HALF) for h in range(2)]
        deal(S, q1_grouped[1][:], q1_raw[:], range(2, PACK))
        deal(V, q1_grouped[0][:], q1_raw[:], range(0, 2))
        for n in (2, 0, 1):
            quantise(k1, k1_grouped[n][:], k1_parts[n].start)
        q1 = new_operand(E4, "q1")
        for h in range(2):
            quantise(q1, q1_grouped[h][:], h * HALF)
        weave(V, pw0_grouped[1][:], pw0_planes[1][:])
        weave(V, dom0_grouped[1][:], dom0_raw[:, :, HALVES[1]])
        quantise(pw0, pw0_grouped[1][:], HALF)
        quantise(dom0, dom0_grouped[1][:], HALF)
        a1 = [product("bank1", dom0, 1, pw0, HALVES[0])]
        a0 = [product("bank0", dom0, 0, pw0, HALVES[0])]
        scores1 = [product("bank%d" % (4 + t), q1, t, k1) for t in range(PACK)]
        a1.append(product("bank4", dom0, 1, pw0, HALVES[1]))
        a0.append(product("bank5", dom0, 0, pw0, HALVES[1]))
        a2 = product("bank6", dom0, 2, pw0)
        a3 = product("bank7", dom0, 3, pw0)
        staged_a1 = [stage(S, a1[0][:], "staged_a1_0", X + KB)]
        staged_a0 = [stage(S, a0[0][:], "staged_a0_0", X)]
        scatter(S, dv_windows[1], staged_a1[0][:], 0, HALVES[0])

        dom1_grouped = new_grouped("dom1_grouped", X + 3 * KB)
        weave(G, dom1_grouped[:], dom1_raw[:])
        v_gathered = [new_planes("v_gathered%d" % b, (DOM0 + 4 * KB, X + 16 * KB)[b], BF16) for b in range(B)]
        scatter(V, dv_windows[0], staged_a0[0][:], 0, HALVES[0])
        gather_plane(V, v_gathered[0][:, 0, :], v_planes[0], listed(0))
        p1 = new_planes("p1", K2, F32)
        weights(p1, scores1, neg_lse1)
        staged_a1.append(stage(S, a1[1][:], "staged_a1_1", Q0 + 3 * KB))
        staged_a0.append(stage(S, a0[1][:], "staged_a0_1", Q0 + 4 * KB))
        scatter(S, dv_windows[1], staged_a1[1][:], 0, HALVES[1])
        scatter(S, dv_windows[0], staged_a0[1][:], 0, HALVES[1])
        pw1_planes = new_planes("pw1_planes", DOM1, F32)
        gate(pw1_planes, p1, 1)
        dom1 = quantised(dom1_grouped, E5, "dom1")
        pw1_grouped = new_grouped("pw1_grouped", X + 14 * KB)
        weave(G, pw1_grouped[:], pw1_planes[:])
        for j in range(1, PACK):
            gather_plane(V, v_gathered[0][:, j, :], v_planes[j], listed(0))
        staged_a2 = stage(S, a2[:], "staged_a2", Q1)
        staged_a3 = stage(S, a3[:], "staged_a3", Q0 + 6 * KB)
        for h in range(2):
            scatter(S, dv_windows[2], staged_a2[:, HALVES[h]], 0, HALVES[h])
            scatter(S, dv_windows[3], staged_a3[:, HALVES[h]], 0, HALVES[h])
        neg_delta = work.tile([P, B, PACK], F32, name="neg_delta", offset=K2 + 7 * KB, align_bytes=64)
        nc.gpsimd.tensor_scalar(neg_delta[:], delta_raw[:], -1.0, 0.0, ALU.mult, ALU.add)
        pw1 = quantised(pw1_grouped, E4, "pw1", X + 34 * KB)
        dv1 = {j: product("bank%d" % j, dom1, j, pw1) for j in range(PACK)}
        v0_grouped = new_grouped("v0_grouped", X + 12 * KB)
        weave(G, v0_grouped[:], v_gathered[0][:])
        qm0_grouped = new_grouped("qm0_grouped", DOM0 + 4 * KB)
        weave(G, qm0_grouped[:], qm0_raw[:])
        staged_b = {}

        def stage_pair(pair, at):
            for h in range(2):
                for j in (pair, pair + 1):
                    staged_b[j, h] = stage(V, dv1[j][:, HALVES[h]], "staged_b%d_%d" % (j, h), at + KB * (2 * h + j - pair))

        for j in range(PACK):
            gather_plane(V, v_gathered[1][:, j, :], v_planes[j], listed(1))
            if j == 0:
                stage_pair(0, X + 5 * KB)
        do0_grouped = new_grouped("do0_grouped", QM0)
        deal(V, do0_grouped[:], do0_raw[:])
        v0 = quantised(v0_grouped, E4, "v0", QM0 + 4 * KB)
        do0 = quantised(do0_grouped, E5, "do0")
        dp0 = [product("bank%d" % (4 + t), do0, t, v0) for t in range(PACK)]
        v1_grouped = new_grouped("v1_grouped", QM0)
        weave(G, v1_grouped[:], v_gathered[1][:])
        stage_pair(2, X + 12 * KB)
        for pair in range(0, PACK, 2):
            for h in range(2):
                for j in (pair, pair + 1):
                    scatter(S, dv_windows[j], staged_b[j, h][:], 1, HALVES[h])
            store(out_1, pair, dv_windows[pair])
            store(out_1, pair + 1, dv_windows[pair + 1])
        ds0_planes = new_planes("ds0_planes", Q1 + 2 * KB, BF16)
        for t in range(PACK):
            for h in range(2):
                score_gradient(ds0_planes[:, :, HALVES[h]], dp0, pw0_planes[h], 0, HALVES[h], range(t, t + 1))
        do1_grouped = new_grouped("do1_grouped", X + 16 * KB)
        deal(V, do1_grouped[:], do1_raw[:])
        v1 = quantised(v1_grouped, E4, "v1")
        do1 = quantised(do1_grouped, E5, "do1")
        dp1 = [product("bank%d" % (4 + t), do1, t, v1) for t in range(PACK)]
        ds0_grouped = new_grouped("ds0_grouped", DO1)
        weave(V, ds0_grouped[:], ds0_planes[:])
        qm0 = quantised(qm0_grouped, E4, "qm0", X + 16 * KB)
        ds0 = quantised(ds0_grouped, E5, "ds0")
        dk0 = {j: product("bank%d" % j, qm0, j, ds0) for j in (1, 0, 2, 3)}
        qm1_grouped = new_grouped("qm1_grouped", DO1)
        weave(G, qm1_grouped[:], qm1_raw[:])
        ds1_planes = new_planes("ds1_planes", DO0, BF16)
        score_gradient(ds1_planes[:], dp1, pw1_planes, 1, WHOLE)
        staged_c = {j: stage(S, dk0[j][:], "staged_c%d" % j, V3 + 2 * KB * j) for j in (1, 0, 2)}
        ds1_grouped = new_grouped("ds1_grouped", DO0 + 4 * KB)
        weave(G, ds1_grouped[:], ds1_planes[:])
        scatter(V, dk_windows[1], staged_c[1][:], 0)
        for j, h in ((0, 0), (2, 0), (0, 1)):
            scatter(S, dk_windows[j], staged_c[j][:, HALVES[h]], 0, HALVES[h])
        ds1 = quantised(ds1_grouped, E5, "ds1")
        qm1 = new_operand(E4, "qm1", DO0 + 3 * KB + 512)
        for h in range(2):
            quantise(qm1, qm1_grouped[:, 2 * W * h : 2 * W * (h + 1)], h * HALF)
        dk1 = {j: product("bank%d" % (4 + j), qm1, j, ds1) for j in (1, 0, 3, 2)}
        staged_last = work.tile([P, B * N], F32, name="staged_last", offset=DO0 - KB, align_bytes=64)
        copy_on(V, staged_last[:, 0:N], dk0[3][:])
        staged_d = {1: stage(V, dk1[1][:], "staged_d1", V2 + 2 * KB)}
        staged_d[0] = [stage(V, dk1[0][:, HALVES[h]], "staged_d0_%d" % h, V2 + KB * h) for h in range(2)]
        copy_on(V, staged_last[:, N : 2 * N], dk1[3][:])
        scatter(V, dk_windows[1], staged_d[1][:], 1)
        store(out_0, 1, dk_windows[1])
        scatter(S, dk_windows[2], staged_c[2][:, HALVES[1]], 0, HALVES[1])
        scatter(S, dk_windows[0], staged_d[0][0][:], 1, HALVES[0])
        staged_d[2] = stage(S, dk1[2][:], "staged_d2", V2 - KB)
        scatter(S, dk_windows[0], staged_d[0][1][:], 1, HALVES[1])
        scatter(S, dk_windows[2], staged_d[2][:, HALVES[0]], 1, HALVES[0])
        store(out_0, 0, dk_windows[0], S)
        scatter(S, dk_windows[2], staged_d[2][:, HALVES[1]], 1, HALVES[1])
        store(out_0, 2, dk_windows[2], S)
        nc.vector.tensor_copy(dk_windows[3][:].indirect(offsets[:]), staged_last[:])
        store(out_0, 3, dk_windows[3])
